import numpy as np, ml_dtypes
CORES = [66,74,82,90,194,202,210,218]
N = 8
import mx_ref
BF = ml_dtypes.bfloat16
def entries(a):
    return np.ascontiguousarray(a.T).reshape(-1)
def table(e):
    return np.ascontiguousarray(np.reshape(e, (-1, 16)).T).astype(np.int32)
def cols(t, e):
    v = np.concatenate([t.reshape(128, -1, 4), np.zeros((128, 1, 4), BF)], axis=1)
    return np.ascontiguousarray(v[:, e]).reshape(128, -1)
def f(rng, *shape):
    return mx_ref.flush((rng.standard_normal(shape, dtype=np.float32) * np.exp2(rng.integers(-2, 3, shape[:-1] + (1,)))).astype(BF))
def wide(rng, *shape, cols=0):
    v = rng.standard_normal(shape, dtype=np.float32) * np.exp2(rng.integers(-12, 13, shape)).astype(np.float32)
    if cols: v *= np.repeat(np.exp2(rng.integers(-cols, cols + 1, shape[:-2] + (1, shape[-1] // 4))) * (rng.random(shape[:-2] + (1, shape[-1] // 4)) > 0.0625), 4, axis=-1).astype(np.float32)
    return mx_ref.flush(v.astype(BF))
T, S, O, CAPP = 128, 256, 2, (64, 96, 128)
B = len(CAPP)
def wanters(q, b):
    return sum(1 << e for e in range(N) if (e ^ q ^ (1 << b)) % (2 << b) == 0)
def holders(q, b):
    return (q >> b) << b, ((q >> b) + 1) << b
def limit(rng, m, keep, lo, hi, s, most):
    v = m.reshape(-1)
    e = np.flatnonzero(v[lo * T:hi * T] & s) + lo * T
    e = e[np.argsort(rng.random(len(e)) - ((keep.reshape(-1)[e] & s) != 0))][most:]
    v[e] &= ~s
def masks(rng, keep=None, off=None, share=0.55):
    keep = np.zeros((N, T), int) if keep is None else keep
    off = np.zeros((N, T), bool) if off is None else off
    for r in range(N):
        if not ((keep >> r) & 1).any(): keep[r, rng.choice(np.flatnonzero(~off[r]))] |= 1 << r
    n = rng.integers(1, 4, (N, T)) * (rng.random((N, T)) < share)
    m = ((np.argsort(rng.random((N, T, N)), axis=2) < n[:, :, None]) * (1 << np.arange(N))).sum(axis=2)
    m = np.ascontiguousarray(np.where(off, 0, m) | keep)
    for b in range(B):
        for q in range(N): limit(rng, m, keep, *holders(q, b), wanters(q, b), CAPP[b])
    for r in range(N): limit(rng, m, keep, 0, N, 1 << r, S)
    return {"dm": np.stack([table(v) for v in m])}
def setup_inputs(rng):
    return {"x": f(rng, N, 128, 4 * T), **masks(rng), "w": f(rng, N, 128, 512 * O)}
def setup_inputs_comb(rng):
    k = np.zeros((N, T), int); c = np.arange(T); s = int(rng.integers(0, 16)); p = int(rng.integers(0, N)); g = p ^ (N >> 1)
    for e in range(N): k[:, (c - e - s) % 4 == 0] |= 1 << e
    lo, hi = holders(p, B - 1)
    k[lo:hi] &= ~(1 << g)
    k[p, c % 16 != s] |= 1 << g
    assert not check_inputs({"dm": np.stack([table(v) for v in k])})
    return {**setup_inputs(rng), **masks(rng, k)}
def setup_inputs_turn(rng):
    k = np.zeros((N, T), int); g = int(rng.integers(0, N))
    k[g ^ 1, rng.permutation(T)[:CAPP[0]]] |= 1 << g
    k[g ^ 3, rng.permutation(T)[:CAPP[0]]] |= 1 << g
    h = rng.permutation(T)
    k[g, h[:CAPP[0]]] |= 1 << (g ^ 3)
    k[g, h[CAPP[0]:2 * CAPP[0]]] |= 1 << (g ^ 2)
    if N == 8: k[g ^ 6, rng.permutation(T)[:CAPP[1]]] |= 1 << (g ^ 4)
    return {**setup_inputs(rng), **masks(rng, k)}
def setup_inputs_none(rng):
    z = np.zeros((N, T), bool); k = np.zeros((N, T), int); p = int(rng.integers(0, N))
    for r in range(N): z[r, rng.permutation(T)[:T // 2]] = True
    k[p ^ 1, rng.choice(np.flatnonzero(~z[p ^ 1]))] |= 1 << p
    d = {**setup_inputs(rng), **masks(rng, k, off=z, share=1)}
    d["dm"][p] = 0
    return d
def setup_inputs_full(rng):
    k = np.zeros((N, T), int); g = int(rng.integers(0, N)); s = int(rng.integers(0, T))
    k[g ^ 1, (np.arange(CAPP[0]) + s) % T] |= 1 << (g ^ 2)
    k[g, (np.arange(S - sum(CAPP[1:])) + s) % T] |= 1 << g
    for b in range(1, B):
        for r in range(N):
            if r >> b == (g >> b) ^ 1: k[r, (np.arange(CAPP[b] >> b) + s) % T] |= 1 << g
    assert not check_inputs({"dm": np.stack([table(v) for v in k])})
    return {**setup_inputs(rng), **masks(rng, k, share=1)}
def setup_inputs_spread(rng):
    d = setup_inputs(rng); d["x"] = wide(rng, N, 128, 4 * T, cols=8); return d
def check_inputs(d):
    bad = []
    m = np.stack([entries(v) for v in d["dm"]]).astype(np.int64)
    if m.min() < 0 or m.max() >= 1 << N: bad.append("dm")
    for r in range(N):
        if ((m >> r) & 1).sum() > S: bad.append("arrivals")
    for b in range(B):
        for q in range(N):
            lo, hi = holders(q, b)
            if ((m[lo:hi] & wanters(q, b)) != 0).sum() > CAPP[b]: bad.append("CAPP_" + str(b))
    return bad
def reference(x, dm, w):
    m = np.stack([entries(v) for v in dm])
    every = np.concatenate(list(x), axis=1)
    y = np.zeros((N, 128, O * S), np.float32); ln = np.zeros((N, 1, 2), np.float32)
    for r in range(N):
        e = np.flatnonzero((m.reshape(-1) >> r) & 1); n = len(e)
        k = np.full(S, -1); k[:n] = e
        a = mx_ref.quantize(cols(every, k))
        for o in range(O):
            y[r][:, S * o:S * o + n] = mx_ref.matmul(mx_ref.quantize(np.ascontiguousarray(w[r][:, 512 * o:512 * o + 512])), a)[:, :n]
        ln[r, 0, 0] = n; ln[r, 0, 1] = np.count_nonzero((m[r] >> r) & 1)
    return {"y": y, "ln": ln}

@@ -1,0 +1,442 @@
+from concourse.bass import DstId, RemoteDMATransfer
+from concourse.mybir import dt, AluOpType, ActivationFunctionType
+
+A = AluOpType
+F = ActivationFunctionType
+U8, U32 = dt.uint8, dt.uint32
+N, COLS, S = 8, 128, 256
+H0, H1, H2 = 64, 96, 128
+PAIR = COLS + H0
+NEAR = PAIR + H1
+ZERO = NEAR + H2
+N1, N2 = (3, 3), (4, 4)
+NF, NE = 3, 2
+LOW = 64.0
+
+CODE, PLANE = "float8_e4m3fn_x4", "uint8"
+BLK = 208
+SCRATCH = {
+    "dmi": ("sbuf", [128, 8], "int32"), "xt": ("sbuf", [128, 520], "bfloat16"), "wt": ("sbuf", [128, 1024], "bfloat16"),
+    "c0c": ("sbuf", [128, COLS + 2], CODE), "c0s": ("sbuf", [128, COLS + 2], PLANE),
+    "c1c": ("sbuf", [128, PAIR + 2], CODE), "c1s": ("sbuf", [128, PAIR + 2], PLANE),
+    "c2c": ("sbuf", [128, NEAR + 2], CODE), "c2s": ("sbuf", [128, NEAR + 2], PLANE),
+    "a2c": ("sbuf", [128, H2], CODE), "a2s": ("sbuf", [128, H2], PLANE),
+    "wqc": ("sbuf", [128, 256], CODE), "wqs": ("sbuf", [128, 256], PLANE),
+    "sl0c": ("sbuf", [128, H0], CODE), "sl0s": ("sbuf", [128, H0], PLANE),
+    "sl1c": ("sbuf", [128, H1], CODE), "sl1s": ("sbuf", [128, H1], PLANE),
+    "sl2c": ("sbuf", [128, H2], CODE), "sl2s": ("sbuf", [128, H2], PLANE),
+    "tab": ("sbuf", [128, 32], "uint16"), "lt1": ("sbuf", [128, 4], "uint16"), "lt3": ("sbuf", [128, 4], "uint16"),
+    "lt2": ("sbuf", [128, 6], "uint16"), "nfa": ("sbuf", [128, 2], "float32"), "nfo": ("sbuf", [128, 2], "float32"),
+    "lut": ("sbuf", [128, 1024], "bfloat16"), "lv": ("sbuf", [128, 16], "int32"), "la": ("sbuf", [128, 16], "int32"),
+    "pa": ("sbuf", [128, 16], "bfloat16"), "pb": ("sbuf", [128, 128], "bfloat16"), "zi": ("sbuf", [128, 2], "int32"),
+    "za": ("sbuf", [128, 2], "int32"), "zb": ("sbuf", [128, 2], "int32"), "ra16": ("sbuf", [128, 1], "float32"),
+    "ra32": ("sbuf", [128, 1], "float32"), "b16": ("sbuf", [128, 8], "float32"), "b32": ("sbuf", [128, 8], "float32"),
+    "kf": ("sbuf", [128, 8], "float32"), "kg": ("sbuf", [128, 8], "float32"), "ki": ("sbuf", [128, 8], "float32"),
+    "cu": ("sbuf", [128, 4], "uint16"), "one": ("sbuf", [128, NEAR], "bfloat16"),
+    "fb": ("sbuf", [128, 7 * BLK], "bfloat16"), "f0": ("sbuf", [128, COLS], "bfloat16"), "f1": ("sbuf", [128, PAIR], "bfloat16"),
+    "f2": ("sbuf", [128, NEAR], "bfloat16"), "fs": ("sbuf", [128, NEAR], "bfloat16"), "k0": ("sbuf", [128, COLS], "bfloat16"),
+    "k1": ("sbuf", [128, PAIR], "bfloat16"), "k2": ("sbuf", [128, NEAR], "bfloat16"), "ks": ("sbuf", [128, NEAR], "bfloat16"),
+    "e1": ("sbuf", [128, 1], "float32"), "ba": ("sbuf", [128, 1], "float32"), "bb": ("sbuf", [128, 1], "float32"),
+    "bs": ("sbuf", [128, 1], "float32"),
+    "js": ("sbuf", [128, 6144], "bfloat16"), "jv": ("sbuf", [128, 6144], "bfloat16"), "jw": ("sbuf", [128, 6144], "bfloat16"),
+    "cs": ("sbuf", [128, 32], "float32"), "hs": ("sbuf", [128, 8], "float32"), "rr": ("sbuf", [128, 32], "bfloat16"),
+    "ra": ("sbuf", [128, 32], "bfloat16"), "rb": ("sbuf", [128, 64], "bfloat16"), "rc": ("sbuf", [128, 64], "bfloat16"),
+    "ad": ("sbuf", [128, 16], "float32"),
+    "ke": ("sbuf", [128, 8], "float32"), "ga": ("sbuf", [128, 8], "float32"), "gb": ("sbuf", [128, 8], "float32"),
+    "gt": ("sbuf", [128, 8], "float32"),
+    "t0": ("sbuf", [128, 4], "uint16"), "t1": ("sbuf", [128, 6], "uint16"), "t2": ("sbuf", [128, 8], "uint16"),
+    "tf": ("sbuf", [128, 16], "uint16"), "lnb": ("sbuf", [1, 2], "float32"),
+    "g0": ("sbuf", [128, ZERO + 16], "float32"), "g1": ("sbuf", [128, ZERO + 16], "float32"),
+    "y0": ("sbuf", [128, 256], "float32"), "y1": ("sbuf", [128, 256], "float32"),
+    "ps": ("psum", [128, 2048], "float32"),
+}
+ARR = ["rm1", "rm2", "l1", "l2", "l3", "nf", "h0c", "h0s", "h1c", "h1s", "h2c", "h2s"]
+SEMAPHORES = ["qv", "qs", "qt", "qp", "ld", "lx", "lw", "cp1", "cp2", "sya", "syb", "sln", "loc"] + ARR
+
+
+def rank_program(g, core, T, topo):
+    q = T.rank_of(core)
+    if q is None:
+        return
+    V, SC, TE, Y = g.vector, g.scalar, g.tensor, g.sync
+    queue = {"v": V, "s": SC, "t": TE, "p": g, "y": Y}
+    done = {"v": 0, "s": 0, "t": 0, "p": 0}
+    seen = {}
+
+    def need(e, *deps):
+        best = {}
+        for d in deps:
+            best[d[0]] = max(best.get(d[0], 0), d[1])
+        for s in best:
+            if seen.get((e, s), 0) < best[s]:
+                queue[e].wait_ge(T.sem[s], best[s])
+                seen[(e, s)] = best[s]
+
+    def mark(e, ins):
+        ins.then_inc(T.sem["q" + e], 1)
+        done[e] += 1
+        return ("q" + e, done[e])
+
+    sent = [0]
+
+    def send(dst, out, in_, sem, *deps):
+        need("p", *deps)
+        rid, pid = topo.addr(dst, core)
+        g.remote_dma(out, in_, T.sem[sem], T.sem["loc"], pid, rid, topo.mask(core, dst))
+        sent[0] += len(topo.engines(core, dst))
+
+    def spread(dsts, outs, in_, sem, *deps):
+        need("p", *deps)
+        ids = []
+        m = topo.mask(core, dsts[0])
+        for d in dsts:
+            rid, pid = topo.addr(d, core)
+            ids.append(DstId(rid=rid, pnc=pid))
+            m &= topo.mask(core, d)
+        g.remote_dma_fused([RemoteDMATransfer(dst_ids=ids, dma_engine_mask=m, remote_sem=T.sem[sem], srcs=[in_], dsts=outs)],
+                           local_sem=T.sem["loc"])
+        sent[0] += bin(m).count("1")
+
+    def arrived(sem, *srcs):
+        return (sem, sum(len(topo.engines(s, core)) for s in srcs))
+
+    at = lambda x: T.cores[q ^ x]
+    codes = lambda t, a, b: t[:, a:b].bitcast(U8)
+
+    hi, up, far = q & 1, (q >> 1) & 1, q >> 2
+    po, ps = H0 * hi, COLS * (1 - hi)
+    cp, cb = H1 * up, PAIR * (1 - up)
+    gn, gf = H2 * far, NEAR * (1 - far)
+    bits = lambda *ranks: sum(1 << e for e in ranks)
+    look = lambda l: T.lut[:, 256 * l:256 * l + 256]
+    M0, M1, M2, MS = range(4)
+    tab = lambda x: T.tab[:, 8 * x:8 * x + 8]
+    bit = lambda e: [[0, 256 >> (e + 1)], [1, 2], [0, 1 << e]]
+    R1, R2, RS, X2, XS, W2, WS = range(7)
+    blk = lambda b, a, n: T.fb[:, BLK * b + a:BLK * b + a + n]
+    others = lambda b: blk(b, H0, COLS)
+    tail = lambda b: blk(b, H0, BLK - H0)
+    whole = lambda b: blk(b, 0, BLK)
+
+    for i in range(8):
+        (Y if i % 2 == 0 else SC).dma_start(T.dmi[16 * i:16 * i + 16, :], T.dm[:, :]).then_inc(T.sem.ld, 16)
+    Y.dma_start(T.xt[:, 0:512], T.x[:, :]).then_inc(T.sem.lx, 16)
+    Y.dma_start(T.wt[:, :], T.w[:, :]).then_inc(T.sem.lw, 16)
+
+    iota = lambda o, pat: mark("p", g.iota(o, pat, 0, 0, allow_small_or_imprecise_dtypes=True))
+    tlv = mark("p", g.iota(T.lv[:, :], [[1, 16]], 0, 0))
+    tzi = mark("p", g.iota(T.zi[:, :], [[0, 2]], 0, 1))
+    tb16 = iota(T.b16[:, :], [[16, 8]])
+    par = bits(*[e for e in range(4) if (e ^ q) & 1])
+    low = (q ^ 2) & 3
+    tpb = iota(T.pb[:, 0:16 << low], [[0, 8], [1, 2], [0, 1 << low]])
+    a = mark("v", V.memset(look(M0), 1.0))
+    need("v", tlv)
+    b = mark("v", V.tensor_scalar(T.la[:, :], T.lv[:, :], par, None, A.bitwise_and))
+    tone = mark("v", V.memset(T.one[:, :], 1.0))
+    need("v", b)
+    b = mark("v", V.tensor_scalar(T.pa[:, :], T.la[:, :], 0.0, None, A.is_gt))
+    need("v", tzi)
+    tza = mark("v", V.tensor_scalar(T.za[:, :], T.zi[:, :], 15, None, A.bitwise_and))
+    need("s", a, b)
+    tl = {}
+    for u in range(16):
+        if not u & par:
+            tl[M0] = mark("s", SC.activation(T.lut[:, 16 * u:16 * u + 16], T.pa[:, :], F.Copy))
+    a = mark("v", V.memset(look(M1), 1.0))
+    need("v", tza)
+    b = mark("v", V.tensor_scalar(T.ra16[:, :], T.za[:, 0:1], 0.5, None, A.add))
+    need("s", b, tb16)
+    tkf = mark("s", SC.activation(T.kf[:, :], T.b16[:, :], F.Identity, bias=T.ra16[:, :]))
+    txz = mark("v", V.memset(T.xt[:, 512:520], 0.0))
+    tfz = mark("v", V.memset(T.fb[:, PAIR:7 * BLK:BLK], 0.0))
+    need("s", a, tpb)
+    n = 16 << low
+    for u in range(0, 256, 2 * n):
+        tl[M1] = mark("s", SC.activation(T.lut[:, 256 + u:256 + u + n], T.pb[:, 0:n], F.Copy))
+
+    use = {"js": 0, "jv": 0, "cs": 0, "ad": 0}
+
+    def take(name, n):
+        o = use[name]
+        use[name] += n
+        return o
+
+    def scan(out, fl, init, *deps):
+        need("v", tone, *deps)
+        n = int(out.shape[1])
+        return mark("v", V.tensor_tensor_scan(out, T.one[:, 0:n], fl, init, A.mult, A.add))
+
+    def flags(e, out, l, masks, total, *deps):
+        need(e, tl[l], *deps)
+        if e == "v":
+            return mark(e, V.tensor_copy(out, look(l).indirect(masks)))
+        return mark(e, SC.activation(out, look(l).indirect(masks), F.Copy, accum_out=total))
+
+    def gather(out, win, tab_, *deps):
+        need("s", tfz, *deps)
+        return mark("s", SC.activation(out, win.indirect(tab_), F.Copy))
+
+    k_ = lambda t, j: (lambda i: t[:, j + i:j + i + 1])
+
+    def compare(key, kcol, skip, nv, *deps):
+        b, c, n = key
+        o = take("jv", nv * n)
+        need("v", *deps)
+        for i in range(nv):
+            a_ = mark("v", V.tensor_scalar(T.jv[:, o + i * n + skip(i):o + i * n + n], b[:, c + skip(i):c + n], kcol(i), 0.5,
+                                           A.is_le, A.subtract))
+        return o, n, skip, nv, a_
+
+    def total(cmp, init, *deps):
+        o, n, skip, nv, a_ = cmp
+        need("v", a_)
+        for i in range(nv):
+            at_ = slice(o + i * n + skip(i), o + i * n + n)
+            a_ = scan(T.jw[:, at_], T.jv[:, at_], init(i), *deps)
+        return (lambda i: T.jw[:, o + i * n + n - 1:o + i * n + n]), T.jw[:, o + n - 1:o + nv * n:n], a_
+
+    def on_scalar(key, kcol, skip, ns, *deps):
+        b, c, n = key
+        o_ = take("cs", ns)
+        need("s", *deps)
+        n -= skip
+        for i in range(ns):
+            o = take("js", n)
+            a_ = mark("s", SC.activation(T.js[:, o:o + n], b[:, c + skip:c + skip + n], F.Sign, bias=kcol(i), scale=-1.0,
+                                         accum_out=T.cs[:, o_ + i:o_ + i + 1]))
+        return T.cs[:, o_:o_ + ns], a_
+
+    def early_s(key, first, nv, ns, *deps):
+        return on_scalar(key, k_(T.kf, nv), 16 * nv if first else 0, ns, tkf, *deps)
+
+    def early_v(key, first, nv, *deps):
+        return total(compare(key, k_(T.kf, 0), lambda i: 16 * i if first else 0, nv, tkf, *deps), lambda i: 8.0 * i)
+
+    def late_s(key, first, nv, ns, *deps):
+        return on_scalar(key, k_(T.kf, nv), 0 if first else 16 * nv, ns, tkf, *deps)
+
+    def late_v(key, first, nv, *deps):
+        return compare(key, k_(T.kf, 0), lambda i: 0 if first else 16 * i, nv, tkf, *deps)
+
+    def complete(tab_, n, nv, ns, va, sa, sb):
+        o = take("ad", ns)
+        need("v", sa[1], sb[1])
+        a_ = mark("v", V.tensor_tensor(T.ad[:, o:o + ns], sa[0], sb[0], A.add))
+        need("v", va[2])
+        mark("v", V.tensor_scalar(tab_[:, 0:nv], va[1], n / 2, None, A.add))
+        need("v", a_)
+        return mark("v", V.tensor_scalar(tab_[:, nv:nv + ns], T.ad[:, o:o + ns], 0.5, (n + 16 * nv) / 2, A.mult, A.add))
+
+    def pick_codes(out, src, n, tab_, *deps):
+        need("v", *deps)
+        return mark("v", V.tensor_copy(T[out + "c"][:, 0:n].bitcast(U32), T[src + "c"][:, :].bitcast(U32).indirect(tab_[:, :])))
+
+    def pick_plane(out, src, n, tab_, *deps):
+        need("s", *deps)
+        return mark("s", SC.activation(T[out + "s"][:, 0:n], T[src + "s"][:, :].indirect(tab_[:, :]), F.Copy))
+
+    def ship(dst, to, a_, src, n, sem, tok):
+        send(dst, codes(T[to + "c"], a_, a_ + n), codes(T[src + "c"], 0, n), sem + "c", tok[0])
+        send(dst, T[to + "s"][:, a_:a_ + n], T[src + "s"][:, 0:n], sem + "s", tok[1])
+
+    need("v", ("ld", 128))
+    tm = mark("v", V.tensor_copy(tab(0), T.dmi[:, :]))
+    send(at(1), tab(1), tab(0), "rm1", tm)
+    tb32 = iota(T.b32[:, :], [[32, 8]])
+    tl[M2] = iota(look(M2), bit(q ^ 4))
+
+    f = flags("v", T.f0[:, :], M0, tab(0), None, tm)
+    ti = scan(T.k0[:, :], T.f0[:, :], 0.0, f)
+    key = (T.k0, 0, COLS)
+    sb = on_scalar(key, k_(T.kf, 2), 32, 2, tkf, ti)
+    need("s", tone)
+    mark("s", SC.activation(T.g0[:, ZERO:ZERO + 16], T.one[:, 0:16], F.Copy, scale=0.0))
+    tz = mark("s", SC.activation(T.g1[:, ZERO:ZERO + 16], T.one[:, 0:16], F.Copy, scale=0.0))
+    va = total(compare(key, k_(T.kf, 0), lambda i: 16 * i, 2, tkf, ti), lambda i: 8.0 * i)
+    need("v", ("lx", 16), txz)
+    tq0 = mark("v", V.quantize_mx(T.c0c[:, :], T.c0s[:, :], T.xt[:, :]))
+    need("v", va[2])
+    mark("v", V.tensor_scalar(T.t0[:, 0:2], va[1], COLS / 2, None, A.add))
+    need("v", sb[1])
+    t0 = mark("v", V.tensor_scalar(T.t0[:, 2:4], sb[0], 0.5, (COLS + 32) / 2, A.mult, A.add))
+    send(at(1), T.lt1[:, :], T.t0[:, :], "l1", t0)
+    spread([at(2), at(3)], [tab(2), tab(3)], tab(0), "rm2")
+    ship(at(1), "c1", COLS * hi, "sl0", H0, "h0", (pick_codes("sl0", "c0", H0, T.t0, t0, tq0), pick_plane("sl0", "c0", H0, T.t0, t0, tq0)))
+    send(at(3), T.lt3[:, :], T.t0[:, :], "l3", t0)
+    tl[MS] = iota(look(MS), bit(q))
+
+    need("y", tq0)
+    tot = COLS + 2 * hi
+    Y.dma_start(codes(T.c1c, po, po + tot), codes(T.c0c, 0, tot)).then_inc(T.sem.cp1, 16)
+    Y.dma_start(T.c1s[:, po:po + tot], T.c0s[:, 0:tot]).then_inc(T.sem.cp1, 16)
+    w1 = 32
+    if not hi:
+        Y.dma_start(codes(T.c1c, PAIR, PAIR + 2), codes(T.c0c, COLS, COLS + 2)).then_inc(T.sem.cp1, 16)
+        Y.dma_start(T.c1s[:, PAIR:PAIR + 2], T.c0s[:, COLS:COLS + 2]).then_inc(T.sem.cp1, 16)
+        w1 = 64
+    Y.dma_start(codes(T.c2c, cp + po, cp + po + COLS), codes(T.c0c, 0, COLS)).then_inc(T.sem.cp2, 16)
+    Y.dma_start(T.c2s[:, cp + po:cp + po + COLS], T.c0s[:, 0:COLS]).then_inc(T.sem.cp2, 16)
+    Y.dma_start(codes(T.c2c, NEAR, NEAR + 2), codes(T.c0c, COLS, COLS + 2)).then_inc(T.sem.cp2, 16)
+    Y.dma_start(T.c2s[:, NEAR:NEAR + 2], T.c0s[:, COLS:COLS + 2]).then_inc(T.sem.cp2, 16)
+    h0a = [arrived("h0c", at(1)), arrived("h0s", at(1))]
+    need("y", *h0a)
+    Y.dma_start(codes(T.c2c, cp + ps, cp + ps + H0), codes(T.c1c, ps, ps + H0)).then_inc(T.sem.cp2, 16)
+    Y.dma_start(T.c2s[:, cp + ps:cp + ps + H0], T.c1s[:, ps:ps + H0]).then_inc(T.sem.cp2, 16)
+    w1, w2 = ("cp1", w1), ("cp2", 96)
+
+    rm1, rm2 = arrived("rm1", at(1)), arrived("rm2", at(2), at(3))
+    l1, l2, l3 = arrived("l1", at(1)), arrived("l2", at(2)), arrived("l3", at(3))
+    e1 = flags("s", T.f1[:, po:po + COLS], M1, tab(0), None, tm)
+    d1 = flags("s", others(R1), M1, tab(1), T.e1[:, :] if hi else None, rm1)
+    a = mark("v", V.tensor_scalar(T.zb[:, :], T.zi[:, :], 31, None, A.bitwise_and))
+    mark("v", V.tensor_scalar(T.cu[:, 0:2], T.za[:, :], 0.0, None, A.add))
+    tcu = mark("v", V.tensor_scalar(T.cu[:, 2:4], T.za[:, :], 16.0, None, A.add))
+    need("v", a)
+    a = mark("v", V.tensor_scalar(T.ra32[:, :], T.zb[:, 0:1], 0.5, None, A.add))
+    need("s", a, tb32)
+    tkg = mark("s", SC.activation(T.kg[:, :], T.b32[:, :], F.Identity, bias=T.ra32[:, :]))
+    need("s", tkg)
+    tki = mark("s", SC.activation(T.ki[:, :], T.kg[:, :], F.Copy, bias=-0.5))
+    trr = mark("v", V.memset(T.rr[:, :], 0.0))
+    need("v", ("lw", 16))
+    tqw = mark("v", V.quantize_mx(T.wqc[:, :], T.wqs[:, :], T.wt[:, :]))
+
+    own, came = (T.k1, po, COLS), (T.k1, ps, H0)
+    if hi:
+        ta = scan(T.k1[:, po:po + COLS], T.f1[:, po:po + COLS], T.e1[:, :], e1, d1)
+    else:
+        ta = scan(T.k1[:, po:po + COLS], T.f1[:, po:po + COLS], 0.0, e1)
+    sa = early_s(own, not hi, *N1, ta)
+    va = early_v(own, not hi, N1[0], ta)
+    es = flags("v", T.fs[:, cp + po:cp + po + COLS], MS, tab(0), None, tm)
+    d2 = flags("s", others(R2), M2, tab(1), None, rm1)
+    s1 = gather(T.f1[:, ps:ps + H0], tail(R1), T.lt1[:, :], l1, d1)
+    tb = scan(T.k1[:, ps:ps + H0], T.f1[:, ps:ps + H0], 0.0 if hi else T.k1[:, po + COLS - 1:po + COLS], ta, s1)
+    vb = total(late_v(came, not hi, N1[0], tb), va[0], va[2])
+    e2 = flags("s", T.f2[:, cp + po:cp + po + COLS], M2, tab(0), None, tm)
+    sb = late_s(came, not hi, *N1, tb)
+    t1 = complete(T.t1, PAIR, *N1, vb, sa, sb)
+    send(at(2), T.lt2[:, :], T.t1[:, :], "l2", t1)
+    s2 = gather(T.f2[:, cp + ps:cp + ps + H0], tail(R2), T.lt1[:, :], l1, d2)
+    da = flags("s", blk(W2, po, COLS), M2, tab(2), T.ba[:, :], rm2)
+    db = flags("s", others(X2), M2, tab(3), T.bb[:, :], rm2)
+    need("s", da, db)
+    tbs = mark("s", SC.activation(T.bs[:, :], T.ba[:, :], F.Identity, bias=T.bb[:, :]))
+    d3 = flags("v", others(RS), MS, tab(1), None, rm1)
+    d4 = flags("v", others(XS), MS, tab(3), None, rm2)
+
+    own, came = (T.k2, cp, PAIR), (T.k2, cb, H1)
+    end = T.k2[:, cp + PAIR - 1:cp + PAIR]
+    if up:
+        ta = scan(T.k2[:, cp:cp + PAIR], T.f2[:, cp:cp + PAIR], T.bs[:, :], e2, s2, tbs)
+    else:
+        ta = scan(T.k2[:, cp:cp + PAIR], T.f2[:, cp:cp + PAIR], 0.0, e2, s2)
+    ship(at(2), "c2", PAIR * up, "sl1", H1, "h1",
+         (pick_codes("sl1", "c1", H1, T.t1, t1, w1, *h0a), pick_plane("sl1", "c1", H1, T.t1, t1, w1, *h0a)))
+    need("s", ta, tbs)
+    if up:
+        mark("s", SC.activation(T.nfo[:, 0:1], end, F.Copy))
+        tnf = mark("s", SC.activation(T.nfo[:, 1:2], end, F.Copy, scale=-1.0))
+    else:
+        tnf = mark("s", SC.activation(T.nfo[:, 0:1], end, F.Identity, bias=T.bs[:, :]))
+        need("s", tnf)
+        tnf = mark("s", SC.activation(T.nfo[:, 1:2], T.nfo[:, 0:1], F.Copy, scale=-1.0))
+    send(at(4), T.nfa[:, :], T.nfo[:, :], "nf", tnf)
+    sa = early_s(own, not up, *N2, ta)
+    va = early_v(own, not up, N2[0], ta)
+    s3 = gather(blk(W2, ps, H0), tail(X2), T.lt3[:, :], l3, db)
+    d5 = flags("v", blk(WS, po, COLS), MS, tab(2), None, rm2)
+    if far:
+        need("v", tki)
+        tga = mark("v", V.tensor_scalar(T.ga[:, :], T.ki[:, :], float(H2), None, A.min))
+    s5 = gather(T.fs[:, cp + ps:cp + ps + H0], tail(RS), T.lt1[:, :], l1, d3)
+    s6 = gather(blk(WS, ps, H0), tail(XS), T.lt3[:, :], l3, d4)
+    s4 = gather(T.f2[:, cb:cb + H1], whole(W2), T.lt2[:, :], l2, s3, da)
+    tb = scan(T.k2[:, cb:cb + H1], T.f2[:, cb:cb + H1], 0.0 if up else end, ta, s4)
+    s7 = gather(T.fs[:, cb:cb + H1], whole(WS), T.lt2[:, :], l2, d5, s6)
+    sb = late_s(came, not up, *N2, tb)
+    vb = late_v(came, not up, N2[0], tb)
+    tss = scan(T.ks[:, :], T.fs[:, :], 0.0, es, s5, s7)
+    nf = arrived("nf", at(4))
+    tke, kE = tkg, T.kg
+    if far:
+        need("s", nf, tkg)
+        tke, kE = mark("s", SC.activation(T.ke[:, :], T.kg[:, :], F.Identity, bias=T.nfa[:, 1:2])), T.ke
+        need("s", tke)
+    vb = total(vb, va[0], va[2])
+    near = (T.ks, 0, NEAR)
+    on_scalar(near, k_(kE, NF), 0, NE, tke, tss)
+    t2 = complete(T.t2, NEAR, *N2, vb, sa, sb)
+    h1a = [arrived("h1c", at(2)), arrived("h1s", at(2))]
+    ship(at(4), "a2", 0, "sl2", H2, "h2",
+         (pick_codes("sl2", "c2", H2, T.t2, t2, w2, *h1a), pick_plane("sl2", "c2", H2, T.t2, t2, w2, *h1a)))
+
+    def product(o, bank, c, n, *deps):
+        need("t", tqw, *deps)
+        return mark("t", TE.matmul_mx(T.ps[:, 512 * bank:512 * bank + n], T.wqc[:, 128 * o:128 * o + 128], T.wqs[:, 128 * o:128 * o + 128],
+                                      T[c + "c"][:, 0:n], T[c + "s"][:, 0:n], True, True))
+    m0 = product(0, 0, "c2", NEAR, w2, *h1a)
+    m1 = product(1, 1, "c2", NEAR)
+
+    cmp = compare(near, k_(kE, 0), lambda i: 0, NF, tke, tss)
+    _, lst = on_scalar(near, k_(kE, NF + NE), 0, 8 - NF - NE, tke, tss)
+    ls_ = T.cs[:, use["cs"] - 8 + NF:use["cs"]]
+    need("s", lst)
+    ths = mark("s", SC.activation(T.hs[:, 0:8 - NF], ls_, F.Copy, scale=0.5, bias=-LOW))
+    need("v", tki)
+    if far:
+        need("v", nf)
+        a = mark("v", V.tensor_scalar(T.gb[:, :], T.ki[:, :], T.nfa[:, 0:1], float(H2), A.is_ge, A.mult))
+        _, lv_, lvt = total(cmp, lambda i: -LOW)
+        need("v", tga, a)
+        tgt = mark("v", V.tensor_tensor(T.gt[:, :], T.ga[:, :], T.gb[:, :], A.max))
+    else:
+        tgt = mark("v", V.tensor_scalar(T.gt[:, :], T.ki[:, :], T.ks[:, NEAR - 1:NEAR], 0.0, A.subtract, A.max))
+        _, lv_, lvt = total(cmp, lambda i: -LOW)
+    need("v", lvt, tgt, trr)
+    mark("v", V.tensor_tensor(T.rr[:, 0:NF], lv_, T.gt[:, 0:NF], A.add))
+    need("v", ths)
+    a = mark("v", V.tensor_tensor(T.rr[:, NF:8], T.hs[:, 0:8 - NF], T.gt[:, NF:8], A.add))
+    need("v", a)
+    a = mark("v", V.transpose(T.ra[:, :], T.rr[:, :]))
+    need("v", a, tcu)
+    a = mark("v", V.tensor_copy(T.rb[:, :], T.ra[:, :].indirect(T.cu[:, :])))
+    need("v", a)
+    a = mark("v", V.transpose(T.rc[:, :], T.rb[:, :]))
+    need("v", a)
+    mark("v", V.tensor_scalar(T.tf[:, 0:16:2], T.rc[:, 0:8], NEAR / 2 + LOW, float(ZERO), A.add, A.min))
+    ttf = mark("v", V.tensor_scalar(T.tf[:, 1:16:2], T.rc[:, 32:40], NEAR / 2 + LOW, float(ZERO), A.add, A.min))
+    need("s", m0)
+    g0a = mark("s", SC.activation(T.g0[:, gn:gn + NEAR], T.ps[:, 0:NEAR], F.Copy))
+    need("s", m1)
+    g1a = mark("s", SC.activation(T.g1[:, gn:gn + NEAR], T.ps[:, 512:512 + NEAR], F.Copy))
+
+    h2a = [arrived("h2c", at(4)), arrived("h2s", at(4))]
+    m2 = product(0, 2, "a2", H2, *h2a)
+    m3 = product(1, 3, "a2", H2)
+    need("s", m2)
+    b0 = mark("s", SC.activation(T.g0[:, gf:gf + H2], T.ps[:, 1024:1024 + H2], F.Copy))
+    need("s", m3)
+    b1 = mark("s", SC.activation(T.g1[:, gf:gf + H2], T.ps[:, 1536:1536 + H2], F.Copy))
+    need("v", b0, g0a, tz, ttf)
+    y0 = mark("v", V.tensor_copy(T.y0[:, :], T.g0[:, :].indirect(T.tf[:, :])))
+    need("s", b1, g1a, tz, ttf)
+    y1 = mark("s", SC.activation(T.y1[:, :], T.g1[:, :].indirect(T.tf[:, :]), F.Copy))
+    need("y", y0)
+    Y.dma_start(T.y[:, 0:S], T.y0[:, :]).then_inc(T.sem.sya, 16)
+    need("s", y1)
+    SC.dma_start(T.y[:, S:2 * S], T.y1[:, :]).then_inc(T.sem.syb, 16)
+    need("s", tss, nf)
+    mark("s", SC.activation(T.lnb[0:1, 0:1], T.nfa[0:1, 0:1], F.Identity, bias=T.ks[0:1, NEAR - 1:NEAR]))
+    c = cp + po
+    if c:
+        tln = mark("s", SC.activation(T.lnb[0:1, 1:2], T.ks[0:1, c - 1:c], F.Identity, bias=T.ks[0:1, c + COLS - 1:c + COLS], scale=-1.0))
+    else:
+        tln = mark("s", SC.activation(T.lnb[0:1, 1:2], T.ks[0:1, COLS - 1:COLS], F.Copy))
+    need("y", tln)
+    Y.dma_start(T.ln[:, :], T.lnb[:, :]).then_inc(T.sem.sln, 16)
+
+    need("p", ("loc", sent[0]), ("qv", done["v"]), ("qs", done["s"]), ("qt", done["t"]), ("qp", done["p"]))
+    need("y", ("sln", 16), ("sya", 16))
+    need("s", ("syb", 16))

@@ -8,49 +8,49 @@ N, COLS, S = 8, 128, 256
 H0, H1, H2 = 64, 96, 128
 PAIR = COLS + H0
 NEAR = PAIR + H1
-ZERO = NEAR + H2
-N1, N2 = (3, 3), (4, 4)
-NF, NE = 3, 2
-LOW = 64.0
+ZERO = S + H2
+GW = ZERO + 8
+BIG = 256.0
+VW, VB = 2 * COLS, 264
+PC = 8 * (VW - 1)
 
+XC = VW - 1
+OPT = {"j0v": 2, "pv": 3, "xv": 1, "r2": 2, "gx": 0, "sl": 2, "kx": 0, "cq": 1}
 CODE, PLANE = "float8_e4m3fn_x4", "uint8"
-BLK = 208
 SCRATCH = {
-    "dmi": ("sbuf", [128, 8], "int32"), "xt": ("sbuf", [128, 520], "bfloat16"), "wt": ("sbuf", [128, 1024], "bfloat16"),
+    "dmi": ("sbuf", [128, 8], "int32"), "xt": ("sbuf", [128, 1024], "bfloat16"), "wt": ("sbuf", [128, 1024], "bfloat16"),
     "c0c": ("sbuf", [128, COLS + 2], CODE), "c0s": ("sbuf", [128, COLS + 2], PLANE),
-    "c1c": ("sbuf", [128, PAIR + 2], CODE), "c1s": ("sbuf", [128, PAIR + 2], PLANE),
-    "c2c": ("sbuf", [128, NEAR + 2], CODE), "c2s": ("sbuf", [128, NEAR + 2], PLANE),
+    "c1c": ("sbuf", [128, PAIR + COLS], CODE), "c1s": ("sbuf", [128, PAIR + COLS], PLANE),
+    "c2c": ("sbuf", [128, NEAR + COLS], CODE), "c2s": ("sbuf", [128, NEAR + COLS], PLANE),
+    "ti": ("sbuf", [128, 4], "uint16"),
+    "cnc": ("sbuf", [128, S], CODE), "cns": ("sbuf", [128, S], PLANE),
     "a2c": ("sbuf", [128, H2], CODE), "a2s": ("sbuf", [128, H2], PLANE),
     "wqc": ("sbuf", [128, 256], CODE), "wqs": ("sbuf", [128, 256], PLANE),
     "sl0c": ("sbuf", [128, H0], CODE), "sl0s": ("sbuf", [128, H0], PLANE),
     "sl1c": ("sbuf", [128, H1], CODE), "sl1s": ("sbuf", [128, H1], PLANE),
     "sl2c": ("sbuf", [128, H2], CODE), "sl2s": ("sbuf", [128, H2], PLANE),
-    "tab": ("sbuf", [128, 32], "uint16"), "lt1": ("sbuf", [128, 4], "uint16"), "lt3": ("sbuf", [128, 4], "uint16"),
-    "lt2": ("sbuf", [128, 6], "uint16"), "nfa": ("sbuf", [128, 2], "float32"), "nfo": ("sbuf", [128, 2], "float32"),
-    "lut": ("sbuf", [128, 1024], "bfloat16"), "lv": ("sbuf", [128, 16], "int32"), "la": ("sbuf", [128, 16], "int32"),
-    "pa": ("sbuf", [128, 16], "bfloat16"), "pb": ("sbuf", [128, 128], "bfloat16"), "zi": ("sbuf", [128, 2], "int32"),
-    "za": ("sbuf", [128, 2], "int32"), "zb": ("sbuf", [128, 2], "int32"), "ra16": ("sbuf", [128, 1], "float32"),
-    "ra32": ("sbuf", [128, 1], "float32"), "b16": ("sbuf", [128, 8], "float32"), "b32": ("sbuf", [128, 8], "float32"),
-    "kf": ("sbuf", [128, 8], "float32"), "kg": ("sbuf", [128, 8], "float32"), "ki": ("sbuf", [128, 8], "float32"),
-    "cu": ("sbuf", [128, 4], "uint16"), "one": ("sbuf", [128, NEAR], "bfloat16"),
-    "fb": ("sbuf", [128, 7 * BLK], "bfloat16"), "f0": ("sbuf", [128, COLS], "bfloat16"), "f1": ("sbuf", [128, PAIR], "bfloat16"),
-    "f2": ("sbuf", [128, NEAR], "bfloat16"), "fs": ("sbuf", [128, NEAR], "bfloat16"), "k0": ("sbuf", [128, COLS], "bfloat16"),
-    "k1": ("sbuf", [128, PAIR], "bfloat16"), "k2": ("sbuf", [128, NEAR], "bfloat16"), "ks": ("sbuf", [128, NEAR], "bfloat16"),
-    "e1": ("sbuf", [128, 1], "float32"), "ba": ("sbuf", [128, 1], "float32"), "bb": ("sbuf", [128, 1], "float32"),
-    "bs": ("sbuf", [128, 1], "float32"),
-    "js": ("sbuf", [128, 6144], "bfloat16"), "jv": ("sbuf", [128, 6144], "bfloat16"), "jw": ("sbuf", [128, 6144], "bfloat16"),
-    "cs": ("sbuf", [128, 32], "float32"), "hs": ("sbuf", [128, 8], "float32"), "rr": ("sbuf", [128, 32], "bfloat16"),
-    "ra": ("sbuf", [128, 32], "bfloat16"), "rb": ("sbuf", [128, 64], "bfloat16"), "rc": ("sbuf", [128, 64], "bfloat16"),
-    "ad": ("sbuf", [128, 16], "float32"),
-    "ke": ("sbuf", [128, 8], "float32"), "ga": ("sbuf", [128, 8], "float32"), "gb": ("sbuf", [128, 8], "float32"),
-    "gt": ("sbuf", [128, 8], "float32"),
+    "xi": ("sbuf", [128, 16], "int32"), "tx": ("sbuf", [128, 8], "uint16"), "tab": ("sbuf", [128, 32], "uint16"),
+    "nfo": ("sbuf", [128, 1], "float32"), "nfa": ("sbuf", [128, 1], "float32"),
+    "lut": ("sbuf", [128, 448], "bfloat16"), "zi": ("sbuf", [128, 2], "int32"), "za": ("sbuf", [128, 2], "int32"),
+    "zh": ("sbuf", [128, 2], "int32"), "ra": ("sbuf", [128, 1], "float32"), "c64": ("sbuf", [128, 2], "float32"),
+    "cu": ("sbuf", [128, 2], "uint16"), "b16": ("sbuf", [128, 32], "float32"), "ki": ("sbuf", [128, 20], "float32"),
+    "kc": ("sbuf", [128, 6], "float32"),
+    "f0": ("sbuf", [128, COLS], "bfloat16"), "k0": ("sbuf", [128, COLS], "bfloat16"), "gg": ("sbuf", [128, 2 * VB], "bfloat16"),
+    "bz": ("sbuf", [128, 2 * VW + 2], "bfloat16"), "kk": ("sbuf", [128, 2 * VB], "bfloat16"),
+    "n0": ("sbuf", [128, 1], "float32"), "kz": ("sbuf", [128, 4], "float32"), "kp": ("sbuf", [128, 6], "float32"),
+    "kx": ("sbuf", [128, 4], "float32"),
+    "js": ("sbuf", [128, 14 * VW], "bfloat16"), "jv": ("sbuf", [128, 4 * VW], "bfloat16"), "jw": ("sbuf", [128, VW], "bfloat16"),
+    "cs": ("sbuf", [128, 8], "float32"), "w1": ("sbuf", [128, 8 * VW], "float32"), "w2": ("sbuf", [128, VW + 32], "float32"),
+    "nh": ("sbuf", [128, 3], "float32"), "nb": ("sbuf", [128, 1], "bfloat16"), "ad": ("sbuf", [128, 4], "float32"),
+    "pa": ("sbuf", [128, 4], "float32"),
+    "ta": ("sbuf", [128, 80], "float32"), "tb": ("sbuf", [128, 32], "float32"), "tc": ("sbuf", [128, 32], "float32"),
     "t0": ("sbuf", [128, 4], "uint16"), "t1": ("sbuf", [128, 6], "uint16"), "t2": ("sbuf", [128, 8], "uint16"),
-    "tf": ("sbuf", [128, 16], "uint16"), "lnb": ("sbuf", [1, 2], "float32"),
-    "g0": ("sbuf", [128, ZERO + 16], "float32"), "g1": ("sbuf", [128, ZERO + 16], "float32"),
-    "y0": ("sbuf", [128, 256], "float32"), "y1": ("sbuf", [128, 256], "float32"),
+    "tq": ("sbuf", [128, 16], "float32"), "tn": ("sbuf", [128, 16], "uint16"), "tf": ("sbuf", [128, 16], "uint16"),
+    "an": ("sbuf", [128, 4], "float32"), "la": ("sbuf", [128, 48], "float32"), "lnb": ("sbuf", [128, 2], "float32"),
+    "gr": ("sbuf", [128, 2 * GW], "float32"), "y0": ("sbuf", [128, 256], "float32"), "y1": ("sbuf", [128, 256], "float32"),
     "ps": ("psum", [128, 2048], "float32"),
 }
-ARR = ["rm1", "rm2", "l1", "l2", "l3", "nf", "h0c", "h0s", "h1c", "h1s", "h2c", "h2s"]
+ARR = ["rm1", "rm2", "nf", "h0c", "h0s", "h1c", "h1s", "h2c", "h2s"]
 SEMAPHORES = ["qv", "qs", "qt", "qp", "ld", "lx", "lw", "cp1", "cp2", "sya", "syb", "sln", "loc"] + ARR
 
 
@@ -77,6 +77,14 @@ def rank_program(g, core, T, topo):
         done[e] += 1
         return ("q" + e, done[e])
 
+    def v(call, *a, after=()):
+        need("v", *after)
+        return mark("v", call(*a))
+
+    def s(out, in_, func, after=(), **k):
+        need("s", *after)
+        return mark("s", SC.activation(out, in_, func, **k))
+
     sent = [0]
 
     def send(dst, out, in_, sem, *deps):
@@ -85,357 +93,311 @@ def rank_program(g, core, T, topo):
         g.remote_dma(out, in_, T.sem[sem], T.sem["loc"], pid, rid, topo.mask(core, dst))
         sent[0] += len(topo.engines(core, dst))
 
-    def spread(dsts, outs, in_, sem, *deps):
+    def part(src, dst, a, b):
+        e = topo.engines(src, dst)
+        return e[a * len(e) // 4:b * len(e) // 4]
+
+    def fused(writes, *deps):
         need("p", *deps)
-        ids = []
-        m = topo.mask(core, dsts[0])
-        for d in dsts:
+        tr = []
+        for d, out, in_, sem, a, b in writes:
             rid, pid = topo.addr(d, core)
-            ids.append(DstId(rid=rid, pnc=pid))
-            m &= topo.mask(core, d)
-        g.remote_dma_fused([RemoteDMATransfer(dst_ids=ids, dma_engine_mask=m, remote_sem=T.sem[sem], srcs=[in_], dsts=outs)],
-                           local_sem=T.sem["loc"])
-        sent[0] += bin(m).count("1")
+            tr.append(RemoteDMATransfer(dst_ids=[DstId(rid=rid, pnc=pid)], dma_engine_mask=sum(1 << e for e in part(core, d, a, b)),
+                                        remote_sem=T.sem[sem], srcs=[in_], dsts=[out]))
+            sent[0] += len(part(core, d, a, b))
+        g.remote_dma_fused(tr, local_sem=T.sem["loc"])
 
     def arrived(sem, *srcs):
-        return (sem, sum(len(topo.engines(s, core)) for s in srcs))
+        return (sem, sum(len(topo.engines(c, core)) for c in srcs))
 
     at = lambda x: T.cores[q ^ x]
     codes = lambda t, a, b: t[:, a:b].bitcast(U8)
+    Q = [slice(32 * i, 32 * i + 32) for i in range(4)]
+    LOW, UP, ALL = slice(0, 64), slice(64, 128), slice(0, 128)
 
     hi, up, far = q & 1, (q >> 1) & 1, q >> 2
-    po, ps = H0 * hi, COLS * (1 - hi)
-    cp, cb = H1 * up, PAIR * (1 - up)
-    gn, gf = H2 * far, NEAR * (1 - far)
-    bits = lambda *ranks: sum(1 << e for e in ranks)
-    look = lambda l: T.lut[:, 256 * l:256 * l + 256]
-    M0, M1, M2, MS = range(4)
-    tab = lambda x: T.tab[:, 8 * x:8 * x + 8]
-    bit = lambda e: [[0, 256 >> (e + 1)], [1, 2], [0, 1 << e]]
-    R1, R2, RS, X2, XS, W2, WS = range(7)
-    blk = lambda b, a, n: T.fb[:, BLK * b + a:BLK * b + a + n]
-    others = lambda b: blk(b, H0, COLS)
-    tail = lambda b: blk(b, H0, BLK - H0)
-    whole = lambda b: blk(b, 0, BLK)
+    last = hi ^ up
+    p1 = COLS * up
+    cp = (COLS + H1) * up
+    vo, vs = COLS * last, COLS * (1 - last)
+    gn, gf = H2 * far, S * (1 - far)
+    s1 = -BIG if last else BIG
+    row = lambda t, a, n: t[:, a + n - 1:a - 1 if a else None:-1] if up else t[:, a:a + n]
+    half, to = (-0.5 if up else 0.5), (lambda c, n: COLS + n - 1 - c if up else c)
+    lut1, lut2, lut0, lutm = T.lut[:, 0:96], T.lut[:, 128:224], T.lut[:, 256:352], T.lut[:, 352:448]
+    end_p, end_x = (lambda r: T.kk[r, VW:VW + 1]), (lambda r: T.kk[r, VB + VW:VB + VW + 1])
 
     for i in range(8):
         (Y if i % 2 == 0 else SC).dma_start(T.dmi[16 * i:16 * i + 16, :], T.dm[:, :]).then_inc(T.sem.ld, 16)
     Y.dma_start(T.xt[:, 0:512], T.x[:, :]).then_inc(T.sem.lx, 16)
     Y.dma_start(T.wt[:, :], T.w[:, :]).then_inc(T.sem.lw, 16)
 
-    iota = lambda o, pat: mark("p", g.iota(o, pat, 0, 0, allow_small_or_imprecise_dtypes=True))
-    tlv = mark("p", g.iota(T.lv[:, :], [[1, 16]], 0, 0))
+    place = lambda d: d - hi
+    bit = lambda b: [[0, 64 >> b], [1, 4], [0, 1 << b]] if b < 6 else [[0, 2], [1, 2], [0, 64]]
+    both = lambda e: [slice(0, e + 1, e), slice(16 * e, 17 * e + 1, e)]
+    iota = lambda o, pat, base=0: mark("p", g.iota(o, pat, base, 0, allow_small_or_imprecise_dtypes=True))
     tzi = mark("p", g.iota(T.zi[:, :], [[0, 2]], 0, 1))
-    tb16 = iota(T.b16[:, :], [[16, 8]])
-    par = bits(*[e for e in range(4) if (e ^ q) & 1])
-    low = (q ^ 2) & 3
-    tpb = iota(T.pb[:, 0:16 << low], [[0, 8], [1, 2], [0, 1 << low]])
-    a = mark("v", V.memset(look(M0), 1.0))
-    need("v", tlv)
-    b = mark("v", V.tensor_scalar(T.la[:, :], T.lv[:, :], par, None, A.bitwise_and))
-    tone = mark("v", V.memset(T.one[:, :], 1.0))
-    need("v", b)
-    b = mark("v", V.tensor_scalar(T.pa[:, :], T.la[:, :], 0.0, None, A.is_gt))
-    need("v", tzi)
-    tza = mark("v", V.tensor_scalar(T.za[:, :], T.zi[:, :], 15, None, A.bitwise_and))
-    need("s", a, b)
-    tl = {}
-    for u in range(16):
-        if not u & par:
-            tl[M0] = mark("s", SC.activation(T.lut[:, 16 * u:16 * u + 16], T.pa[:, :], F.Copy))
-    a = mark("v", V.memset(look(M1), 1.0))
-    need("v", tza)
-    b = mark("v", V.tensor_scalar(T.ra16[:, :], T.za[:, 0:1], 0.5, None, A.add))
-    need("s", b, tb16)
-    tkf = mark("s", SC.activation(T.kf[:, :], T.b16[:, :], F.Identity, bias=T.ra16[:, :]))
-    txz = mark("v", V.memset(T.xt[:, 512:520], 0.0))
-    tfz = mark("v", V.memset(T.fb[:, PAIR:7 * BLK:BLK], 0.0))
-    need("s", a, tpb)
-    n = 16 << low
-    for u in range(0, 256, 2 * n):
-        tl[M1] = mark("s", SC.activation(T.lut[:, 256 + u:256 + u + n], T.pb[:, 0:n], F.Copy))
+    need("p", tb16 := iota(T.b16[:, :], [[16, 32]], -256))
+    need("p", iota(T.lut[Q[1], 0:256], bit(place(q ^ 4))))
+    need("p", tl := iota(T.lut[UP, 0:256], bit(place(q))))
+    b16 = lambda r, a: T.b16[r, (a + 256) // 16:(a + 256) // 16 + 6]
 
-    use = {"js": 0, "jv": 0, "cs": 0, "ad": 0}
+    v(V.memset, T.lut[:, 257:352], 1.0)
+    tl0 = v(V.memset, T.lut[:, 256:257], 0.0)
+    za = v(V.tensor_scalar, T.za[:, :], T.zi[:, :], 15, None, A.bitwise_and, after=[tzi])
+    zh = v(V.tensor_scalar, T.zh[:, :], T.zi[:, :], 16, None, A.bitwise_and)
+    v(V.memset, T.lut[Q[0], 0:128], 1.0)
+    tra = v(V.tensor_scalar, T.ra[:, :], T.za[:, 0:1], 0.5, None, A.add, after=[za])
+    tq0 = v(V.memset, T.lut[Q[0], 128:256], 0.0)
+    t64 = v(V.tensor_scalar, T.c64[:, :], T.zh[:, :], 4.0, T.ra[:, :], A.mult, A.add, after=[tra, zh])
+    tbz = v(V.memset, T.bz[:, 0:VW + 2], 0.0)
+    tcu = v(V.tensor_scalar, T.cu[:, :], T.c64[:, :], -0.5, None, A.add, after=[t64])
+    txz = v(V.memset, T.xt[:, 512:1024], 0.0)
+    tgz = v(V.memset, T.gg[:, VW:2 * VB:VB], 0.0)
 
-    def take(name, n):
-        o = use[name]
-        use[name] += n
-        return o
+    def quantize(to, a, b, n, *deps):
+        return v(V.quantize_mx, T[to + "c"][:, a:a + n], T[to + "s"][:, a:a + n], T.xt[:, 4 * b:4 * (b + n)], after=deps)
 
-    def scan(out, fl, init, *deps):
-        need("v", tone, *deps)
-        n = int(out.shape[1])
-        return mark("v", V.tensor_tensor_scan(out, T.one[:, 0:n], fl, init, A.mult, A.add))
+    quantize("c1", PAIR * (1 - up), COLS, COLS, txz)
+    quantize("c2", NEAR * (1 - up), COLS, COLS)
 
-    def flags(e, out, l, masks, total, *deps):
-        need(e, tl[l], *deps)
-        if e == "v":
-            return mark(e, V.tensor_copy(out, look(l).indirect(masks)))
-        return mark(e, SC.activation(out, look(l).indirect(masks), F.Copy, accum_out=total))
+    def fill(o, rows, val, *deps):
+        return s(o, T.lut[rows, 257:257 + int(o.shape[1])], F.Copy, after=[tl0, *deps], scale=0.0, bias=val)
 
-    def gather(out, win, tab_, *deps):
-        need("s", tfz, *deps)
-        return mark("s", SC.activation(out, win.indirect(tab_), F.Copy))
+    def put(rows, base, cols, val, *deps):
+        for c in cols:
+            t = fill(T.lut[rows, base + c.start:base + c.stop:c.step or 1], rows, val, *deps)
+        return t
 
-    k_ = lambda t, j: (lambda i: t[:, j + i:j + i + 1])
+    put(ALL, 352, [slice(1, 96)], 0.0)
+    put(ALL, 352, [slice(0, 1)], s1)
+    fill(T.ta[:, 32:48], ALL, 0.0)
+    tz = fill(T.gr[:, ZERO:2 * GW:GW], ALL, 0.0)
+    tno = fill(T.nfo[:, :], ALL, 0.0)
+    tw2 = fill(T.w2[:, XC - 16:XC + 32], ALL, 0.0)
+    tki = s(T.ki[:, :], T.b16[:, 12:32], F.Identity, after=[tra, tb16], bias=T.ra[:, :])
+    tl1 = put(Q[0], 0, both(1 << place(q & 3)), 0.0, tq0)
+    kb = T.kc if up else T.kp
+    s(kb[Q[0], :], b16(Q[0], -H1 * up), F.Identity, bias=T.ra[Q[0], :])
+    for i, a in ((1, -H2 * up), (2, -S * up), (3, 128 - S * up)):
+        tk = s(kb[Q[i], :], b16(Q[i], a), F.Identity, after=[t64], bias=T.c64[Q[i], 0:1])
+    if up:
+        tk = s(T.kp[:, :], T.kc[:, :], F.Copy, after=[tk], scale=-1.0)
+    tl2 = put(ALL, 128, both(1 << place((q ^ 2) & 3)), BIG, tl)
 
-    def compare(key, kcol, skip, nv, *deps):
-        b, c, n = key
-        o = take("jv", nv * n)
-        need("v", *deps)
-        for i in range(nv):
-            a_ = mark("v", V.tensor_scalar(T.jv[:, o + i * n + skip(i):o + i * n + n], b[:, c + skip(i):c + n], kcol(i), 0.5,
-                                           A.is_le, A.subtract))
-        return o, n, skip, nv, a_
+    def pick_codes(out, src, tab_, *deps):
+        return v(V.tensor_copy, T[out + "c"][:, :].bitcast(U32), T[src + "c"][:, :].bitcast(U32).indirect(tab_[:, :]), after=deps)
 
-    def total(cmp, init, *deps):
-        o, n, skip, nv, a_ = cmp
-        need("v", a_)
-        for i in range(nv):
-            at_ = slice(o + i * n + skip(i), o + i * n + n)
-            a_ = scan(T.jw[:, at_], T.jv[:, at_], init(i), *deps)
-        return (lambda i: T.jw[:, o + i * n + n - 1:o + i * n + n]), T.jw[:, o + n - 1:o + nv * n:n], a_
-
-    def on_scalar(key, kcol, skip, ns, *deps):
-        b, c, n = key
-        o_ = take("cs", ns)
-        need("s", *deps)
-        n -= skip
-        for i in range(ns):
-            o = take("js", n)
-            a_ = mark("s", SC.activation(T.js[:, o:o + n], b[:, c + skip:c + skip + n], F.Sign, bias=kcol(i), scale=-1.0,
-                                         accum_out=T.cs[:, o_ + i:o_ + i + 1]))
-        return T.cs[:, o_:o_ + ns], a_
-
-    def early_s(key, first, nv, ns, *deps):
-        return on_scalar(key, k_(T.kf, nv), 16 * nv if first else 0, ns, tkf, *deps)
-
-    def early_v(key, first, nv, *deps):
-        return total(compare(key, k_(T.kf, 0), lambda i: 16 * i if first else 0, nv, tkf, *deps), lambda i: 8.0 * i)
-
-    def late_s(key, first, nv, ns, *deps):
-        return on_scalar(key, k_(T.kf, nv), 0 if first else 16 * nv, ns, tkf, *deps)
-
-    def late_v(key, first, nv, *deps):
-        return compare(key, k_(T.kf, 0), lambda i: 0 if first else 16 * i, nv, tkf, *deps)
-
-    def complete(tab_, n, nv, ns, va, sa, sb):
-        o = take("ad", ns)
-        need("v", sa[1], sb[1])
-        a_ = mark("v", V.tensor_tensor(T.ad[:, o:o + ns], sa[0], sb[0], A.add))
-        need("v", va[2])
-        mark("v", V.tensor_scalar(tab_[:, 0:nv], va[1], n / 2, None, A.add))
-        need("v", a_)
-        return mark("v", V.tensor_scalar(tab_[:, nv:nv + ns], T.ad[:, o:o + ns], 0.5, (n + 16 * nv) / 2, A.mult, A.add))
-
-    def pick_codes(out, src, n, tab_, *deps):
-        need("v", *deps)
-        return mark("v", V.tensor_copy(T[out + "c"][:, 0:n].bitcast(U32), T[src + "c"][:, :].bitcast(U32).indirect(tab_[:, :])))
-
-    def pick_plane(out, src, n, tab_, *deps):
-        need("s", *deps)
-        return mark("s", SC.activation(T[out + "s"][:, 0:n], T[src + "s"][:, :].indirect(tab_[:, :]), F.Copy))
+    def pick_plane(out, src, tab_, *deps):
+        return s(T[out + "s"][:, :], T[src + "s"][:, :].indirect(tab_[:, :]), F.Copy, after=deps)
 
     def ship(dst, to, a_, src, n, sem, tok):
         send(dst, codes(T[to + "c"], a_, a_ + n), codes(T[src + "c"], 0, n), sem + "c", tok[0])
         send(dst, T[to + "s"][:, a_:a_ + n], T[src + "s"][:, 0:n], sem + "s", tok[1])
 
-    need("v", ("ld", 128))
-    tm = mark("v", V.tensor_copy(tab(0), T.dmi[:, :]))
-    send(at(1), tab(1), tab(0), "rm1", tm)
-    tb32 = iota(T.b32[:, :], [[32, 8]])
-    tl[M2] = iota(look(M2), bit(q ^ 4))
+    def copy(to, a_, src, b_, n, sem):
+        Y.dma_start(codes(T[to + "c"], a_, a_ + n), codes(T[src + "c"], b_, b_ + n)).then_inc(T.sem[sem], 16)
+        Y.dma_start(T[to + "s"][:, a_:a_ + n], T[src + "s"][:, b_:b_ + n]).then_inc(T.sem[sem], 16)
 
-    f = flags("v", T.f0[:, :], M0, tab(0), None, tm)
-    ti = scan(T.k0[:, :], T.f0[:, :], 0.0, f)
-    key = (T.k0, 0, COLS)
-    sb = on_scalar(key, k_(T.kf, 2), 32, 2, tkf, ti)
-    need("s", tone)
-    mark("s", SC.activation(T.g0[:, ZERO:ZERO + 16], T.one[:, 0:16], F.Copy, scale=0.0))
-    tz = mark("s", SC.activation(T.g1[:, ZERO:ZERO + 16], T.one[:, 0:16], F.Copy, scale=0.0))
-    va = total(compare(key, k_(T.kf, 0), lambda i: 16 * i, 2, tkf, ti), lambda i: 8.0 * i)
-    need("v", ("lx", 16), txz)
-    tq0 = mark("v", V.quantize_mx(T.c0c[:, :], T.c0s[:, :], T.xt[:, :]))
-    need("v", va[2])
-    mark("v", V.tensor_scalar(T.t0[:, 0:2], va[1], COLS / 2, None, A.add))
-    need("v", sb[1])
-    t0 = mark("v", V.tensor_scalar(T.t0[:, 2:4], sb[0], 0.5, (COLS + 32) / 2, A.mult, A.add))
-    send(at(1), T.lt1[:, :], T.t0[:, :], "l1", t0)
-    spread([at(2), at(3)], [tab(2), tab(3)], tab(0), "rm2")
-    ship(at(1), "c1", COLS * hi, "sl0", H0, "h0", (pick_codes("sl0", "c0", H0, T.t0, t0, tq0), pick_plane("sl0", "c0", H0, T.t0, t0, tq0)))
-    send(at(3), T.lt3[:, :], T.t0[:, :], "l3", t0)
-    tl[MS] = iota(look(MS), bit(q))
+    js = [0]
 
-    need("y", tq0)
-    tot = COLS + 2 * hi
-    Y.dma_start(codes(T.c1c, po, po + tot), codes(T.c0c, 0, tot)).then_inc(T.sem.cp1, 16)
-    Y.dma_start(T.c1s[:, po:po + tot], T.c0s[:, 0:tot]).then_inc(T.sem.cp1, 16)
-    w1 = 32
-    if not hi:
-        Y.dma_start(codes(T.c1c, PAIR, PAIR + 2), codes(T.c0c, COLS, COLS + 2)).then_inc(T.sem.cp1, 16)
-        Y.dma_start(T.c1s[:, PAIR:PAIR + 2], T.c0s[:, COLS:COLS + 2]).then_inc(T.sem.cp1, 16)
-        w1 = 64
-    Y.dma_start(codes(T.c2c, cp + po, cp + po + COLS), codes(T.c0c, 0, COLS)).then_inc(T.sem.cp2, 16)
-    Y.dma_start(T.c2s[:, cp + po:cp + po + COLS], T.c0s[:, 0:COLS]).then_inc(T.sem.cp2, 16)
-    Y.dma_start(codes(T.c2c, NEAR, NEAR + 2), codes(T.c0c, COLS, COLS + 2)).then_inc(T.sem.cp2, 16)
-    Y.dma_start(T.c2s[:, NEAR:NEAR + 2], T.c0s[:, COLS:COLS + 2]).then_inc(T.sem.cp2, 16)
-    h0a = [arrived("h0c", at(1)), arrived("h0s", at(1))]
-    need("y", *h0a)
-    Y.dma_start(codes(T.c2c, cp + ps, cp + ps + H0), codes(T.c1c, ps, ps + H0)).then_inc(T.sem.cp2, 16)
-    Y.dma_start(T.c2s[:, cp + ps:cp + ps + H0], T.c1s[:, ps:ps + H0]).then_inc(T.sem.cp2, 16)
-    w1, w2 = ("cp1", w1), ("cp2", 96)
+    def junk(n, r=ALL):
+        js[0] += n
+        return T.js[r, js[0] - n:js[0]]
 
-    rm1, rm2 = arrived("rm1", at(1)), arrived("rm2", at(2), at(3))
-    l1, l2, l3 = arrived("l1", at(1)), arrived("l2", at(2)), arrived("l3", at(3))
-    e1 = flags("s", T.f1[:, po:po + COLS], M1, tab(0), None, tm)
-    d1 = flags("s", others(R1), M1, tab(1), T.e1[:, :] if hi else None, rm1)
-    a = mark("v", V.tensor_scalar(T.zb[:, :], T.zi[:, :], 31, None, A.bitwise_and))
-    mark("v", V.tensor_scalar(T.cu[:, 0:2], T.za[:, :], 0.0, None, A.add))
-    tcu = mark("v", V.tensor_scalar(T.cu[:, 2:4], T.za[:, :], 16.0, None, A.add))
-    need("v", a)
-    a = mark("v", V.tensor_scalar(T.ra32[:, :], T.zb[:, 0:1], 0.5, None, A.add))
-    need("s", a, tb32)
-    tkg = mark("s", SC.activation(T.kg[:, :], T.b32[:, :], F.Identity, bias=T.ra32[:, :]))
-    need("s", tkg)
-    tki = mark("s", SC.activation(T.ki[:, :], T.kg[:, :], F.Copy, bias=-0.5))
-    trr = mark("v", V.memset(T.rr[:, :], 0.0))
-    need("v", ("lw", 16))
-    tqw = mark("v", V.quantize_mx(T.wqc[:, :], T.wqs[:, :], T.wt[:, :]))
+    def count_s(acc, key, kcol, *deps):
+        return s(junk(int(key.shape[1])), key, F.Sign, after=deps, bias=kcol, scale=-1.0, accum_out=acc)
 
-    own, came = (T.k1, po, COLS), (T.k1, ps, H0)
+    def compare_v(o, key, kcol, *deps):
+        return v(V.tensor_scalar, o, key, kcol, 0.5, A.is_le, A.subtract, after=deps)
+
+    def total_v(out, o, init, *deps):
+        return v(V.tensor_tensor_scan, out, o, o, init, A.add, A.add, after=deps)
+
+    tti = v(V.tensor_scalar, T.ti[:, :], T.ki[:, 4:8], p1 + COLS * (1 - hi) - 0.5, None, A.add, after=[tki])
+
+    a = v(V.tensor_scalar, T.xi[:, 8:16], T.dmi[:, :], 1 - hi, 0x55, A.logical_shift_right, A.bitwise_and, after=[("ld", 128)])
+    b = v(V.tensor_scalar, T.xi[:, 0:8], T.dmi[:, :], hi, 0x55, A.logical_shift_right, A.bitwise_and)
+    same, other = T.tab[:, 8 * (q & 3):8 * (q & 3) + 8], T.tx[:, :]
+    tm = v(V.tensor_copy, other, T.xi[:, 8:16], after=[a])
+    ts = v(V.tensor_copy, same, T.xi[:, 0:8], after=[b])
+    send(at(1), same, other, "rm1", tm)
+    rm1, rm2 = arrived("rm1", at(1)), arrived("rm2", at(2))
+
+    f = s(T.f0[:, :], lut0.indirect(other), F.Copy, after=[tm, tl0], accum_out=None if hi else T.n0[:, :])
+    tq = quantize("c0", 0, 0, COLS + 2, ("lx", 16), txz)
+    w1 = quantize("c1", p1 + H0 * hi, 0, COLS)
+    ti = v(V.tensor_tensor_scan, T.k0[:, :], T.f0[:, :], T.bz[:, 129 * last:129 * last + COLS], 0.0, A.add, A.add, after=[f, tbz])
     if hi:
-        ta = scan(T.k1[:, po:po + COLS], T.f1[:, po:po + COLS], T.e1[:, :], e1, d1)
+        kz, tkz = (lambda i: T.ki[:, 4 + i:5 + i]), tki
     else:
-        ta = scan(T.k1[:, po:po + COLS], T.f1[:, po:po + COLS], 0.0, e1)
-    sa = early_s(own, not hi, *N1, ta)
-    va = early_v(own, not hi, N1[0], ta)
-    es = flags("v", T.fs[:, cp + po:cp + po + COLS], MS, tab(0), None, tm)
-    d2 = flags("s", others(R2), M2, tab(1), None, rm1)
-    s1 = gather(T.f1[:, ps:ps + H0], tail(R1), T.lt1[:, :], l1, d1)
-    tb = scan(T.k1[:, ps:ps + H0], T.f1[:, ps:ps + H0], 0.0 if hi else T.k1[:, po + COLS - 1:po + COLS], ta, s1)
-    vb = total(late_v(came, not hi, N1[0], tb), va[0], va[2])
-    e2 = flags("s", T.f2[:, cp + po:cp + po + COLS], M2, tab(0), None, tm)
-    sb = late_s(came, not hi, *N1, tb)
-    t1 = complete(T.t1, PAIR, *N1, vb, sa, sb)
-    send(at(2), T.lt2[:, :], T.t1[:, :], "l2", t1)
-    s2 = gather(T.f2[:, cp + ps:cp + ps + H0], tail(R2), T.lt1[:, :], l1, d2)
-    da = flags("s", blk(W2, po, COLS), M2, tab(2), T.ba[:, :], rm2)
-    db = flags("s", others(X2), M2, tab(3), T.bb[:, :], rm2)
-    need("s", da, db)
-    tbs = mark("s", SC.activation(T.bs[:, :], T.ba[:, :], F.Identity, bias=T.bb[:, :]))
-    d3 = flags("v", others(RS), MS, tab(1), None, rm1)
-    d4 = flags("v", others(XS), MS, tab(3), None, rm2)
+        kz, tkz = (lambda i: T.kz[:, i:i + 1]), s(T.kz[:, :], T.ki[:, 0:4], F.Identity, after=[f, tki], bias=T.n0[:, :])
+    go = s(row(T.gg, vo, COLS), lut1.indirect(same), F.Copy, after=[tl1, tl, ts])
+    nv = OPT["j0v"]
+    for i in range(nv, 4):
+        sb = count_s(T.cs[:, i:i + 1], T.k0[:, :], kz(i), ti, tkz)
+        if i == nv:
+            tl1 = put(ALL, 0, [slice(0, 1)], s1, go)
+    ca = [compare_v(T.jv[:, COLS * i:COLS * i + COLS], T.k0[:, :], kz(i), ti, tkz) for i in range(nv)]
+    va = [total_v(T.jw[:, COLS * i:COLS * i + COLS], T.jv[:, COLS * i:COLS * i + COLS], 0.0, ca[i]) for i in range(nv)]
 
-    own, came = (T.k2, cp, PAIR), (T.k2, cb, H1)
-    end = T.k2[:, cp + PAIR - 1:cp + PAIR]
-    if up:
-        ta = scan(T.k2[:, cp:cp + PAIR], T.f2[:, cp:cp + PAIR], T.bs[:, :], e2, s2, tbs)
+    if nv:
+        v(V.tensor_scalar, T.t0[:, 0:nv], T.jw[:, COLS - 1:COLS * nv:COLS], 0.5, COLS / 2, A.mult, A.add, after=va)
+    t0 = v(V.tensor_scalar, T.t0[:, nv:4], T.cs[:, nv:4], 0.5, COLS / 2, A.mult, A.add, after=[sb])
+    if OPT["r2"] == 1:
+        send(at(2), T.tab[:, 16 * up:16 * up + 16], T.tab[:, 16 * up:16 * up + 16], "rm2", rm1, ts)
+    if OPT["r2"] == 2:
+        fused([(at(2), same, same, "rm2", 0, 2), (at(3), same, other, "rm2", 2, 4)], ts)
+    ship(at(1), "c1", p1 + COLS * hi, "sl0", H0, "h0", (pick_codes("sl0", "c0", T.t0, t0, tq), pick_plane("sl0", "c0", T.t0, t0, tq)))
+    if OPT["r2"] == 0:
+        send(at(2), T.tab[:, 16 * up:16 * up + 16], T.tab[:, 16 * up:16 * up + 16], "rm2", rm1, ts)
+
+    h0a = [arrived("h0c", at(1)), arrived("h0s", at(1))]
+    if OPT["cq"] == 0:
+        need("y", w1, *h0a)
+        copy("c2", cp, "c1", p1, PAIR, "cp2")
+        w2 = [("cp2", 32)]
+    if OPT["cq"] == 2:
+        need("y", w1, *h0a)
+        copy("c2", cp + COLS * (1 - hi), "c1", p1 + COLS * (1 - hi), H0, "cp2")
+        w2 = [("cp2", 32)]
+
+    def keys(b, init, *deps):
+        return v(V.tensor_tensor_scan, T.kk[:, VB * b:VB * b + VW + 1], T.gg[:, VB * b:VB * b + VW + 1],
+                 T.bz[:, (VW + 1) * b:(VW + 1) * (b + 1)], init, A.add, A.subtract, after=deps)
+
+    x1 = 8 * ((q ^ 1) & 3)
+    g1 = v(V.tensor_copy, row(T.gg, vs, COLS), lut1.indirect(T.tab[:, x1:x1 + 8]), after=[rm1, tl1])
+    b1 = s(row(T.bz, vs + 1, COLS), lutm.indirect(T.tab[:, x1:x1 + 8]), F.Copy, after=[rm1, tbz], accum_out=None if last else T.nh[:, 0:1])
+    kp = keys(0, 0.0, g1, b1, go, tgz)
+    key_p, key_x = T.kk[:, 0:VW], T.kk[:, VB:VB + VW]
+
+    def flags_x():
+        return s(row(T.gg, VB, VW), lut2.indirect(T.tab[:, 16 * (1 - up):16 * (1 - up) + 16]), F.Copy, after=[rm2, tl2])
+
+    def marks_x():
+        return s(T.bz[:, VW + 2:2 * VW + 2], T.gg[:, VB:VB + VW], F.Relu, after=[gx], scale=2.0, bias=-BIG, accum_out=T.nh[:, 1:2])
+
+    pv = OPT["pv"]
+    mine = [(i, 48 - 16 * i) if up else (5 - i, 80 - 16 * i) for i in range(pv)]
+    theirs = [i for i in range(6) if i not in [m[0] for m in mine]]
+    if OPT["gx"] == -1:
+        gx = flags_x()
+    for i in theirs:
+        ps_ = count_s(T.w1[:, PC + i:PC + i + 1], key_p, T.kp[:, i:i + 1], kp, tk)
+    if OPT["gx"] == 0:
+        gx = flags_x()
+    b2 = marks_x()
+    jv = lambda i, n: T.jv[:, VW * (1 + i) + n:VW * (2 + i)]
+    ca = [compare_v(jv(j, n), T.kk[:, n:VW], T.kp[:, i:i + 1], kp, tk) for j, (i, n) in enumerate(mine)]
+    pa = [total_v(T.w1[:, i + 8 * n:8 * VW:8], jv(j, n), float(n), ca[j]) for j, (i, n) in enumerate(mine)]
+    for r in Q:
+        t1 = v(V.tensor_scalar, T.t1[r, :], T.w1[Q[0], PC:PC + 6], half, to(VW / 2 - H0 * last, PAIR), A.mult, A.add, after=[ps_, *pa])
+    if OPT.get("kx", 0) == 0:
+        kx = keys(1, end_p(ALL), b2, kp)
+
+    R = Q[2]
+    pk = pick_codes("sl1", "c1", T.t1, t1, w1, *h0a)
+    pl = pick_plane("sl1", "c1", T.t1, t1, w1, *h0a)
+    if OPT.get("kx", 0) == 1:
+        kx = keys(1, end_p(ALL), b2, kp)
+    ship(at(2), "c2", (PAIR if up else COLS), "sl1", H1, "h1", (pk, pl))
+    if last:
+        b = s(T.nb[:, :], T.nh[:, 1:2], F.Copy, after=[b2], scale=2 / BIG, bias=-2.0 * (VW - H1))
     else:
-        ta = scan(T.k2[:, cp:cp + PAIR], T.f2[:, cp:cp + PAIR], 0.0, e2, s2)
-    ship(at(2), "c2", PAIR * up, "sl1", H1, "h1",
-         (pick_codes("sl1", "c1", H1, T.t1, t1, w1, *h0a), pick_plane("sl1", "c1", H1, T.t1, t1, w1, *h0a)))
-    need("s", ta, tbs)
-    if up:
-        mark("s", SC.activation(T.nfo[:, 0:1], end, F.Copy))
-        tnf = mark("s", SC.activation(T.nfo[:, 1:2], end, F.Copy, scale=-1.0))
-    else:
-        tnf = mark("s", SC.activation(T.nfo[:, 0:1], end, F.Identity, bias=T.bs[:, :]))
-        need("s", tnf)
-        tnf = mark("s", SC.activation(T.nfo[:, 1:2], T.nfo[:, 0:1], F.Copy, scale=-1.0))
-    send(at(4), T.nfa[:, :], T.nfo[:, :], "nf", tnf)
-    sa = early_s(own, not up, *N2, ta)
-    va = early_v(own, not up, N2[0], ta)
-    s3 = gather(blk(W2, ps, H0), tail(X2), T.lt3[:, :], l3, db)
-    d5 = flags("v", blk(WS, po, COLS), MS, tab(2), None, rm2)
-    if far:
-        need("v", tki)
-        tga = mark("v", V.tensor_scalar(T.ga[:, :], T.ki[:, :], float(H2), None, A.min))
-    s5 = gather(T.fs[:, cp + ps:cp + ps + H0], tail(RS), T.lt1[:, :], l1, d3)
-    s6 = gather(blk(WS, ps, H0), tail(XS), T.lt3[:, :], l3, d4)
-    s4 = gather(T.f2[:, cb:cb + H1], whole(W2), T.lt2[:, :], l2, s3, da)
-    tb = scan(T.k2[:, cb:cb + H1], T.f2[:, cb:cb + H1], 0.0 if up else end, ta, s4)
-    s7 = gather(T.fs[:, cb:cb + H1], whole(WS), T.lt2[:, :], l2, d5, s6)
-    sb = late_s(came, not up, *N2, tb)
-    vb = late_v(came, not up, N2[0], tb)
-    tss = scan(T.ks[:, :], T.fs[:, :], 0.0, es, s5, s7)
+        b = s(T.nh[:, 2:3], T.nh[:, 1:2], F.Identity, after=[b2, b1], bias=T.nh[:, 0:1])
+    number = lambda out, r: s(out, end_x(r), F.Copy, after=[tno, kx])
+    send(at(4), T.nfa[:, :], T.nfo[:, :], "nf", number(T.nfo[R, :], Q[1]))
+    if not last:
+        b = s(T.nb[:, :], T.nh[:, 2:3], F.Copy, after=[b], scale=2 / BIG, bias=-2.0 * (VW - H1 + COLS - H0))
+    xv = OPT["xv"]
+    for i in range(xv, 4):
+        x3 = count_s(T.cs[:, 4 + i:5 + i], key_x, T.kp[:, i:i + 1], kx)
+    if xv:
+        a = compare_v(jv(0, 0), key_x, T.kp[:, 0:1], kx, *pa)
+    b = v(V.tensor_scalar, T.ad[:, :], T.kp[:, 0:4], end_p(ALL), T.nb[:, :], A.is_gt, A.mult, after=[b])
+    if OPT["cq"]:
+        w2q = quantize("c2", cp + H0 * hi, 0, COLS)
+    if OPT["cq"] == 1:
+        a_ = cp + COLS * (1 - hi)
+        w2 = [v(V.tensor_copy, T.c2c[:, a_:a_ + H0].bitcast(U32), T.c1c[:, :].bitcast(U32).indirect(T.ti[:, :]), after=[tti]),
+              s(T.c2s[:, a_:a_ + H0], T.c1s[:, :].indirect(T.ti[:, :]), F.Copy, after=[tti])]
+    if OPT["cq"]:
+        w2 = w2 + [w2q]
+    tpa = v(V.tensor_tensor, T.pa[:, :], T.ad[:, :], T.w1[:, PC:PC + 4], A.add, after=[b])
+    if xv:
+        x0 = total_v(T.w2[:, 0:VW], jv(0, 0), T.pa[:, 0:1], a, tpa, tw2)
+
+    tan = number(T.an[R, 0:1], R)
     nf = arrived("nf", at(4))
-    tke, kE = tkg, T.kg
-    if far:
-        need("s", nf, tkg)
-        tke, kE = mark("s", SC.activation(T.ke[:, :], T.kg[:, :], F.Identity, bias=T.nfa[:, 1:2])), T.ke
-        need("s", tke)
-    vb = total(vb, va[0], va[2])
-    near = (T.ks, 0, NEAR)
-    on_scalar(near, k_(kE, NF), 0, NE, tke, tss)
-    t2 = complete(T.t2, NEAR, *N2, vb, sa, sb)
+    near, away = T.an[R, 0:1], T.nfa[R, :]
+    first, second, n1, n2 = (away, near, H2, S) if far else (near, away, S, H2)
+    tln = s(junk(COLS, R), T.gg[R, vo:vo + COLS], F.Copy, accum_out=T.lnb[R, 1:2])
+
+    def spread_last():
+        if up:
+            a = s(T.an[R, 3:4], second, F.Copy, after=[tan, nf], scale=-0.5, bias=n1 + n2 / 2 - 0.5)
+            s(T.an[R, 1:2], second, F.Copy, scale=0.5, bias=-n2 / 2)
+        else:
+            s(T.an[R, 1:2], first, F.Copy, after=[tan, nf], scale=0.5, bias=-n1 / 2)
+            s(T.an[R, 2:3], first, F.Copy, scale=-0.5, bias=n1 / 2 - 0.5)
+        b = s(T.la[R, 0:16], T.ki[R, 4:20], F.Sign, scale=-1.0, bias=first)
+        if up:
+            b = s(T.an[R, 2:3], first, F.Identity, after=[a], scale=-1.0, bias=T.an[R, 3:4])
+        tA = s(T.lnb[R, 0:1], near, F.Identity, bias=away)
+        for r in Q:
+            a_ = s(T.la[r, 16:32], T.la[R, 0:16], F.Identity, after=[b], scale=T.an[R, 1:2], bias=T.an[R, 2:3])
+        return a_, tA
+    if OPT["sl"] == 0:
+        tla, tA = spread_last()
+
+    a = v(V.tensor_tensor, T.w2[:, XC + 4 * xv:XC + 16:4], T.cs[:, 4 + xv:8], T.pa[:, xv:4], A.add, after=[x3, tw2, tpa])
+    v(V.transpose, T.ta[:, 0:32], T.w2[:, XC:XC + 32], after=[a])
+    a = v(V.transpose, T.ta[:, 48:80], T.w2[:, XC - 16:XC + 16])
+    a = v(V.tensor_scalar, T.tb[:, :], T.ta[:, :].indirect(T.cu[:, :]), half, to(VW - H0 * last, NEAR), A.mult, A.add, after=[a, tcu])
+    tt = v(V.transpose, T.tc[:, :], T.tb[:, :], after=[a])
+    for r in Q:
+        t2 = v(V.tensor_copy, T.t2[r, :], T.tc[Q[1], 0:32:4], after=[tt])
+    for r in Q[0:2]:
+        for i in range(2):
+            a = s(T.tq[r, 8 * i:8 * i + 8], T.tc[Q[2 + i], 0:32:4], F.Copy, after=[tt])
+    a = s(T.tq[UP, :], T.tq[LOW, :], F.Copy, after=[a])
     h1a = [arrived("h1c", at(2)), arrived("h1s", at(2))]
-    ship(at(4), "a2", 0, "sl2", H2, "h2",
-         (pick_codes("sl2", "c2", H2, T.t2, t2, w2, *h1a), pick_plane("sl2", "c2", H2, T.t2, t2, w2, *h1a)))
+    ship(at(4), "a2", 0, "sl2", H2, "h2", (pick_codes("sl2", "c2", T.t2, t2, *w2, *h1a), pick_plane("sl2", "c2", T.t2, t2, *w2, *h1a)))
+    tqw = v(V.quantize_mx, T.wqc[:, :], T.wqs[:, :], T.wt[:, :], after=[("lw", 16)])
+
+    if OPT["sl"] == 1:
+        tla, tA = spread_last()
+    tn = v(V.tensor_copy, T.tn[:, :], T.tq[:, :], after=[a])
+    pn = (pick_codes("cn", "c2", T.tn, tn), pick_plane("cn", "c2", T.tn, tn))
 
     def product(o, bank, c, n, *deps):
         need("t", tqw, *deps)
         return mark("t", TE.matmul_mx(T.ps[:, 512 * bank:512 * bank + n], T.wqc[:, 128 * o:128 * o + 128], T.wqs[:, 128 * o:128 * o + 128],
                                       T[c + "c"][:, 0:n], T[c + "s"][:, 0:n], True, True))
-    m0 = product(0, 0, "c2", NEAR, w2, *h1a)
-    m1 = product(1, 1, "c2", NEAR)
+    m0 = product(0, 0, "cn", S, *pn)
+    m1 = product(1, 1, "cn", S)
 
-    cmp = compare(near, k_(kE, 0), lambda i: 0, NF, tke, tss)
-    _, lst = on_scalar(near, k_(kE, NF + NE), 0, 8 - NF - NE, tke, tss)
-    ls_ = T.cs[:, use["cs"] - 8 + NF:use["cs"]]
-    need("s", lst)
-    ths = mark("s", SC.activation(T.hs[:, 0:8 - NF], ls_, F.Copy, scale=0.5, bias=-LOW))
-    need("v", tki)
-    if far:
-        need("v", nf)
-        a = mark("v", V.tensor_scalar(T.gb[:, :], T.ki[:, :], T.nfa[:, 0:1], float(H2), A.is_ge, A.mult))
-        _, lv_, lvt = total(cmp, lambda i: -LOW)
-        need("v", tga, a)
-        tgt = mark("v", V.tensor_tensor(T.gt[:, :], T.ga[:, :], T.gb[:, :], A.max))
-    else:
-        tgt = mark("v", V.tensor_scalar(T.gt[:, :], T.ki[:, :], T.ks[:, NEAR - 1:NEAR], 0.0, A.subtract, A.max))
-        _, lv_, lvt = total(cmp, lambda i: -LOW)
-    need("v", lvt, tgt, trr)
-    mark("v", V.tensor_tensor(T.rr[:, 0:NF], lv_, T.gt[:, 0:NF], A.add))
-    need("v", ths)
-    a = mark("v", V.tensor_tensor(T.rr[:, NF:8], T.hs[:, 0:8 - NF], T.gt[:, NF:8], A.add))
-    need("v", a)
-    a = mark("v", V.transpose(T.ra[:, :], T.rr[:, :]))
-    need("v", a, tcu)
-    a = mark("v", V.tensor_copy(T.rb[:, :], T.ra[:, :].indirect(T.cu[:, :])))
-    need("v", a)
-    a = mark("v", V.transpose(T.rc[:, :], T.rb[:, :]))
-    need("v", a)
-    mark("v", V.tensor_scalar(T.tf[:, 0:16:2], T.rc[:, 0:8], NEAR / 2 + LOW, float(ZERO), A.add, A.min))
-    ttf = mark("v", V.tensor_scalar(T.tf[:, 1:16:2], T.rc[:, 32:40], NEAR / 2 + LOW, float(ZERO), A.add, A.min))
-    need("s", m0)
-    g0a = mark("s", SC.activation(T.g0[:, gn:gn + NEAR], T.ps[:, 0:NEAR], F.Copy))
-    need("s", m1)
-    g1a = mark("s", SC.activation(T.g1[:, gn:gn + NEAR], T.ps[:, 512:512 + NEAR], F.Copy))
+    if OPT["sl"] == 2:
+        tla, tA = spread_last()
+    a = v(V.tensor_tensor, T.la[:, 32:48], T.la[:, 16:32], T.ki[:, 4:20], A.add, after=[tla])
+    ttf = v(V.tensor_scalar, T.tf[:, :], T.la[:, 32:48], float(ZERO), None, A.min, after=[a])
+    need("y", tA, tln)
+    Y.dma_start(T.ln[:, :], T.lnb[64:65, :]).then_inc(T.sem.sln, 16)
+    g0a = v(V.tensor_copy, T.gr[:, gn:gn + S], T.ps[:, 0:S], after=[m0])
+    g1a = s(T.gr[:, GW + gn:GW + gn + S], T.ps[:, 512:512 + S], F.Copy, after=[m1])
 
     h2a = [arrived("h2c", at(4)), arrived("h2s", at(4))]
     m2 = product(0, 2, "a2", H2, *h2a)
     m3 = product(1, 3, "a2", H2)
-    need("s", m2)
-    b0 = mark("s", SC.activation(T.g0[:, gf:gf + H2], T.ps[:, 1024:1024 + H2], F.Copy))
-    need("s", m3)
-    b1 = mark("s", SC.activation(T.g1[:, gf:gf + H2], T.ps[:, 1536:1536 + H2], F.Copy))
-    need("v", b0, g0a, tz, ttf)
-    y0 = mark("v", V.tensor_copy(T.y0[:, :], T.g0[:, :].indirect(T.tf[:, :])))
-    need("s", b1, g1a, tz, ttf)
-    y1 = mark("s", SC.activation(T.y1[:, :], T.g1[:, :].indirect(T.tf[:, :]), F.Copy))
+    f0 = v(V.tensor_copy, T.gr[:, gf:gf + H2], T.ps[:, 1024:1024 + H2], after=[m2])
+    f1 = s(T.gr[:, GW + gf:GW + gf + H2], T.ps[:, 1536:1536 + H2], F.Copy, after=[m3])
+    y0 = v(V.tensor_copy, T.y0[:, :], T.gr[:, 0:ZERO + 1].indirect(T.tf[:, :]), after=[f0, g0a, tz, ttf])
+    y1 = s(T.y1[:, :], T.gr[:, GW:GW + ZERO + 1].indirect(T.tf[:, :]), F.Copy, after=[f1, g1a, tz, ttf])
     need("y", y0)
     Y.dma_start(T.y[:, 0:S], T.y0[:, :]).then_inc(T.sem.sya, 16)
     need("s", y1)
     SC.dma_start(T.y[:, S:2 * S], T.y1[:, :]).then_inc(T.sem.syb, 16)
-    need("s", tss, nf)
-    mark("s", SC.activation(T.lnb[0:1, 0:1], T.nfa[0:1, 0:1], F.Identity, bias=T.ks[0:1, NEAR - 1:NEAR]))
-    c = cp + po
-    if c:
-        tln = mark("s", SC.activation(T.lnb[0:1, 1:2], T.ks[0:1, c - 1:c], F.Identity, bias=T.ks[0:1, c + COLS - 1:c + COLS], scale=-1.0))
-    else:
-        tln = mark("s", SC.activation(T.lnb[0:1, 1:2], T.ks[0:1, COLS - 1:COLS], F.Copy))
-    need("y", tln)
-    Y.dma_start(T.ln[:, :], T.lnb[:, :]).then_inc(T.sem.sln, 16)
 
     need("p", ("loc", sent[0]), ("qv", done["v"]), ("qs", done["s"]), ("qt", done["t"]), ("qp", done["p"]))
     need("y", ("sln", 16), ("sya", 16))

@@ -11,18 +11,27 @@ NEAR = PAIR + H1
 ZERO = S + H2
 GW = ZERO + 8
 BIG = 256.0
+ROUND = 1.5 * 2 ** 31
 VW, VB = 2 * COLS, 264
 PC = 8 * (VW - 1)
-
 XC = VW - 1
-OPT = {"j0v": 2, "pv": 3, "xv": 1, "r2": 2, "gx": 0, "sl": 2, "kx": 0, "cq": 1}
+
+ORDER = {
+    "v": "and1 and0 cast1 castz cast0 castq q0 q1 k0 q2 a0 a1 b0 b1 t0 pk0 g1 kp pa0 m2 pb0 kx u1 ad1 t1 pp pk1 xa ad sc pa xb x "
+         "qw0 turn1 qw1 turn2 turn3 t2 pk2 tn pkn l2 la tf n0 f0 y00",
+    "s": "m0 km f kz go c0 c1 c2 c3 c4 c5 mark pl0 m1 gx nb1 p0 nh p1 nb p2 p3 ca nf x0 x1 pl1 x2 x3 ss an t2a own tq pl2 pln l0 l1 all n1 f1 y10 sy10",
+    "p": "rm1 rm2 sl1 h0c h0s snf h1c h1s h2c h2s",
+    "t": "mn0 mn1 mf0 mf1",
+    "y": "sw sc2 sln sy00",
+}
+OC = 8 * (COLS - 1)
+OPT = {"j0v": 2, "pv": 1, "xv": 1, "m2": "v", "ns": 1, "sw": "", "nl": 8, "e1": 1, "cq": 1, "t2": "s"}
 CODE, PLANE = "float8_e4m3fn_x4", "uint8"
 SCRATCH = {
     "dmi": ("sbuf", [128, 8], "int32"), "xt": ("sbuf", [128, 1024], "bfloat16"), "wt": ("sbuf", [128, 1024], "bfloat16"),
     "c0c": ("sbuf", [128, COLS + 2], CODE), "c0s": ("sbuf", [128, COLS + 2], PLANE),
-    "c1c": ("sbuf", [128, PAIR + COLS], CODE), "c1s": ("sbuf", [128, PAIR + COLS], PLANE),
+    "c1c": ("sbuf", [128, PAIR], CODE), "c1s": ("sbuf", [128, PAIR], PLANE),
     "c2c": ("sbuf", [128, NEAR + COLS], CODE), "c2s": ("sbuf", [128, NEAR + COLS], PLANE),
-    "ti": ("sbuf", [128, 4], "uint16"),
     "cnc": ("sbuf", [128, S], CODE), "cns": ("sbuf", [128, S], PLANE),
     "a2c": ("sbuf", [128, H2], CODE), "a2s": ("sbuf", [128, H2], PLANE),
     "wqc": ("sbuf", [128, 256], CODE), "wqs": ("sbuf", [128, 256], PLANE),
@@ -31,17 +40,18 @@ SCRATCH = {
     "sl2c": ("sbuf", [128, H2], CODE), "sl2s": ("sbuf", [128, H2], PLANE),
     "xi": ("sbuf", [128, 16], "int32"), "tx": ("sbuf", [128, 8], "uint16"), "tab": ("sbuf", [128, 32], "uint16"),
     "nfo": ("sbuf", [128, 1], "float32"), "nfa": ("sbuf", [128, 1], "float32"),
-    "lut": ("sbuf", [128, 448], "bfloat16"), "zi": ("sbuf", [128, 2], "int32"), "za": ("sbuf", [128, 2], "int32"),
+    "lut": ("sbuf", [128, 544], "bfloat16"), "zi": ("sbuf", [128, 2], "int32"), "za": ("sbuf", [128, 2], "int32"),
     "zh": ("sbuf", [128, 2], "int32"), "ra": ("sbuf", [128, 1], "float32"), "c64": ("sbuf", [128, 2], "float32"),
-    "cu": ("sbuf", [128, 2], "uint16"), "b16": ("sbuf", [128, 32], "float32"), "ki": ("sbuf", [128, 20], "float32"),
-    "kc": ("sbuf", [128, 6], "float32"),
-    "f0": ("sbuf", [128, COLS], "bfloat16"), "k0": ("sbuf", [128, COLS], "bfloat16"), "gg": ("sbuf", [128, 2 * VB], "bfloat16"),
+    "cu": ("sbuf", [128, 2], "uint16"), "b16": ("sbuf", [128, 32], "float32"), "ki": ("sbuf", [128, 22], "float32"),
+    "kc": ("sbuf", [128, 4], "float32"), "kp": ("sbuf", [128, 4], "float32"), "ti": ("sbuf", [128, 4], "uint16"),
+    "fb": ("sbuf", [128, 2 * COLS + 2], "bfloat16"), "k0": ("sbuf", [128, COLS], "bfloat16"), "n0": ("sbuf", [128, 2], "float32"),
+    "km": ("sbuf", [128, 6], "float32"), "tr": ("sbuf", [128, 8], "float32"), "gg": ("sbuf", [128, 2 * VB], "bfloat16"),
     "bz": ("sbuf", [128, 2 * VW + 2], "bfloat16"), "kk": ("sbuf", [128, 2 * VB], "bfloat16"),
-    "n0": ("sbuf", [128, 1], "float32"), "kz": ("sbuf", [128, 4], "float32"), "kp": ("sbuf", [128, 6], "float32"),
-    "kx": ("sbuf", [128, 4], "float32"),
-    "js": ("sbuf", [128, 14 * VW], "bfloat16"), "jv": ("sbuf", [128, 4 * VW], "bfloat16"), "jw": ("sbuf", [128, VW], "bfloat16"),
+    "kz": ("sbuf", [128, 6], "float32"), "tz": ("sbuf", [128, 8], "uint16"),
+    "lt": ("sbuf", [128, 8], "float32"), "u1": ("sbuf", [128, 6], "float32"),
+    "js": ("sbuf", [128, 14 * VW], "bfloat16"), "jv": ("sbuf", [128, 6 * VW], "bfloat16"), "w0": ("sbuf", [128, 8 * COLS], "float32"),
     "cs": ("sbuf", [128, 8], "float32"), "w1": ("sbuf", [128, 8 * VW], "float32"), "w2": ("sbuf", [128, VW + 32], "float32"),
-    "nh": ("sbuf", [128, 3], "float32"), "nb": ("sbuf", [128, 1], "bfloat16"), "ad": ("sbuf", [128, 4], "float32"),
+    "nh": ("sbuf", [128, 4], "float32"), "nb": ("sbuf", [128, 3], "bfloat16"), "ad": ("sbuf", [128, 12], "float32"),
     "pa": ("sbuf", [128, 4], "float32"),
     "ta": ("sbuf", [128, 80], "float32"), "tb": ("sbuf", [128, 32], "float32"), "tc": ("sbuf", [128, 32], "float32"),
     "t0": ("sbuf", [128, 4], "uint16"), "t1": ("sbuf", [128, 6], "uint16"), "t2": ("sbuf", [128, 8], "uint16"),
@@ -50,8 +60,8 @@ SCRATCH = {
     "gr": ("sbuf", [128, 2 * GW], "float32"), "y0": ("sbuf", [128, 256], "float32"), "y1": ("sbuf", [128, 256], "float32"),
     "ps": ("psum", [128, 2048], "float32"),
 }
-ARR = ["rm1", "rm2", "nf", "h0c", "h0s", "h1c", "h1s", "h2c", "h2s"]
-SEMAPHORES = ["qv", "qs", "qt", "qp", "ld", "lx", "lw", "cp1", "cp2", "sya", "syb", "sln", "loc"] + ARR
+ARR = ["rm1", "rm2", "l1", "nf", "h0c", "h0s", "h1c", "h1s", "h2c", "h2s"]
+SEMAPHORES = ["qv", "qs", "qt", "qp", "ld", "lx", "lw", "cp2", "sya", "syb", "sln", "loc"] + ARR
 
 
 def rank_program(g, core, T, topo):
@@ -87,28 +97,22 @@ def rank_program(g, core, T, topo):
 
     sent = [0]
 
-    def send(dst, out, in_, sem, *deps):
-        need("p", *deps)
+    def send(dst, out, in_, sem, share=1):
         rid, pid = topo.addr(dst, core)
-        g.remote_dma(out, in_, T.sem[sem], T.sem["loc"], pid, rid, topo.mask(core, dst))
-        sent[0] += len(topo.engines(core, dst))
+        e = topo.engines(core, dst)[::share]
+        g.remote_dma(out, in_, T.sem[sem], T.sem["loc"], pid, rid, sum(1 << n for n in e))
+        sent[0] += len(e)
 
-    def part(src, dst, a, b):
-        e = topo.engines(src, dst)
-        return e[a * len(e) // 4:b * len(e) // 4]
-
-    def fused(writes, *deps):
-        need("p", *deps)
+    def send2(writes, sem):
         tr = []
-        for d, out, in_, sem, a, b in writes:
+        for i, (d, out, in_) in enumerate(writes):
             rid, pid = topo.addr(d, core)
-            tr.append(RemoteDMATransfer(dst_ids=[DstId(rid=rid, pnc=pid)], dma_engine_mask=sum(1 << e for e in part(core, d, a, b)),
+            e = topo.engines(core, d)
+            e = e[i * len(e) // 2:(i + 1) * len(e) // 2]
+            tr.append(RemoteDMATransfer(dst_ids=[DstId(rid=rid, pnc=pid)], dma_engine_mask=sum(1 << n for n in e),
                                         remote_sem=T.sem[sem], srcs=[in_], dsts=[out]))
-            sent[0] += len(part(core, d, a, b))
+            sent[0] += len(e)
         g.remote_dma_fused(tr, local_sem=T.sem["loc"])
-
-    def arrived(sem, *srcs):
-        return (sem, sum(len(topo.engines(c, core)) for c in srcs))
 
     at = lambda x: T.cores[q ^ x]
     codes = lambda t, a, b: t[:, a:b].bitcast(U8)
@@ -117,288 +121,270 @@ def rank_program(g, core, T, topo):
 
     hi, up, far = q & 1, (q >> 1) & 1, q >> 2
     last = hi ^ up
-    p1 = COLS * up
+    QO, QP = Q[2 + hi], Q[3 - hi]
+    s0 = BIG if hi else -BIG
     cp = (COLS + H1) * up
     vo, vs = COLS * last, COLS * (1 - last)
     gn, gf = H2 * far, S * (1 - far)
     s1 = -BIG if last else BIG
     row = lambda t, a, n: t[:, a + n - 1:a - 1 if a else None:-1] if up else t[:, a:a + n]
     half, to = (-0.5 if up else 0.5), (lambda c, n: COLS + n - 1 - c if up else c)
-    lut1, lut2, lut0, lutm = T.lut[:, 0:96], T.lut[:, 128:224], T.lut[:, 256:352], T.lut[:, 352:448]
+    lut1, lut2, lut0, lutm, lutz = (T.lut[:, a:a + 96] for a in (0, 128, 256, 352, 448))
     end_p, end_x = (lambda r: T.kk[r, VW:VW + 1]), (lambda r: T.kk[r, VB + VW:VB + VW + 1])
 
-    for i in range(8):
+    for i in range(OPT["nl"]):
         (Y if i % 2 == 0 else SC).dma_start(T.dmi[16 * i:16 * i + 16, :], T.dm[:, :]).then_inc(T.sem.ld, 16)
     Y.dma_start(T.xt[:, 0:512], T.x[:, :]).then_inc(T.sem.lx, 16)
-    Y.dma_start(T.wt[:, :], T.w[:, :]).then_inc(T.sem.lw, 16)
 
     place = lambda d: d - hi
     bit = lambda b: [[0, 64 >> b], [1, 4], [0, 1 << b]] if b < 6 else [[0, 2], [1, 2], [0, 64]]
     both = lambda e: [slice(0, e + 1, e), slice(16 * e, 17 * e + 1, e)]
     iota = lambda o, pat, base=0: mark("p", g.iota(o, pat, base, 0, allow_small_or_imprecise_dtypes=True))
     tzi = mark("p", g.iota(T.zi[:, :], [[0, 2]], 0, 1))
-    need("p", tb16 := iota(T.b16[:, :], [[16, 32]], -256))
-    need("p", iota(T.lut[Q[1], 0:256], bit(place(q ^ 4))))
-    need("p", tl := iota(T.lut[UP, 0:256], bit(place(q))))
-    b16 = lambda r, a: T.b16[r, (a + 256) // 16:(a + 256) // 16 + 6]
+    tb16 = iota(T.b16[:, :], [[16, 32]], -256)
+    need("p", tb16)
+    need("p", iota(T.lut[LOW, 0:256], bit(place(q ^ 4))))
+    tl = iota(T.lut[UP, 0:256], bit(place(q)))
+    b16 = lambda r, a: T.b16[r, (a + 256) // 16:(a + 256) // 16 + 4]
 
-    v(V.memset, T.lut[:, 257:352], 1.0)
-    tl0 = v(V.memset, T.lut[:, 256:257], 0.0)
+    def quantize(to, a, b, n):
+        return V.quantize_mx(T[to + "c"][:, a:a + n], T[to + "s"][:, a:a + n], T.xt[:, 4 * b:4 * (b + n)])
+
+    tbz = v(V.memset, T.bz[:, 0:VW + 2], 0.0)
     za = v(V.tensor_scalar, T.za[:, :], T.zi[:, :], 15, None, A.bitwise_and, after=[tzi])
     zh = v(V.tensor_scalar, T.zh[:, :], T.zi[:, :], 16, None, A.bitwise_and)
-    v(V.memset, T.lut[Q[0], 0:128], 1.0)
+    v(V.memset, lut0, 1.0)
     tra = v(V.tensor_scalar, T.ra[:, :], T.za[:, 0:1], 0.5, None, A.add, after=[za])
-    tq0 = v(V.memset, T.lut[Q[0], 128:256], 0.0)
+    tl0 = v(V.memset, T.lut[:, 352:544], 0.0)
     t64 = v(V.tensor_scalar, T.c64[:, :], T.zh[:, :], 4.0, T.ra[:, :], A.mult, A.add, after=[tra, zh])
-    tbz = v(V.memset, T.bz[:, 0:VW + 2], 0.0)
-    tcu = v(V.tensor_scalar, T.cu[:, :], T.c64[:, :], -0.5, None, A.add, after=[t64])
     txz = v(V.memset, T.xt[:, 512:1024], 0.0)
-    tgz = v(V.memset, T.gg[:, VW:2 * VB:VB], 0.0)
+    v(V.tensor_scalar, T.cu[:, :], T.c64[:, :], -0.5, None, A.add, after=[t64])
+    v(quantize, "c2", NEAR * (1 - up), COLS, COLS, after=[txz])
+    v(V.memset, T.lt[:, 4 * hi + 2 - 2 * hi:4 * hi + 4 - 2 * hi], float(COLS if hi else -COLS))
+    v(V.memset, T.fb[:, COLS:COLS + 1], 0.0)
+    v(V.memset, T.gg[:, VW:2 * VB:VB], 0.0)
 
-    def quantize(to, a, b, n, *deps):
-        return v(V.quantize_mx, T[to + "c"][:, a:a + n], T[to + "s"][:, a:a + n], T.xt[:, 4 * b:4 * (b + n)], after=deps)
-
-    quantize("c1", PAIR * (1 - up), COLS, COLS, txz)
-    quantize("c2", NEAR * (1 - up), COLS, COLS)
-
-    def fill(o, rows, val, *deps):
-        return s(o, T.lut[rows, 257:257 + int(o.shape[1])], F.Copy, after=[tl0, *deps], scale=0.0, bias=val)
+    def fill(o, rows, val):
+        return SC.activation(o, T.bz[rows, 0:int(o.shape[1])], F.Copy, scale=0.0, bias=val)
 
     def put(rows, base, cols, val, *deps):
+        need("s", *deps)
         for c in cols:
-            t = fill(T.lut[rows, base + c.start:base + c.stop:c.step or 1], rows, val, *deps)
+            t = mark("s", fill(T.lut[rows, base + c.start:base + c.stop:c.step or 1], rows, val))
         return t
 
-    put(ALL, 352, [slice(1, 96)], 0.0)
+    need("s", tbz)
+    for o in (T.ta[:, 32:48], T.gr[:, ZERO:2 * GW:GW], T.nfo[:, :], T.w2[:, XC - 16:XC + 32]):
+        mark("s", fill(o, ALL, 0.0))
+    a = put(UP, 256, both(1 << place(q & 3)), 0.0, tl0)
+    put(LOW, 256, [slice(0, 1)], 0.0)
     put(ALL, 352, [slice(0, 1)], s1)
-    fill(T.ta[:, 32:48], ALL, 0.0)
-    tz = fill(T.gr[:, ZERO:2 * GW:GW], ALL, 0.0)
-    tno = fill(T.nfo[:, :], ALL, 0.0)
-    tw2 = fill(T.w2[:, XC - 16:XC + 32], ALL, 0.0)
-    tki = s(T.ki[:, :], T.b16[:, 12:32], F.Identity, after=[tra, tb16], bias=T.ra[:, :])
-    tl1 = put(Q[0], 0, both(1 << place(q & 3)), 0.0, tq0)
+    put(QP, 448, [slice(0, 1)], s0)
+    tki = s(T.ki[:, :], T.b16[:, 10:32], F.Identity, after=[tra, tb16], bias=T.ra[:, :])
+    put(QP, 256, [slice(0, 1)], s0, a)
     kb = T.kc if up else T.kp
-    s(kb[Q[0], :], b16(Q[0], -H1 * up), F.Identity, bias=T.ra[Q[0], :])
-    for i, a in ((1, -H2 * up), (2, -S * up), (3, 128 - S * up)):
-        tk = s(kb[Q[i], :], b16(Q[i], a), F.Identity, after=[t64], bias=T.c64[Q[i], 0:1])
+    for i, a, n, c in ((0, 0, H2, T.ra), (1, 64, H2, T.ra), (2, 0, S, T.c64), (3, 128, S, T.c64)):
+        tk = s(kb[Q[i], :], b16(Q[i], a - (n if up else S)), F.Identity, after=[t64], bias=c[Q[i], 0:1])
+    s(T.kz[LOW if hi else UP, :], T.ki[LOW if hi else UP, 6:12], F.Copy, after=[tki])
     if up:
-        tk = s(T.kp[:, :], T.kc[:, :], F.Copy, after=[tk], scale=-1.0)
-    tl2 = put(ALL, 128, both(1 << place((q ^ 2) & 3)), BIG, tl)
+        s(T.kp[:, :], T.kc[:, :], F.Copy, after=[tk], scale=-1.0, bias=-BIG)
+    put(ALL, 128, both(1 << place((q ^ 2) & 3)), BIG, tl)
+    v(V.tensor_scalar, T.ti[:, :], T.ki[:, 6:10], COLS * (1 - hi) - 0.5, None, A.add, after=[tki])
 
-    def pick_codes(out, src, tab_, *deps):
-        return v(V.tensor_copy, T[out + "c"][:, :].bitcast(U32), T[src + "c"][:, :].bitcast(U32).indirect(tab_[:, :]), after=deps)
+    arrived = lambda sem, src: (sem, len(topo.engines(src, core)))
+    tok = {"cv": ("qv", done["v"]), "cs": ("qs", done["s"]), "cp": tl, "dm": ("ld", 16 * OPT["nl"]), "xl": ("lx", 16), "wl": ("lw", 16),
+           "Rm1": ("rm1", len(topo.engines(at(1), core)[::OPT["e1"]])), "Rm2": arrived("rm2", at(2)), "Nf": arrived("nf", at(4)),
+           "L1": arrived("l1", at(1))}
+    for b in range(3):
+        tok["H%dc" % b], tok["H%ds" % b] = arrived("h%dc" % b, at(1 << b)), arrived("h%ds" % b, at(1 << b))
+    ops = {}
 
-    def pick_plane(out, src, tab_, *deps):
-        return s(T[out + "s"][:, :], T[src + "s"][:, :].indirect(tab_[:, :]), F.Copy, after=deps)
+    def op(name, e, deps, *calls):
+        ops[name] = (e, deps.split(), calls)
 
-    def ship(dst, to, a_, src, n, sem, tok):
-        send(dst, codes(T[to + "c"], a_, a_ + n), codes(T[src + "c"], 0, n), sem + "c", tok[0])
-        send(dst, T[to + "s"][:, a_:a_ + n], T[src + "s"][:, 0:n], sem + "s", tok[1])
-
-    def copy(to, a_, src, b_, n, sem):
-        Y.dma_start(codes(T[to + "c"], a_, a_ + n), codes(T[src + "c"], b_, b_ + n)).then_inc(T.sem[sem], 16)
-        Y.dma_start(T[to + "s"][:, a_:a_ + n], T[src + "s"][:, b_:b_ + n]).then_inc(T.sem[sem], 16)
-
+    act = lambda o, i, f, **k: (lambda: SC.activation(o, i, f, **k))
+    ts = lambda *a: (lambda: V.tensor_scalar(*a))
+    cp_ = lambda o, i: (lambda: V.tensor_copy(o, i))
     js = [0]
 
     def junk(n, r=ALL):
         js[0] += n
         return T.js[r, js[0] - n:js[0]]
 
-    def count_s(acc, key, kcol, *deps):
-        return s(junk(int(key.shape[1])), key, F.Sign, after=deps, bias=kcol, scale=-1.0, accum_out=acc)
+    count = lambda acc, key, k: act(junk(int(key.shape[1])), key, F.Sign, bias=k, scale=-1.0, accum_out=acc)
+    compare = lambda o, key, k: ts(o, key, k, 0.5, A.is_le, A.subtract)
+    total = lambda out, o, init: (lambda: V.tensor_tensor_scan(out, o, o, init, A.add, A.add))
 
-    def compare_v(o, key, kcol, *deps):
-        return v(V.tensor_scalar, o, key, kcol, 0.5, A.is_le, A.subtract, after=deps)
+    def pick(names, deps, out, a, n, src, tab_):
+        op(names[0], "v", deps[0], cp_(T[out + "c"][:, a:a + n].bitcast(U32), T[src + "c"][:, :].bitcast(U32).indirect(tab_[:, :])))
+        op(names[1], "s", deps[1], act(T[out + "s"][:, a:a + n], T[src + "s"][:, :].indirect(tab_[:, :]), F.Copy))
 
-    def total_v(out, o, init, *deps):
-        return v(V.tensor_tensor_scan, out, o, o, init, A.add, A.add, after=deps)
+    def step(b, deps, src, tab_, n, to_, a):
+        c, p_, o = "pk%d" % b, "pl%d" % b, "sl%d" % b
+        pick((c, p_), deps, o, 0, n, src, tab_)
+        op("h%dc" % b, "p", c, lambda: send(at(1 << b), codes(T[to_ + "c"], a, a + n), codes(T[o + "c"], 0, n), "h%dc" % b))
+        op("h%ds" % b, "p", p_, lambda: send(at(1 << b), T[to_ + "s"][:, a:a + n], T[o + "s"][:, 0:n], "h%ds" % b))
 
-    tti = v(V.tensor_scalar, T.ti[:, :], T.ki[:, 4:8], p1 + COLS * (1 - hi) - 0.5, None, A.add, after=[tki])
-
-    a = v(V.tensor_scalar, T.xi[:, 8:16], T.dmi[:, :], 1 - hi, 0x55, A.logical_shift_right, A.bitwise_and, after=[("ld", 128)])
-    b = v(V.tensor_scalar, T.xi[:, 0:8], T.dmi[:, :], hi, 0x55, A.logical_shift_right, A.bitwise_and)
     same, other = T.tab[:, 8 * (q & 3):8 * (q & 3) + 8], T.tx[:, :]
-    tm = v(V.tensor_copy, other, T.xi[:, 8:16], after=[a])
-    ts = v(V.tensor_copy, same, T.xi[:, 0:8], after=[b])
-    send(at(1), same, other, "rm1", tm)
-    rm1, rm2 = arrived("rm1", at(1)), arrived("rm2", at(2))
+    nl = OPT["nl"]
+    L = slice(0, 16 * nl)
+    parts = [slice(16 * nl * i, 16 * nl * (i + 1)) for i in range(8 // nl)]
+    op("and1", "v", "dm", ts(T.xi[L, 8:16], T.dmi[L, :], 1 - hi, 0x55, A.logical_shift_right, A.bitwise_and))
+    op("and0", "v", "dm", ts(T.xi[L, 0:8], T.dmi[L, :], hi, 0x55, A.logical_shift_right, A.bitwise_and))
+    op("cast1", "v", "and1", *[cp_(T.tx[r, :], T.xi[L, 8:16]) for r in parts])
+    op("cast0", "v", "and0", *[cp_(T.tab[r, 8 * (q & 3):8 * (q & 3) + 8], T.xi[L, 0:8]) for r in parts])
+    op("rm1", "p", "cast1", lambda: send(at(1), same, other, "rm1", OPT["e1"]))
+    op("rm2", "p", "cast0 cast1", lambda: send2([(at(2), same, same), (at(3), same, other)], "rm2"))
+    op("q0", "v", "xl cv", lambda: quantize("c0", 0, 0, COLS + 2))
+    op("q1", "v", "xl", lambda: quantize("c1", H0 * hi, 0, COLS))
+    op("q2", "v", "xl", lambda: quantize("c2", cp + H0 * hi, 0, COLS))
+    for i in range(2):
+        op("qw%d" % i, "v", "wl", lambda i=i: V.quantize_mx(T.wqc[:, 128 * i:128 * i + 128], T.wqs[:, 128 * i:128 * i + 128],
+                                                          T.wt[:, 512 * i:512 * i + 512]))
 
-    f = s(T.f0[:, :], lut0.indirect(other), F.Copy, after=[tm, tl0], accum_out=None if hi else T.n0[:, :])
-    tq = quantize("c0", 0, 0, COLS + 2, ("lx", 16), txz)
-    w1 = quantize("c1", p1 + H0 * hi, 0, COLS)
-    ti = v(V.tensor_tensor_scan, T.k0[:, :], T.f0[:, :], T.bz[:, 129 * last:129 * last + COLS], 0.0, A.add, A.add, after=[f, tbz])
+    op("castz", "v", "and1", cp_(T.tz[:, :], T.xi[:, 8:16]))
+    op("castq", "v", "and0 castz", cp_(T.tz[QO, :], T.xi[QO, 0:8]))
+    op("f", "s", "castq cv cs", act(T.fb[:, 0:COLS], lut0.indirect(T.tz[:, :]), F.Copy, accum_out=T.n0[:, 0:1]))
+    op("m0", "s", "cast1 cv cs", act(T.fb[:, COLS + 1:2 * COLS + 1], lutz.indirect(other), F.Copy, scale=-1.0, accum_out=T.n0[:, 1:2] if hi else None))
+    op("k0", "v", "f m0", lambda: V.tensor_tensor_scan(T.k0[:, :], T.fb[:, 0:COLS], T.fb[:, COLS:2 * COLS], 0.0, A.add, A.add))
     if hi:
-        kz, tkz = (lambda i: T.ki[:, 4 + i:5 + i]), tki
+        op("km", "s", "m0 cs", act(T.km[UP, :], T.ki[UP, 0:6], F.Identity, bias=T.n0[UP, 1:2]))
+        op("kz", "s", "f km", act(T.kz[UP, :], T.km[UP, :], F.Identity, bias=T.n0[UP, 0:1]))
     else:
-        kz, tkz = (lambda i: T.kz[:, i:i + 1]), s(T.kz[:, :], T.ki[:, 0:4], F.Identity, after=[f, tki], bias=T.n0[:, :])
-    go = s(row(T.gg, vo, COLS), lut1.indirect(same), F.Copy, after=[tl1, tl, ts])
+        op("kz", "s", "f cs", act(T.kz[LOW, :], T.ki[LOW, 2:8], F.Identity, bias=T.n0[LOW, 0:1]))
     nv = OPT["j0v"]
-    for i in range(nv, 4):
-        sb = count_s(T.cs[:, i:i + 1], T.k0[:, :], kz(i), ti, tkz)
-        if i == nv:
-            tl1 = put(ALL, 0, [slice(0, 1)], s1, go)
-    ca = [compare_v(T.jv[:, COLS * i:COLS * i + COLS], T.k0[:, :], kz(i), ti, tkz) for i in range(nv)]
-    va = [total_v(T.jw[:, COLS * i:COLS * i + COLS], T.jv[:, COLS * i:COLS * i + COLS], 0.0, ca[i]) for i in range(nv)]
-
-    if nv:
-        v(V.tensor_scalar, T.t0[:, 0:nv], T.jw[:, COLS - 1:COLS * nv:COLS], 0.5, COLS / 2, A.mult, A.add, after=va)
-    t0 = v(V.tensor_scalar, T.t0[:, nv:4], T.cs[:, nv:4], 0.5, COLS / 2, A.mult, A.add, after=[sb])
-    if OPT["r2"] == 1:
-        send(at(2), T.tab[:, 16 * up:16 * up + 16], T.tab[:, 16 * up:16 * up + 16], "rm2", rm1, ts)
-    if OPT["r2"] == 2:
-        fused([(at(2), same, same, "rm2", 0, 2), (at(3), same, other, "rm2", 2, 4)], ts)
-    ship(at(1), "c1", p1 + COLS * hi, "sl0", H0, "h0", (pick_codes("sl0", "c0", T.t0, t0, tq), pick_plane("sl0", "c0", T.t0, t0, tq)))
-    if OPT["r2"] == 0:
-        send(at(2), T.tab[:, 16 * up:16 * up + 16], T.tab[:, 16 * up:16 * up + 16], "rm2", rm1, ts)
-
-    h0a = [arrived("h0c", at(1)), arrived("h0s", at(1))]
-    if OPT["cq"] == 0:
-        need("y", w1, *h0a)
-        copy("c2", cp, "c1", p1, PAIR, "cp2")
-        w2 = [("cp2", 32)]
-    if OPT["cq"] == 2:
-        need("y", w1, *h0a)
-        copy("c2", cp + COLS * (1 - hi), "c1", p1 + COLS * (1 - hi), H0, "cp2")
-        w2 = [("cp2", 32)]
-
-    def keys(b, init, *deps):
-        return v(V.tensor_tensor_scan, T.kk[:, VB * b:VB * b + VW + 1], T.gg[:, VB * b:VB * b + VW + 1],
-                 T.bz[:, (VW + 1) * b:(VW + 1) * (b + 1)], init, A.add, A.subtract, after=deps)
-
-    x1 = 8 * ((q ^ 1) & 3)
-    g1 = v(V.tensor_copy, row(T.gg, vs, COLS), lut1.indirect(T.tab[:, x1:x1 + 8]), after=[rm1, tl1])
-    b1 = s(row(T.bz, vs + 1, COLS), lutm.indirect(T.tab[:, x1:x1 + 8]), F.Copy, after=[rm1, tbz], accum_out=None if last else T.nh[:, 0:1])
-    kp = keys(0, 0.0, g1, b1, go, tgz)
-    key_p, key_x = T.kk[:, 0:VW], T.kk[:, VB:VB + VW]
-
-    def flags_x():
-        return s(row(T.gg, VB, VW), lut2.indirect(T.tab[:, 16 * (1 - up):16 * (1 - up) + 16]), F.Copy, after=[rm2, tl2])
-
-    def marks_x():
-        return s(T.bz[:, VW + 2:2 * VW + 2], T.gg[:, VB:VB + VW], F.Relu, after=[gx], scale=2.0, bias=-BIG, accum_out=T.nh[:, 1:2])
-
-    pv = OPT["pv"]
-    mine = [(i, 48 - 16 * i) if up else (5 - i, 80 - 16 * i) for i in range(pv)]
-    theirs = [i for i in range(6) if i not in [m[0] for m in mine]]
-    if OPT["gx"] == -1:
-        gx = flags_x()
-    for i in theirs:
-        ps_ = count_s(T.w1[:, PC + i:PC + i + 1], key_p, T.kp[:, i:i + 1], kp, tk)
-    if OPT["gx"] == 0:
-        gx = flags_x()
-    b2 = marks_x()
-    jv = lambda i, n: T.jv[:, VW * (1 + i) + n:VW * (2 + i)]
-    ca = [compare_v(jv(j, n), T.kk[:, n:VW], T.kp[:, i:i + 1], kp, tk) for j, (i, n) in enumerate(mine)]
-    pa = [total_v(T.w1[:, i + 8 * n:8 * VW:8], jv(j, n), float(n), ca[j]) for j, (i, n) in enumerate(mine)]
-    for r in Q:
-        t1 = v(V.tensor_scalar, T.t1[r, :], T.w1[Q[0], PC:PC + 6], half, to(VW / 2 - H0 * last, PAIR), A.mult, A.add, after=[ps_, *pa])
-    if OPT.get("kx", 0) == 0:
-        kx = keys(1, end_p(ALL), b2, kp)
-
-    R = Q[2]
-    pk = pick_codes("sl1", "c1", T.t1, t1, w1, *h0a)
-    pl = pick_plane("sl1", "c1", T.t1, t1, w1, *h0a)
-    if OPT.get("kx", 0) == 1:
-        kx = keys(1, end_p(ALL), b2, kp)
-    ship(at(2), "c2", (PAIR if up else COLS), "sl1", H1, "h1", (pk, pl))
-    if last:
-        b = s(T.nb[:, :], T.nh[:, 1:2], F.Copy, after=[b2], scale=2 / BIG, bias=-2.0 * (VW - H1))
+    for i in range(nv):
+        op("a%d" % i, "v", "k0 kz cs", compare(T.jv[:, COLS * i:COLS * i + COLS], T.k0[:, 0:COLS], T.kz[:, i:i + 1]))
+        op("b%d" % i, "v", "a%d" % i, total(T.w0[:, i:8 * COLS:8], T.jv[:, COLS * i:COLS * i + COLS], 0.0))
+    for i in range(nv, 6):
+        op("c%d" % i, "s", "k0 kz cs", count(T.w0[:, OC + i:OC + i + 1], T.k0[:, 0:COLS], T.kz[:, i:i + 1]))
+    op("t0", "v", "b0 b1 b2 c0 c1 c2 c3", *[ts(T.t0[r, :], T.w0[LOW, OC:OC + 4], 0.5, COLS / 2, A.mult, A.add) for r in (LOW, UP)])
+    step(0, ["t0 q0"] * 2, "c0", T.t0, H0, "c1", COLS * hi)
+    own = " ".join(("b%d" if i < nv else "c%d") % i for i in range(6))
+    op("sl1", "p", " ".join(own.split()[2 * hi:2 * hi + 4]), lambda: send(at(1), T.lt[:, 4 * hi:4 * hi + 4], T.w0[:, OC + 2 * hi:OC + 2 * hi + 4], "l1"))
+    op("u1", "v", "L1 cs " + own, lambda: V.tensor_tensor(T.u1[QO, :], T.w0[QO, OC:OC + 6], T.lt[QO, 2 - 2 * hi:8 - 2 * hi], A.add))
+    op("t1", "v", "u1", *[ts(T.t1[r, :], T.u1[QO, :], 0.5, COLS - H0 * hi, A.mult, A.add) for r in Q])
+    step(1, ["t1 q1 cv H0c", "t1 q1 cv H0s"], "c1", T.t1, H1, "c2", PAIR if up else COLS)
+    if OPT["cq"]:
+        pick(("sc", "ss"), ["cv H0c q1", "cv H0s q1"], "c2", cp + COLS * (1 - hi), H0, "c1", T.ti)
     else:
-        b = s(T.nh[:, 2:3], T.nh[:, 1:2], F.Identity, after=[b2, b1], bias=T.nh[:, 0:1])
-    number = lambda out, r: s(out, end_x(r), F.Copy, after=[tno, kx])
-    send(at(4), T.nfa[:, :], T.nfo[:, :], "nf", number(T.nfo[R, :], Q[1]))
-    if not last:
-        b = s(T.nb[:, :], T.nh[:, 2:3], F.Copy, after=[b], scale=2 / BIG, bias=-2.0 * (VW - H1 + COLS - H0))
+        del ops["q2"]
+        op("sc2", "y", "q1 H0c H0s", lambda: Y.dma_start(codes(T.c2c, cp, cp + PAIR), codes(T.c1c, 0, PAIR)).then_inc(T.sem.cp2, 16),
+           lambda: Y.dma_start(T.c2s[:, cp:cp + PAIR], T.c1s[:, :]).then_inc(T.sem.cp2, 16))
+        tok["q2"] = ("cp2", 32)
+
+    x1, x2 = T.tab[:, 8 * ((q ^ 1) & 3):8 * ((q ^ 1) & 3) + 8], T.tab[:, 16 * (1 - up):16 * (1 - up) + 16]
+    keys = lambda b, init: (lambda: V.tensor_tensor_scan(T.kk[:, VB * b:VB * b + VW + 1], T.gg[:, VB * b:VB * b + VW + 1],
+                                                         T.bz[:, (VW + 1) * b:(VW + 1) * (b + 1)], init, A.add, A.subtract))
+    op("go", "s", "cast0 cs cp", act(row(T.gg, vo, COLS), lut1.indirect(same), F.Copy))
+    op("mark", "s", "go", lambda: fill(T.lut[:, 0:1], ALL, s1))
+    op("g1", "v", "Rm1 mark", cp_(row(T.gg, vs, COLS), lut1.indirect(x1)))
+    op("m1", "s", "Rm1 cs cv", act(row(T.bz, vs + 1, COLS), lutm.indirect(x1), F.Copy, accum_out=None if last else T.nh[:, 0:1]))
+    op("kp", "v", "g1 m1 go", keys(0, -BIG))
+    if OPT["m2"] == "s":
+        op("gx", "s", "Rm2 cs", act(row(T.gg, VB, VW), lut2.indirect(x2), F.Copy))
+        op("m2", "s", "gx", act(T.bz[:, VW + 2:2 * VW + 2], T.gg[:, VB:VB + VW], F.Relu, scale=2.0, bias=-BIG, accum_out=T.nh[:, 1:2]))
+        op("nb", "s", "m2", act(T.nb[:, 1:2], T.nh[:, 1:2], F.Copy, scale=2 / BIG, bias=-2.0 * (VW - H1)))
+    else:
+        op("gx", "s", "Rm2 cs", act(row(T.gg, VB, VW), lut2.indirect(x2), F.Copy, accum_out=T.nh[:, 1:2]))
+        op("m2", "v", "gx", ts(T.bz[:, VW + 2:2 * VW + 2], T.gg[:, VB:VB + VW], 2.0, BIG, A.is_gt, A.mult))
+        op("nh", "s", "gx", act(T.nh[:, 2:3], T.nh[:, 1:2], F.Copy, bias=ROUND))
+        op("nb", "s", "nh", act(T.nb[:, 1:2], T.nh[:, 2:3], F.Copy, scale=2 / BIG, bias=-2.0 * (ROUND / BIG + VW - H1)))
+    op("kx", "v", "m2 gx kp", keys(1, end_p(ALL)))
+    pv = OPT["pv"]
+    mine = [(i, 48 - 16 * i) if up else (3 - i, 48 - 16 * i) for i in range(pv)]
+    jv = lambda i, n: T.jv[:, VW * (2 + i) + n:VW * (3 + i)]
+    for j, (i, n) in enumerate(mine):
+        op("pa%d" % j, "v", "kp cs", compare(jv(j, n), T.kk[:, n:VW], T.kp[:, i:i + 1]))
+        op("pb%d" % j, "v", "pa%d" % j, total(T.w1[:, i + 8 * n:8 * VW:8], jv(j, n), float(n)))
+    for j, i in enumerate([i for i in range(4) if i not in [m[0] for m in mine]]):
+        op("p%d" % j, "s", "kp cs", count(T.w1[:, PC + i:PC + i + 1], T.kk[:, 0:VW], T.kp[:, i:i + 1]))
+    P = "pb0 pb1 pb2 p0 p1 p2 p3"
+
+    R = UP
+    op("nf", "s", "kx cs", act(T.nfo[R, :], end_x(LOW), F.Copy, bias=BIG))
+    op("snf", "p", "nf", lambda: send(at(4), T.nfa[:, :], T.nfo[:, :], "nf"))
+    op("an", "s", "kx", act(T.an[R, 0:1], end_x(R), F.Copy, bias=BIG))
     xv = OPT["xv"]
     for i in range(xv, 4):
-        x3 = count_s(T.cs[:, 4 + i:5 + i], key_x, T.kp[:, i:i + 1], kx)
+        op("x%d" % i, "s", "kx cs", count(T.cs[:, 4 + i:5 + i], T.kk[:, VB:VB + VW], T.kp[:, i:i + 1]))
+    pc = T.w1[:, PC:PC + 4]
+    if not last:
+        op("nb1", "s", "m1", act(T.nb[:, 0:1], T.nh[:, 0:1], F.Copy, scale=2 / BIG, bias=-2.0 * (COLS - H0)))
+        op("ad1", "v", "nb1 kp cs", ts(T.ad[:, 4:8], T.kp[:, 0:4], end_p(ALL), T.nb[:, 0:1], A.is_gt, A.mult))
+        op("pp", "v", "ad1 " + P, lambda pc=pc: V.tensor_tensor(T.ad[:, 8:12], T.ad[:, 4:8], pc, A.add))
+        pc = T.ad[:, 8:12]
+    op("ca", "s", "kx", act(T.nb[:, 2:3], T.bz[:, VW + 1 + COLS:VW + 2 + COLS], F.Identity, scale=-1.0, bias=T.kk[:, VB + COLS - 1:VB + COLS]))
+    op("ad", "v", "nb ca cs", ts(T.ad[:, 0:4], T.kp[:, 0:4], T.nb[:, 2:3], T.nb[:, 1:2], A.is_gt, A.mult))
+    op("pa", "v", "ad pp " + P, lambda: V.tensor_tensor(T.pa[:, :], T.ad[:, 0:4], pc, A.add))
     if xv:
-        a = compare_v(jv(0, 0), key_x, T.kp[:, 0:1], kx, *pa)
-    b = v(V.tensor_scalar, T.ad[:, :], T.kp[:, 0:4], end_p(ALL), T.nb[:, :], A.is_gt, A.mult, after=[b])
-    if OPT["cq"]:
-        w2q = quantize("c2", cp + H0 * hi, 0, COLS)
-    if OPT["cq"] == 1:
-        a_ = cp + COLS * (1 - hi)
-        w2 = [v(V.tensor_copy, T.c2c[:, a_:a_ + H0].bitcast(U32), T.c1c[:, :].bitcast(U32).indirect(T.ti[:, :]), after=[tti]),
-              s(T.c2s[:, a_:a_ + H0], T.c1s[:, :].indirect(T.ti[:, :]), F.Copy, after=[tti])]
-    if OPT["cq"]:
-        w2 = w2 + [w2q]
-    tpa = v(V.tensor_tensor, T.pa[:, :], T.ad[:, :], T.w1[:, PC:PC + 4], A.add, after=[b])
-    if xv:
-        x0 = total_v(T.w2[:, 0:VW], jv(0, 0), T.pa[:, 0:1], a, tpa, tw2)
+        op("xa", "v", "kx cs", compare(jv(3, 0), T.kk[:, VB:VB + VW], T.kp[:, 0:1]))
+        op("xb", "v", "xa pa cs", total(T.w2[:, 0:VW], jv(3, 0), T.pa[:, 0:1]))
+    op("x", "v", "x0 x1 x2 x3 pa cs", lambda: V.tensor_tensor(T.w2[:, XC + 4 * xv:XC + 16:4], T.cs[:, 4 + xv:8], T.pa[:, xv:4], A.add))
+    c0 = float(to(VW - H0 * last, NEAR))
+    if OPT["t2"] == "v":
+        op("t2a", "v", "x xb", *[ts(T.t2[r, 4 * i:4 * i + 4], T.w2[Q[i], XC:XC + 16:4], half, c0, A.mult, A.add) for r in Q[0:2] for i in range(2)])
+        op("t2", "v", "t2a", cp_(T.t2[UP, :], T.t2[LOW, :]))
+    else:
+        op("t2a", "s", "x xb", *[act(T.tr[r, 4 * i:4 * i + 4], T.w2[Q[i], XC:XC + 16:4], F.Copy, scale=half, bias=c0) for r in Q[0:2] for i in range(2)])
+        op("t2", "v", "t2a", *[cp_(T.t2[r, :], T.tr[LOW, :]) for r in (LOW, UP)])
+    step(2, ["t2 q2 sc cv H1c", "t2 q2 ss cv H1s"], "c2", T.t2, H2, "a2", 0)
+    op("turn1", "v", "x xb cs", lambda: V.transpose(T.ta[:, 0:32], T.w2[:, XC:XC + 32]),
+       lambda: V.transpose(T.ta[:, 48:80], T.w2[:, XC - 16:XC + 16]))
+    op("turn2", "v", "turn1 cs cv", ts(T.tb[:, :], T.ta[:, :].indirect(T.cu[:, :]), half, c0, A.mult, A.add))
+    op("turn3", "v", "turn2", lambda: V.transpose(T.tc[:, :], T.tb[:, :]))
+    op("tq", "s", "turn3", *[act(T.tq[r, 8 * i:8 * i + 8], T.tc[Q[2 + i], 0:32:4], F.Copy) for r in Q[0:2] for i in range(2)])
+    op("tn", "v", "tq", *[cp_(T.tn[r, :], T.tq[LOW, :]) for r in (LOW, UP)])
+    pick(("pkn", "pln"), ["tn q2 sc cv H1c", "tn q2 ss cv H1s"], "cn", 0, S, "c2", T.tn)
 
-    tan = number(T.an[R, 0:1], R)
-    nf = arrived("nf", at(4))
+    def product(name, deps, o, bank, c, n):
+        op(name, "t", deps, lambda: TE.matmul_mx(T.ps[:, 512 * bank:512 * bank + n], T.wqc[:, 128 * o:128 * o + 128],
+                                                 T.wqs[:, 128 * o:128 * o + 128], T[c + "c"][:, 0:n], T[c + "s"][:, 0:n], True, True))
+    for o in range(2):
+        product("mn%d" % o, "pkn pln qw%d" % o, o, o, "cn", S)
+        product("mf%d" % o, "H2c H2s qw%d" % o, o, 2 + o, "a2", H2)
+    op("n0", "v", "mn0", cp_(T.gr[:, gn:gn + S], T.ps[:, 0:S]))
+    op("n1", "s", "mn1", act(T.gr[:, GW + gn:GW + gn + S], T.ps[:, 512:512 + S], F.Copy))
+    op("f0", "v", "mf0", cp_(T.gr[:, gf:gf + H2], T.ps[:, 1024:1024 + H2]))
+    op("f1", "s", "mf1", act(T.gr[:, GW + gf:GW + gf + H2], T.ps[:, 1536:1536 + H2], F.Copy))
+
     near, away = T.an[R, 0:1], T.nfa[R, :]
     first, second, n1, n2 = (away, near, H2, S) if far else (near, away, S, H2)
-    tln = s(junk(COLS, R), T.gg[R, vo:vo + COLS], F.Copy, accum_out=T.lnb[R, 1:2])
-
-    def spread_last():
-        if up:
-            a = s(T.an[R, 3:4], second, F.Copy, after=[tan, nf], scale=-0.5, bias=n1 + n2 / 2 - 0.5)
-            s(T.an[R, 1:2], second, F.Copy, scale=0.5, bias=-n2 / 2)
+    e0, e1 = ("Nf", "an") if far else ("an", "Nf")
+    if up:
+        op("l0", "s", e0, act(T.an[R, 2:3], first, F.Copy, scale=-1.0, bias=n1 - 0.5))
+        op("l1", "s", e1, act(T.an[R, 1:2], second, F.Copy, scale=-1.0, bias=float(n2)))
+    else:
+        op("l1", "s", e0, act(T.an[R, 1:2], first, F.Copy, scale=-1.0, bias=float(n1)))
+    op("l2", "v", "l1 cs " + e0, ts(T.la[R, 0:16], T.ki[R, 6:22], first, T.an[R, 1:2], A.is_gt, A.mult))
+    op("la", "v", "l2", lambda: V.tensor_tensor(T.la[R, 16:32], T.la[R, 0:16], T.ki[R, 6:22], A.add))
+    op("tf", "v", "la l0", *[ts(T.tf[r, :], T.la[R, 16:32], T.an[R, 2:3] if up else -0.5, float(ZERO), A.add, A.min) for r in (LOW, UP)])
+    store = lambda e, o, i, sem: (lambda: e.dma_start(o, i).then_inc(T.sem[sem], 16) and None)
+    ns = OPT["ns"]
+    for i in range(ns):
+        a, b = S * i // ns, S * (i + 1) // ns
+        op("y0%d" % i, "v", "tf n0 f0 cs", cp_(T.y0[:, a:b], T.gr[:, 0:ZERO + 1].indirect(T.tf[:, a // 16:b // 16])))
+        op("y1%d" % i, "s", "tf n1 f1 cs", act(T.y1[:, a:b], T.gr[:, GW:GW + ZERO + 1].indirect(T.tf[:, a // 16:b // 16]), F.Copy))
+        op("sy0%d" % i, "y", "y0%d" % i, store(Y, T.y[:, a:b], T.y0[:, a:b], "sya"))
+        if i == ns - 1:
+            op("sy1%d" % i, "s", "y1%d" % i, store(SC, T.y[:, S + a:S + b], T.y1[:, a:b], "syb"))
         else:
-            s(T.an[R, 1:2], first, F.Copy, after=[tan, nf], scale=0.5, bias=-n1 / 2)
-            s(T.an[R, 2:3], first, F.Copy, scale=-0.5, bias=n1 / 2 - 0.5)
-        b = s(T.la[R, 0:16], T.ki[R, 4:20], F.Sign, scale=-1.0, bias=first)
-        if up:
-            b = s(T.an[R, 2:3], first, F.Identity, after=[a], scale=-1.0, bias=T.an[R, 3:4])
-        tA = s(T.lnb[R, 0:1], near, F.Identity, bias=away)
-        for r in Q:
-            a_ = s(T.la[r, 16:32], T.la[R, 0:16], F.Identity, after=[b], scale=T.an[R, 1:2], bias=T.an[R, 2:3])
-        return a_, tA
-    if OPT["sl"] == 0:
-        tla, tA = spread_last()
+            op("sy1%d" % i, "y", "y1%d" % i, store(Y, T.y[:, S + a:S + b], T.y1[:, a:b], "sya"))
+    op("sw", "y", OPT["sw"], store(Y, T.wt[:, :], T.w[:, :], "lw"))
+    op("all", "s", "an Nf", act(T.lnb[R, 0:1], near, F.Identity, bias=away))
+    op("own", "s", "go", act(junk(COLS, R), T.gg[R, vo:vo + COLS], F.Copy, accum_out=T.lnb[R, 1:2]))
+    op("sln", "y", "all own", store(Y, T.ln[:, :], T.lnb[64:65, :], "sln"))
 
-    a = v(V.tensor_tensor, T.w2[:, XC + 4 * xv:XC + 16:4], T.cs[:, 4 + xv:8], T.pa[:, xv:4], A.add, after=[x3, tw2, tpa])
-    v(V.transpose, T.ta[:, 0:32], T.w2[:, XC:XC + 32], after=[a])
-    a = v(V.transpose, T.ta[:, 48:80], T.w2[:, XC - 16:XC + 16])
-    a = v(V.tensor_scalar, T.tb[:, :], T.ta[:, :].indirect(T.cu[:, :]), half, to(VW - H0 * last, NEAR), A.mult, A.add, after=[a, tcu])
-    tt = v(V.transpose, T.tc[:, :], T.tb[:, :], after=[a])
-    for r in Q:
-        t2 = v(V.tensor_copy, T.t2[r, :], T.tc[Q[1], 0:32:4], after=[tt])
-    for r in Q[0:2]:
-        for i in range(2):
-            a = s(T.tq[r, 8 * i:8 * i + 8], T.tc[Q[2 + i], 0:32:4], F.Copy, after=[tt])
-    a = s(T.tq[UP, :], T.tq[LOW, :], F.Copy, after=[a])
-    h1a = [arrived("h1c", at(2)), arrived("h1s", at(2))]
-    ship(at(4), "a2", 0, "sl2", H2, "h2", (pick_codes("sl2", "c2", T.t2, t2, *w2, *h1a), pick_plane("sl2", "c2", T.t2, t2, *w2, *h1a)))
-    tqw = v(V.quantize_mx, T.wqc[:, :], T.wqs[:, :], T.wt[:, :], after=[("lw", 16)])
-
-    if OPT["sl"] == 1:
-        tla, tA = spread_last()
-    tn = v(V.tensor_copy, T.tn[:, :], T.tq[:, :], after=[a])
-    pn = (pick_codes("cn", "c2", T.tn, tn), pick_plane("cn", "c2", T.tn, tn))
-
-    def product(o, bank, c, n, *deps):
-        need("t", tqw, *deps)
-        return mark("t", TE.matmul_mx(T.ps[:, 512 * bank:512 * bank + n], T.wqc[:, 128 * o:128 * o + 128], T.wqs[:, 128 * o:128 * o + 128],
-                                      T[c + "c"][:, 0:n], T[c + "s"][:, 0:n], True, True))
-    m0 = product(0, 0, "cn", S, *pn)
-    m1 = product(1, 1, "cn", S)
-
-    if OPT["sl"] == 2:
-        tla, tA = spread_last()
-    a = v(V.tensor_tensor, T.la[:, 32:48], T.la[:, 16:32], T.ki[:, 4:20], A.add, after=[tla])
-    ttf = v(V.tensor_scalar, T.tf[:, :], T.la[:, 32:48], float(ZERO), None, A.min, after=[a])
-    need("y", tA, tln)
-    Y.dma_start(T.ln[:, :], T.lnb[64:65, :]).then_inc(T.sem.sln, 16)
-    g0a = v(V.tensor_copy, T.gr[:, gn:gn + S], T.ps[:, 0:S], after=[m0])
-    g1a = s(T.gr[:, GW + gn:GW + gn + S], T.ps[:, 512:512 + S], F.Copy, after=[m1])
-
-    h2a = [arrived("h2c", at(4)), arrived("h2s", at(4))]
-    m2 = product(0, 2, "a2", H2, *h2a)
-    m3 = product(1, 3, "a2", H2)
-    f0 = v(V.tensor_copy, T.gr[:, gf:gf + H2], T.ps[:, 1024:1024 + H2], after=[m2])
-    f1 = s(T.gr[:, GW + gf:GW + gf + H2], T.ps[:, 1536:1536 + H2], F.Copy, after=[m3])
-    y0 = v(V.tensor_copy, T.y0[:, :], T.gr[:, 0:ZERO + 1].indirect(T.tf[:, :]), after=[f0, g0a, tz, ttf])
-    y1 = s(T.y1[:, :], T.gr[:, GW:GW + ZERO + 1].indirect(T.tf[:, :]), F.Copy, after=[f1, g1a, tz, ttf])
-    need("y", y0)
-    Y.dma_start(T.y[:, 0:S], T.y0[:, :]).then_inc(T.sem.sya, 16)
-    need("s", y1)
-    SC.dma_start(T.y[:, S:2 * S], T.y1[:, :]).then_inc(T.sem.syb, 16)
+    todo = {e: [n for n in ORDER[e].split() if n in ops and ops[n][0] == e] for e in ORDER}
+    assert sum(len(l) for l in todo.values()) == len(ops)
+    while any(todo.values()):
+        e = [e for e in todo if todo[e] and all(d in tok or d not in ops for d in ops[todo[e][0]][1])][0]
+        n = todo[e].pop(0)
+        need(e, *[tok[d] for d in ops[n][1] if d in tok])
+        for call in ops[n][2]:
+            ins = call()
+            tok[n] = mark(e, ins) if e in "vst" and n[0:2] != "sy" else None
 
     need("p", ("loc", sent[0]), ("qv", done["v"]), ("qs", done["s"]), ("qt", done["t"]), ("qp", done["p"]))
-    need("y", ("sln", 16), ("sya", 16))
+    need("y", ("sln", 16), ("sya", 16 * (2 * ns - 1)))
     need("s", ("syb", 16))

@@ -17,21 +17,22 @@ PC = 8 * (VW - 1)
 XC = VW - 1
 
 ORDER = {
-    "v": "and1 and0 cast1 castz cast0 castq q0 q1 k0 q2 a0 a1 b0 b1 t0 pk0 g1 kp pa0 m2 pb0 kx u1 ad1 t1 pp pk1 xa ad sc pa xb x "
-         "qw0 turn1 qw1 turn2 turn3 t2 pk2 tn pkn l2 la tf n0 f0 y00",
-    "s": "m0 km f kz go c0 c1 c2 c3 c4 c5 mark pl0 m1 gx nb1 p0 nh p1 nb p2 p3 ca nf x0 x1 pl1 x2 x3 ss an t2a own tq pl2 pln l0 l1 all n1 f1 y10 sy10",
-    "p": "rm1 rm2 sl1 h0c h0s snf h1c h1s h2c h2s",
+    "v": "and1 and0 cast1 castz cast0 castq go zx cu k0 q0 a0 q1 b0 t0 q2 pk0 g1 ti kp pa0 u1 m2 t1 kx pk1 pb0 ad1 xa pp ad sc pa "
+         "qw0 xb x turn1 qw1 turn2 t2 turn3 pk2 tn pkn l3 l2 lb la n0 tf f0 y00",
+    "s": "m0 lc f km kz mark c1 c2 c3 c4 c5 pl0 m1 gx p0 nh p1 nb1 nb p2 ca pl1 nf x1 x2 x3 ss an zt t2a own zr tq pl2 all l1 pln l0 "
+         "n1 f1 y10 sy10",
+    "p": "rm1 rm2 zg zl zm sl1 h0c h0s zn zw h1c h1s snf h2c h2s",
     "t": "mn0 mn1 mf0 mf1",
     "y": "sw sc2 sln sy00",
 }
 OC = 8 * (COLS - 1)
-OPT = {"j0v": 2, "pv": 1, "xv": 1, "m2": "v", "ns": 1, "sw": "", "nl": 8, "e1": 1, "cq": 1, "t2": "s"}
+OPT = {"j0v": 1, "pv": 1, "xv": 1, "m2": "v", "ns": 1, "sw": "", "nl": 8, "e1": 1, "cq": 1, "t2": "s", "go": "v"}
 CODE, PLANE = "float8_e4m3fn_x4", "uint8"
 SCRATCH = {
-    "dmi": ("sbuf", [128, 8], "int32"), "xt": ("sbuf", [128, 1024], "bfloat16"), "wt": ("sbuf", [128, 1024], "bfloat16"),
+    "dmi": ("sbuf", [128, 8], "int32"), "xt": ("sbuf", [128, 520], "bfloat16"), "wt": ("sbuf", [128, 1024], "bfloat16"),
     "c0c": ("sbuf", [128, COLS + 2], CODE), "c0s": ("sbuf", [128, COLS + 2], PLANE),
     "c1c": ("sbuf", [128, PAIR], CODE), "c1s": ("sbuf", [128, PAIR], PLANE),
-    "c2c": ("sbuf", [128, NEAR + COLS], CODE), "c2s": ("sbuf", [128, NEAR + COLS], PLANE),
+    "c2c": ("sbuf", [128, NEAR], CODE), "c2s": ("sbuf", [128, NEAR], PLANE),
     "cnc": ("sbuf", [128, S], CODE), "cns": ("sbuf", [128, S], PLANE),
     "a2c": ("sbuf", [128, H2], CODE), "a2s": ("sbuf", [128, H2], PLANE),
     "wqc": ("sbuf", [128, 256], CODE), "wqs": ("sbuf", [128, 256], PLANE),
@@ -40,8 +41,8 @@ SCRATCH = {
     "sl2c": ("sbuf", [128, H2], CODE), "sl2s": ("sbuf", [128, H2], PLANE),
     "xi": ("sbuf", [128, 16], "int32"), "tx": ("sbuf", [128, 8], "uint16"), "tab": ("sbuf", [128, 32], "uint16"),
     "nfo": ("sbuf", [128, 1], "float32"), "nfa": ("sbuf", [128, 1], "float32"),
-    "lut": ("sbuf", [128, 544], "bfloat16"), "zi": ("sbuf", [128, 2], "int32"), "za": ("sbuf", [128, 2], "int32"),
-    "zh": ("sbuf", [128, 2], "int32"), "ra": ("sbuf", [128, 1], "float32"), "c64": ("sbuf", [128, 2], "float32"),
+    "lut": ("sbuf", [128, 928], "bfloat16"), "zi": ("sbuf", [128, 2], "int32"), "za": ("sbuf", [128, 2], "int32"),
+    "zh": ("sbuf", [128, 2], "int32"), "ra": ("sbuf", [128, 4], "float32"),
     "cu": ("sbuf", [128, 2], "uint16"), "b16": ("sbuf", [128, 32], "float32"), "ki": ("sbuf", [128, 22], "float32"),
     "kc": ("sbuf", [128, 4], "float32"), "kp": ("sbuf", [128, 4], "float32"), "ti": ("sbuf", [128, 4], "uint16"),
     "fb": ("sbuf", [128, 2 * COLS + 2], "bfloat16"), "k0": ("sbuf", [128, COLS], "bfloat16"), "n0": ("sbuf", [128, 2], "float32"),
@@ -56,7 +57,7 @@ SCRATCH = {
     "ta": ("sbuf", [128, 80], "float32"), "tb": ("sbuf", [128, 32], "float32"), "tc": ("sbuf", [128, 32], "float32"),
     "t0": ("sbuf", [128, 4], "uint16"), "t1": ("sbuf", [128, 6], "uint16"), "t2": ("sbuf", [128, 8], "uint16"),
     "tq": ("sbuf", [128, 16], "float32"), "tn": ("sbuf", [128, 16], "uint16"), "tf": ("sbuf", [128, 16], "uint16"),
-    "an": ("sbuf", [128, 4], "float32"), "la": ("sbuf", [128, 48], "float32"), "lnb": ("sbuf", [128, 2], "float32"),
+    "an": ("sbuf", [128, 4], "float32"), "la": ("sbuf", [128, 64], "float32"), "lnb": ("sbuf", [128, 2], "float32"),
     "gr": ("sbuf", [128, 2 * GW], "float32"), "y0": ("sbuf", [128, 256], "float32"), "y1": ("sbuf", [128, 256], "float32"),
     "ps": ("psum", [128, 2048], "float32"),
 }
@@ -123,13 +124,13 @@ def rank_program(g, core, T, topo):
     last = hi ^ up
     QO, QP = Q[2 + hi], Q[3 - hi]
     s0 = BIG if hi else -BIG
-    cp = (COLS + H1) * up
+    cp = H1 * up
     vo, vs = COLS * last, COLS * (1 - last)
     gn, gf = H2 * far, S * (1 - far)
     s1 = -BIG if last else BIG
     row = lambda t, a, n: t[:, a + n - 1:a - 1 if a else None:-1] if up else t[:, a:a + n]
-    half, to = (-0.5 if up else 0.5), (lambda c, n: COLS + n - 1 - c if up else c)
-    lut1, lut2, lut0, lutm, lutz = (T.lut[:, a:a + 96] for a in (0, 128, 256, 352, 448))
+    half, to = (-0.5 if up else 0.5), (lambda c, n: n - 1 - c if up else c)
+    lut1, lut2, luto, lut0, lutm, lutz = (T.lut[:, a:a + 96] for a in (544, 672, 800, 256, 352, 448))
     end_p, end_x = (lambda r: T.kk[r, VW:VW + 1]), (lambda r: T.kk[r, VB + VW:VB + VW + 1])
 
     for i in range(OPT["nl"]):
@@ -137,32 +138,28 @@ def rank_program(g, core, T, topo):
     Y.dma_start(T.xt[:, 0:512], T.x[:, :]).then_inc(T.sem.lx, 16)
 
     place = lambda d: d - hi
-    bit = lambda b: [[0, 64 >> b], [1, 4], [0, 1 << b]] if b < 6 else [[0, 2], [1, 2], [0, 64]]
+    bit = lambda b: [[0, 32 >> b], [1, 4], [0, 1 << b]] if b < 6 else [[1, 2], [0, 64]]
     both = lambda e: [slice(0, e + 1, e), slice(16 * e, 17 * e + 1, e)]
     iota = lambda o, pat, base=0: mark("p", g.iota(o, pat, base, 0, allow_small_or_imprecise_dtypes=True))
     tzi = mark("p", g.iota(T.zi[:, :], [[0, 2]], 0, 1))
     tb16 = iota(T.b16[:, :], [[16, 32]], -256)
     need("p", tb16)
-    need("p", iota(T.lut[LOW, 0:256], bit(place(q ^ 4))))
-    tl = iota(T.lut[UP, 0:256], bit(place(q)))
+    need("p", iota(T.lut[LOW, 544:672], bit(place(q ^ 4))))
+    tl = iota(T.lut[UP, 544:672], bit(place(q)))
     b16 = lambda r, a: T.b16[r, (a + 256) // 16:(a + 256) // 16 + 4]
 
     def quantize(to, a, b, n):
         return V.quantize_mx(T[to + "c"][:, a:a + n], T[to + "s"][:, a:a + n], T.xt[:, 4 * b:4 * (b + n)])
 
     tbz = v(V.memset, T.bz[:, 0:VW + 2], 0.0)
+    sg = 1.0 - 2 * up
+    v(V.memset, lut0, 1.0)
+    tl0 = v(V.memset, T.lut[:, 352:544], 0.0)
     za = v(V.tensor_scalar, T.za[:, :], T.zi[:, :], 15, None, A.bitwise_and, after=[tzi])
     zh = v(V.tensor_scalar, T.zh[:, :], T.zi[:, :], 16, None, A.bitwise_and)
-    v(V.memset, lut0, 1.0)
-    tra = v(V.tensor_scalar, T.ra[:, :], T.za[:, 0:1], 0.5, None, A.add, after=[za])
-    tl0 = v(V.memset, T.lut[:, 352:544], 0.0)
-    t64 = v(V.tensor_scalar, T.c64[:, :], T.zh[:, :], 4.0, T.ra[:, :], A.mult, A.add, after=[tra, zh])
-    txz = v(V.memset, T.xt[:, 512:1024], 0.0)
-    v(V.tensor_scalar, T.cu[:, :], T.c64[:, :], -0.5, None, A.add, after=[t64])
-    v(quantize, "c2", NEAR * (1 - up), COLS, COLS, after=[txz])
-    v(V.memset, T.lt[:, 4 * hi + 2 - 2 * hi:4 * hi + 4 - 2 * hi], float(COLS if hi else -COLS))
-    v(V.memset, T.fb[:, COLS:COLS + 1], 0.0)
-    v(V.memset, T.gg[:, VW:2 * VB:VB], 0.0)
+    tra = v(V.tensor_scalar, T.ra[:, 0:1], T.za[:, 0:1], 0.5, None, A.add, after=[za])
+    a = v(V.tensor_scalar, T.ra[:, 1:2], T.za[:, 0:1], 0.5, sg, A.add, A.mult)
+    t64 = v(V.tensor_scalar, T.ra[:, 2:4], T.zh[:, :], 4 * sg, T.ra[:, 1:2], A.mult, A.add, after=[a, zh])
 
     def fill(o, rows, val):
         return SC.activation(o, T.bz[rows, 0:int(o.shape[1])], F.Copy, scale=0.0, bias=val)
@@ -174,22 +171,16 @@ def rank_program(g, core, T, topo):
         return t
 
     need("s", tbz)
-    for o in (T.ta[:, 32:48], T.gr[:, ZERO:2 * GW:GW], T.nfo[:, :], T.w2[:, XC - 16:XC + 32]):
-        mark("s", fill(o, ALL, 0.0))
+    mark("s", fill(T.fb[:, COLS:COLS + 1], ALL, 0.0))
     a = put(UP, 256, both(1 << place(q & 3)), 0.0, tl0)
     put(LOW, 256, [slice(0, 1)], 0.0)
     put(ALL, 352, [slice(0, 1)], s1)
     put(QP, 448, [slice(0, 1)], s0)
-    tki = s(T.ki[:, :], T.b16[:, 10:32], F.Identity, after=[tra, tb16], bias=T.ra[:, :])
     put(QP, 256, [slice(0, 1)], s0, a)
-    kb = T.kc if up else T.kp
-    for i, a, n, c in ((0, 0, H2, T.ra), (1, 64, H2, T.ra), (2, 0, S, T.c64), (3, 128, S, T.c64)):
-        tk = s(kb[Q[i], :], b16(Q[i], a - (n if up else S)), F.Identity, after=[t64], bias=c[Q[i], 0:1])
+    tki = s(T.ki[:, :], T.b16[:, 10:32], F.Identity, after=[tra, tb16], bias=T.ra[:, 0:1])
+    for i, a, n, c in ((0, 0, H2, 1), (1, 64, H2, 1), (2, 0, S, 2), (3, 128, S, 2)):
+        s(T.kp[Q[i], :], b16(Q[i], a + (S - n if up else -S)), F.Identity, after=[t64], scale=sg, bias=T.ra[Q[i], c:c + 1])
     s(T.kz[LOW if hi else UP, :], T.ki[LOW if hi else UP, 6:12], F.Copy, after=[tki])
-    if up:
-        s(T.kp[:, :], T.kc[:, :], F.Copy, after=[tk], scale=-1.0, bias=-BIG)
-    put(ALL, 128, both(1 << place((q ^ 2) & 3)), BIG, tl)
-    v(V.tensor_scalar, T.ti[:, :], T.ki[:, 6:10], COLS * (1 - hi) - 0.5, None, A.add, after=[tki])
 
     arrived = lambda sem, src: (sem, len(topo.engines(src, core)))
     tok = {"cv": ("qv", done["v"]), "cs": ("qs", done["s"]), "cp": tl, "dm": ("ld", 16 * OPT["nl"]), "xl": ("lx", 16), "wl": ("lw", 16),
@@ -224,6 +215,21 @@ def rank_program(g, core, T, topo):
         pick((c, p_), deps, o, 0, n, src, tab_)
         op("h%dc" % b, "p", c, lambda: send(at(1 << b), codes(T[to_ + "c"], a, a + n), codes(T[o + "c"], 0, n), "h%dc" % b))
         op("h%ds" % b, "p", p_, lambda: send(at(1 << b), T[to_ + "s"][:, a:a + n], T[o + "s"][:, 0:n], "h%ds" % b))
+
+    zero = lambda o: act(o, T.lut[:, 353:353 + int(o.shape[1])], F.Copy)
+    op("zt", "s", "cv", zero(T.ta[:, 32:48]))
+    flat = lambda o, c: (lambda: g.iota(o, [[0, int(o.shape[1])]], c, 0, allow_small_or_imprecise_dtypes=True))
+    op("zg", "p", "cp", flat(T.gg[:, VW:2 * VB:VB], 0))
+    op("zl", "p", "cp", flat(T.lt[:, 2 + 2 * hi:4 + 2 * hi], COLS if hi else -COLS))
+    op("zn", "p", "cp", flat(T.nfo[:, :], 0))
+    op("zw", "p", "cp", flat(T.w2[:, XC - 16:XC + 32], 0))
+    op("lc", "s", "cp", act(lut2, lut1, F.Copy))
+    op("zm", "p", "lc", *[flat(T.lut[:, 672 + c.start:672 + c.stop:c.step], int(BIG))
+                          for c in both(1 << place((q ^ 2) & 3))])
+    op("zx", "v", "", lambda: V.memset(T.xt[:, 512:520], 0.0))
+    op("cu", "v", "cv", ts(T.cu[:, :], T.ra[:, 2:4], sg, -0.5, A.mult, A.add))
+    op("zr", "s", "cv", zero(T.gr[:, ZERO:2 * GW:GW]))
+    op("ti", "v", "cs", ts(T.ti[:, :], T.ki[:, 6:10], COLS * (1 - hi) - 0.5, None, A.add))
 
     same, other = T.tab[:, 8 * (q & 3):8 * (q & 3) + 8], T.tx[:, :]
     nl = OPT["nl"]
@@ -262,9 +268,10 @@ def rank_program(g, core, T, topo):
     step(0, ["t0 q0"] * 2, "c0", T.t0, H0, "c1", COLS * hi)
     own = " ".join(("b%d" if i < nv else "c%d") % i for i in range(6))
     op("sl1", "p", " ".join(own.split()[2 * hi:2 * hi + 4]), lambda: send(at(1), T.lt[:, 4 * hi:4 * hi + 4], T.w0[:, OC + 2 * hi:OC + 2 * hi + 4], "l1"))
-    op("u1", "v", "L1 cs " + own, lambda: V.tensor_tensor(T.u1[QO, :], T.w0[QO, OC:OC + 6], T.lt[QO, 2 - 2 * hi:8 - 2 * hi], A.add))
-    op("t1", "v", "u1", *[ts(T.t1[r, :], T.u1[QO, :], 0.5, COLS - H0 * hi, A.mult, A.add) for r in Q])
-    step(1, ["t1 q1 cv H0c", "t1 q1 cv H0s"], "c1", T.t1, H1, "c2", PAIR if up else COLS)
+    op("u1", "v", "L1 cs " + own, *[lambda r=r: V.tensor_tensor(T.u1[r, :], T.w0[QO, OC:OC + 6], T.lt[QO, 2 - 2 * hi:8 - 2 * hi], A.add)
+                                    for r in Q[0:2]])
+    op("t1", "v", "u1", *[ts(T.t1[r, :], T.u1[LOW, :], 0.5, COLS - H0 * hi, A.mult, A.add) for r in (LOW, UP)])
+    step(1, ["t1 q1 cv H0c", "t1 q1 cv H0s"], "c1", T.t1, H1, "c2", PAIR * up)
     if OPT["cq"]:
         pick(("sc", "ss"), ["cv H0c q1", "cv H0s q1"], "c2", cp + COLS * (1 - hi), H0, "c1", T.ti)
     else:
@@ -276,8 +283,11 @@ def rank_program(g, core, T, topo):
     x1, x2 = T.tab[:, 8 * ((q ^ 1) & 3):8 * ((q ^ 1) & 3) + 8], T.tab[:, 16 * (1 - up):16 * (1 - up) + 16]
     keys = lambda b, init: (lambda: V.tensor_tensor_scan(T.kk[:, VB * b:VB * b + VW + 1], T.gg[:, VB * b:VB * b + VW + 1],
                                                          T.bz[:, (VW + 1) * b:(VW + 1) * (b + 1)], init, A.add, A.subtract))
-    op("go", "s", "cast0 cs cp", act(row(T.gg, vo, COLS), lut1.indirect(same), F.Copy))
-    op("mark", "s", "go", lambda: fill(T.lut[:, 0:1], ALL, s1))
+    if OPT["go"] == "s":
+        op("go", "s", "cast0 cp", act(row(T.gg, vo, COLS), lut1.indirect(same), F.Copy))
+    else:
+        op("go", "v", "cast0 cp", cp_(row(T.gg, vo, COLS), lut1.indirect(same)))
+    op("mark", "s", "go", lambda: fill(T.lut[:, 544:545], ALL, s1))
     op("g1", "v", "Rm1 mark", cp_(row(T.gg, vs, COLS), lut1.indirect(x1)))
     op("m1", "s", "Rm1 cs cv", act(row(T.bz, vs + 1, COLS), lutm.indirect(x1), F.Copy, accum_out=None if last else T.nh[:, 0:1]))
     op("kp", "v", "g1 m1 go", keys(0, -BIG))
@@ -327,14 +337,14 @@ def rank_program(g, core, T, topo):
         op("t2", "v", "t2a", cp_(T.t2[UP, :], T.t2[LOW, :]))
     else:
         op("t2a", "s", "x xb", *[act(T.tr[r, 4 * i:4 * i + 4], T.w2[Q[i], XC:XC + 16:4], F.Copy, scale=half, bias=c0) for r in Q[0:2] for i in range(2)])
-        op("t2", "v", "t2a", *[cp_(T.t2[r, :], T.tr[LOW, :]) for r in (LOW, UP)])
+        op("t2", "v", "t2a", *[ts(T.t2[r, :], T.tr[LOW, :], NEAR - 1.0, None, A.min) for r in (LOW, UP)])
     step(2, ["t2 q2 sc cv H1c", "t2 q2 ss cv H1s"], "c2", T.t2, H2, "a2", 0)
     op("turn1", "v", "x xb cs", lambda: V.transpose(T.ta[:, 0:32], T.w2[:, XC:XC + 32]),
        lambda: V.transpose(T.ta[:, 48:80], T.w2[:, XC - 16:XC + 16]))
     op("turn2", "v", "turn1 cs cv", ts(T.tb[:, :], T.ta[:, :].indirect(T.cu[:, :]), half, c0, A.mult, A.add))
     op("turn3", "v", "turn2", lambda: V.transpose(T.tc[:, :], T.tb[:, :]))
     op("tq", "s", "turn3", *[act(T.tq[r, 8 * i:8 * i + 8], T.tc[Q[2 + i], 0:32:4], F.Copy) for r in Q[0:2] for i in range(2)])
-    op("tn", "v", "tq", *[cp_(T.tn[r, :], T.tq[LOW, :]) for r in (LOW, UP)])
+    op("tn", "v", "tq", *[ts(T.tn[r, :], T.tq[LOW, :], NEAR - 1.0, None, A.min) for r in (LOW, UP)])
     pick(("pkn", "pln"), ["tn q2 sc cv H1c", "tn q2 ss cv H1s"], "cn", 0, S, "c2", T.tn)
 
     def product(name, deps, o, bank, c, n):
@@ -357,7 +367,12 @@ def rank_program(g, core, T, topo):
     else:
         op("l1", "s", e0, act(T.an[R, 1:2], first, F.Copy, scale=-1.0, bias=float(n1)))
     op("l2", "v", "l1 cs " + e0, ts(T.la[R, 0:16], T.ki[R, 6:22], first, T.an[R, 1:2], A.is_gt, A.mult))
-    op("la", "v", "l2", lambda: V.tensor_tensor(T.la[R, 16:32], T.la[R, 0:16], T.ki[R, 6:22], A.add))
+    ki = T.ki[R, 6:22]
+    if not up:
+        op("l3", "v", "all cs", ts(T.la[R, 32:48], ki, T.lnb[R, 0:1], 4 * BIG, A.is_gt, A.mult))
+        op("lb", "v", "l3", lambda ki=ki: V.tensor_tensor(T.la[R, 48:64], T.la[R, 32:48], ki, A.add))
+        ki = T.la[R, 48:64]
+    op("la", "v", "l2 lb", lambda: V.tensor_tensor(T.la[R, 16:32], T.la[R, 0:16], ki, A.add))
     op("tf", "v", "la l0", *[ts(T.tf[r, :], T.la[R, 16:32], T.an[R, 2:3] if up else -0.5, float(ZERO), A.add, A.min) for r in (LOW, UP)])
     store = lambda e, o, i, sem: (lambda: e.dma_start(o, i).then_inc(T.sem[sem], 16) and None)
     ns = OPT["ns"]
@@ -375,6 +390,11 @@ def rank_program(g, core, T, topo):
     op("own", "s", "go", act(junk(COLS, R), T.gg[R, vo:vo + COLS], F.Copy, accum_out=T.lnb[R, 1:2]))
     op("sln", "y", "all own", store(Y, T.ln[:, :], T.lnb[64:65, :], "sln"))
 
+    for c, users in (("zg", "kp kx"), ("zl", "u1"), ("zn", "nf"), ("zm", "gx"), ("lc", "mark"), ("zw", "xb x"), ("zt cu", "turn2"), ("zr", "y00 y10"), ("ti", "sc ss"), ("zx", "q0")):
+        for n in users.split():
+            if n in ops:
+                ops[n][1].extend(c.split())
+
     todo = {e: [n for n in ORDER[e].split() if n in ops and ops[n][0] == e] for e in ORDER}
     assert sum(len(l) for l in todo.values()) == len(ops)
     while any(todo.values()):
@@ -383,7 +403,7 @@ def rank_program(g, core, T, topo):
         need(e, *[tok[d] for d in ops[n][1] if d in tok])
         for call in ops[n][2]:
             ins = call()
-            tok[n] = mark(e, ins) if e in "vst" and n[0:2] != "sy" else None
+            tok[n] = mark(e, ins) if (e in "vst" and n[0:2] != "sy") or n[0] == "z" else None
 
     need("p", ("loc", sent[0]), ("qv", done["v"]), ("qs", done["s"]), ("qt", done["t"]), ("qp", done["p"]))
     need("y", ("sln", 16), ("sya", 16 * (2 * ns - 1)))

from concourse.bass import DstId, RemoteDMATransfer
from concourse.mybir import dt, AluOpType, ActivationFunctionType

A = AluOpType
F = ActivationFunctionType
U8, U32 = dt.uint8, dt.uint32
N, COLS, S = 8, 128, 256
H0, H1, H2 = 64, 96, 128
PAIR = COLS + H0
NEAR = PAIR + H1
ZERO = S + H2
GW = ZERO + 8
BIG = 256.0
ROUND = 1.5 * 2 ** 31
VW, VB = 2 * COLS, 264
PC = 8 * (VW - 1)
XC = VW - 1

ORDER = {
    "v": "and1 and0 cast1 castz cast0 castq go zx cu k0 q0 a0 q1 b0 t0 q2 pk0 g1 ti kp pa0 u1 m2 t1 kx pk1 pb0 ad1 xa pp ad sc pa "
         "qw0 xb x turn1 qw1 turn2 t2 turn3 pk2 tn pkn l3 l2 lb la n0 tf f0 y00",
    "s": "m0 lc f km kz mark c1 c2 c3 c4 c5 pl0 m1 gx p0 nh p1 nb1 nb p2 ca pl1 nf x1 x2 x3 ss an zt t2a own zr tq pl2 all l1 pln l0 "
         "n1 f1 y10 sy10",
    "p": "rm1 rm2 zg zl zm sl1 h0c h0s zn zw h1c h1s snf h2c h2s",
    "t": "mn0 mn1 mf0 mf1",
    "y": "sw sc2 sln sy00",
}
OC = 8 * (COLS - 1)
OPT = {"j0v": 1, "pv": 1, "xv": 1, "m2": "v", "ns": 1, "sw": "", "nl": 8, "e1": 1, "cq": 1, "t2": "s", "go": "v"}
CODE, PLANE = "float8_e4m3fn_x4", "uint8"
SCRATCH = {
    "dmi": ("sbuf", [128, 8], "int32"), "xt": ("sbuf", [128, 520], "bfloat16"), "wt": ("sbuf", [128, 1024], "bfloat16"),
    "c0c": ("sbuf", [128, COLS + 2], CODE), "c0s": ("sbuf", [128, COLS + 2], PLANE),
    "c1c": ("sbuf", [128, PAIR], CODE), "c1s": ("sbuf", [128, PAIR], PLANE),
    "c2c": ("sbuf", [128, NEAR], CODE), "c2s": ("sbuf", [128, NEAR], PLANE),
    "cnc": ("sbuf", [128, S], CODE), "cns": ("sbuf", [128, S], PLANE),
    "a2c": ("sbuf", [128, H2], CODE), "a2s": ("sbuf", [128, H2], PLANE),
    "wqc": ("sbuf", [128, 256], CODE), "wqs": ("sbuf", [128, 256], PLANE),
    "sl0c": ("sbuf", [128, H0], CODE), "sl0s": ("sbuf", [128, H0], PLANE),
    "sl1c": ("sbuf", [128, H1], CODE), "sl1s": ("sbuf", [128, H1], PLANE),
    "sl2c": ("sbuf", [128, H2], CODE), "sl2s": ("sbuf", [128, H2], PLANE),
    "xi": ("sbuf", [128, 16], "int32"), "tx": ("sbuf", [128, 8], "uint16"), "tab": ("sbuf", [128, 32], "uint16"),
    "nfo": ("sbuf", [128, 1], "float32"), "nfa": ("sbuf", [128, 1], "float32"),
    "lut": ("sbuf", [128, 928], "bfloat16"), "zi": ("sbuf", [128, 2], "int32"), "za": ("sbuf", [128, 2], "int32"),
    "zh": ("sbuf", [128, 2], "int32"), "ra": ("sbuf", [128, 4], "float32"),
    "cu": ("sbuf", [128, 2], "uint16"), "b16": ("sbuf", [128, 32], "float32"), "ki": ("sbuf", [128, 22], "float32"),
    "kc": ("sbuf", [128, 4], "float32"), "kp": ("sbuf", [128, 4], "float32"), "ti": ("sbuf", [128, 4], "uint16"),
    "fb": ("sbuf", [128, 2 * COLS + 2], "bfloat16"), "k0": ("sbuf", [128, COLS], "bfloat16"), "n0": ("sbuf", [128, 2], "float32"),
    "km": ("sbuf", [128, 6], "float32"), "tr": ("sbuf", [128, 8], "float32"), "gg": ("sbuf", [128, 2 * VB], "bfloat16"),
    "bz": ("sbuf", [128, 2 * VW + 2], "bfloat16"), "kk": ("sbuf", [128, 2 * VB], "bfloat16"),
    "kz": ("sbuf", [128, 6], "float32"), "tz": ("sbuf", [128, 8], "uint16"),
    "lt": ("sbuf", [128, 8], "float32"), "u1": ("sbuf", [128, 6], "float32"),
    "js": ("sbuf", [128, 14 * VW], "bfloat16"), "jv": ("sbuf", [128, 6 * VW], "bfloat16"), "w0": ("sbuf", [128, 8 * COLS], "float32"),
    "cs": ("sbuf", [128, 8], "float32"), "w1": ("sbuf", [128, 8 * VW], "float32"), "w2": ("sbuf", [128, VW + 32], "float32"),
    "nh": ("sbuf", [128, 4], "float32"), "nb": ("sbuf", [128, 3], "bfloat16"), "ad": ("sbuf", [128, 12], "float32"),
    "pa": ("sbuf", [128, 4], "float32"),
    "ta": ("sbuf", [128, 80], "float32"), "tb": ("sbuf", [128, 32], "float32"), "tc": ("sbuf", [128, 32], "float32"),
    "t0": ("sbuf", [128, 4], "uint16"), "t1": ("sbuf", [128, 6], "uint16"), "t2": ("sbuf", [128, 8], "uint16"),
    "tq": ("sbuf", [128, 16], "float32"), "tn": ("sbuf", [128, 16], "uint16"), "tf": ("sbuf", [128, 16], "uint16"),
    "an": ("sbuf", [128, 4], "float32"), "la": ("sbuf", [128, 64], "float32"), "lnb": ("sbuf", [128, 2], "float32"),
    "gr": ("sbuf", [128, 2 * GW], "float32"), "y0": ("sbuf", [128, 256], "float32"), "y1": ("sbuf", [128, 256], "float32"),
    "ps": ("psum", [128, 2048], "float32"),
}
ARR = ["rm1", "rm2", "l1", "nf", "h0c", "h0s", "h1c", "h1s", "h2c", "h2s"]
SEMAPHORES = ["qv", "qs", "qt", "qp", "ld", "lx", "lw", "cp2", "sya", "syb", "sln", "loc"] + ARR


def rank_program(g, core, T, topo):
    q = T.rank_of(core)
    if q is None:
        return
    V, SC, TE, Y = g.vector, g.scalar, g.tensor, g.sync
    queue = {"v": V, "s": SC, "t": TE, "p": g, "y": Y}
    done = {"v": 0, "s": 0, "t": 0, "p": 0}
    seen = {}

    def need(e, *deps):
        best = {}
        for d in deps:
            best[d[0]] = max(best.get(d[0], 0), d[1])
        for s in best:
            if seen.get((e, s), 0) < best[s]:
                queue[e].wait_ge(T.sem[s], best[s])
                seen[(e, s)] = best[s]

    def mark(e, ins):
        ins.then_inc(T.sem["q" + e], 1)
        done[e] += 1
        return ("q" + e, done[e])

    def v(call, *a, after=()):
        need("v", *after)
        return mark("v", call(*a))

    def s(out, in_, func, after=(), **k):
        need("s", *after)
        return mark("s", SC.activation(out, in_, func, **k))

    sent = [0]

    def send(dst, out, in_, sem, share=1):
        rid, pid = topo.addr(dst, core)
        e = topo.engines(core, dst)[::share]
        g.remote_dma(out, in_, T.sem[sem], T.sem["loc"], pid, rid, sum(1 << n for n in e))
        sent[0] += len(e)

    def send2(writes, sem):
        tr = []
        for i, (d, out, in_) in enumerate(writes):
            rid, pid = topo.addr(d, core)
            e = topo.engines(core, d)
            e = e[i * len(e) // 2:(i + 1) * len(e) // 2]
            tr.append(RemoteDMATransfer(dst_ids=[DstId(rid=rid, pnc=pid)], dma_engine_mask=sum(1 << n for n in e),
                                        remote_sem=T.sem[sem], srcs=[in_], dsts=[out]))
            sent[0] += len(e)
        g.remote_dma_fused(tr, local_sem=T.sem["loc"])

    at = lambda x: T.cores[q ^ x]
    codes = lambda t, a, b: t[:, a:b].bitcast(U8)
    Q = [slice(32 * i, 32 * i + 32) for i in range(4)]
    LOW, UP, ALL = slice(0, 64), slice(64, 128), slice(0, 128)

    hi, up, far = q & 1, (q >> 1) & 1, q >> 2
    last = hi ^ up
    QO, QP = Q[2 + hi], Q[3 - hi]
    s0 = BIG if hi else -BIG
    cp = H1 * up
    vo, vs = COLS * last, COLS * (1 - last)
    gn, gf = H2 * far, S * (1 - far)
    s1 = -BIG if last else BIG
    row = lambda t, a, n: t[:, a + n - 1:a - 1 if a else None:-1] if up else t[:, a:a + n]
    half, to = (-0.5 if up else 0.5), (lambda c, n: n - 1 - c if up else c)
    lut1, lut2, luto, lut0, lutm, lutz = (T.lut[:, a:a + 96] for a in (544, 672, 800, 256, 352, 448))
    end_p, end_x = (lambda r: T.kk[r, VW:VW + 1]), (lambda r: T.kk[r, VB + VW:VB + VW + 1])

    for i in range(OPT["nl"]):
        (Y if i % 2 == 0 else SC).dma_start(T.dmi[16 * i:16 * i + 16, :], T.dm[:, :]).then_inc(T.sem.ld, 16)
    Y.dma_start(T.xt[:, 0:512], T.x[:, :]).then_inc(T.sem.lx, 16)

    place = lambda d: d - hi
    bit = lambda b: [[0, 32 >> b], [1, 4], [0, 1 << b]] if b < 6 else [[1, 2], [0, 64]]
    both = lambda e: [slice(0, e + 1, e), slice(16 * e, 17 * e + 1, e)]
    iota = lambda o, pat, base=0: mark("p", g.iota(o, pat, base, 0, allow_small_or_imprecise_dtypes=True))
    tzi = mark("p", g.iota(T.zi[:, :], [[0, 2]], 0, 1))
    tb16 = iota(T.b16[:, :], [[16, 32]], -256)
    need("p", tb16)
    need("p", iota(T.lut[LOW, 544:672], bit(place(q ^ 4))))
    tl = iota(T.lut[UP, 544:672], bit(place(q)))
    b16 = lambda r, a: T.b16[r, (a + 256) // 16:(a + 256) // 16 + 4]

    def quantize(to, a, b, n):
        return V.quantize_mx(T[to + "c"][:, a:a + n], T[to + "s"][:, a:a + n], T.xt[:, 4 * b:4 * (b + n)])

    tbz = v(V.memset, T.bz[:, 0:VW + 2], 0.0)
    sg = 1.0 - 2 * up
    v(V.memset, lut0, 1.0)
    tl0 = v(V.memset, T.lut[:, 352:544], 0.0)
    za = v(V.tensor_scalar, T.za[:, :], T.zi[:, :], 15, None, A.bitwise_and, after=[tzi])
    zh = v(V.tensor_scalar, T.zh[:, :], T.zi[:, :], 16, None, A.bitwise_and)
    tra = v(V.tensor_scalar, T.ra[:, 0:1], T.za[:, 0:1], 0.5, None, A.add, after=[za])
    a = v(V.tensor_scalar, T.ra[:, 1:2], T.za[:, 0:1], 0.5, sg, A.add, A.mult)
    t64 = v(V.tensor_scalar, T.ra[:, 2:4], T.zh[:, :], 4 * sg, T.ra[:, 1:2], A.mult, A.add, after=[a, zh])

    def fill(o, rows, val):
        return SC.activation(o, T.bz[rows, 0:int(o.shape[1])], F.Copy, scale=0.0, bias=val)

    def put(rows, base, cols, val, *deps):
        need("s", *deps)
        for c in cols:
            t = mark("s", fill(T.lut[rows, base + c.start:base + c.stop:c.step or 1], rows, val))
        return t

    need("s", tbz)
    mark("s", fill(T.fb[:, COLS:COLS + 1], ALL, 0.0))
    a = put(UP, 256, both(1 << place(q & 3)), 0.0, tl0)
    put(LOW, 256, [slice(0, 1)], 0.0)
    put(ALL, 352, [slice(0, 1)], s1)
    put(QP, 448, [slice(0, 1)], s0)
    put(QP, 256, [slice(0, 1)], s0, a)
    tki = s(T.ki[:, :], T.b16[:, 10:32], F.Identity, after=[tra, tb16], bias=T.ra[:, 0:1])
    for i, a, n, c in ((0, 0, H2, 1), (1, 64, H2, 1), (2, 0, S, 2), (3, 128, S, 2)):
        s(T.kp[Q[i], :], b16(Q[i], a + (S - n if up else -S)), F.Identity, after=[t64], scale=sg, bias=T.ra[Q[i], c:c + 1])
    s(T.kz[LOW if hi else UP, :], T.ki[LOW if hi else UP, 6:12], F.Copy, after=[tki])

    arrived = lambda sem, src: (sem, len(topo.engines(src, core)))
    tok = {"cv": ("qv", done["v"]), "cs": ("qs", done["s"]), "cp": tl, "dm": ("ld", 16 * OPT["nl"]), "xl": ("lx", 16), "wl": ("lw", 16),
           "Rm1": ("rm1", len(topo.engines(at(1), core)[::OPT["e1"]])), "Rm2": arrived("rm2", at(2)), "Nf": arrived("nf", at(4)),
           "L1": arrived("l1", at(1))}
    for b in range(3):
        tok["H%dc" % b], tok["H%ds" % b] = arrived("h%dc" % b, at(1 << b)), arrived("h%ds" % b, at(1 << b))
    ops = {}

    def op(name, e, deps, *calls):
        ops[name] = (e, deps.split(), calls)

    act = lambda o, i, f, **k: (lambda: SC.activation(o, i, f, **k))
    ts = lambda *a: (lambda: V.tensor_scalar(*a))
    cp_ = lambda o, i: (lambda: V.tensor_copy(o, i))
    js = [0]

    def junk(n, r=ALL):
        js[0] += n
        return T.js[r, js[0] - n:js[0]]

    count = lambda acc, key, k: act(junk(int(key.shape[1])), key, F.Sign, bias=k, scale=-1.0, accum_out=acc)
    compare = lambda o, key, k: ts(o, key, k, 0.5, A.is_le, A.subtract)
    total = lambda out, o, init: (lambda: V.tensor_tensor_scan(out, o, o, init, A.add, A.add))

    def pick(names, deps, out, a, n, src, tab_):
        op(names[0], "v", deps[0], cp_(T[out + "c"][:, a:a + n].bitcast(U32), T[src + "c"][:, :].bitcast(U32).indirect(tab_[:, :])))
        op(names[1], "s", deps[1], act(T[out + "s"][:, a:a + n], T[src + "s"][:, :].indirect(tab_[:, :]), F.Copy))

    def step(b, deps, src, tab_, n, to_, a):
        c, p_, o = "pk%d" % b, "pl%d" % b, "sl%d" % b
        pick((c, p_), deps, o, 0, n, src, tab_)
        op("h%dc" % b, "p", c, lambda: send(at(1 << b), codes(T[to_ + "c"], a, a + n), codes(T[o + "c"], 0, n), "h%dc" % b))
        op("h%ds" % b, "p", p_, lambda: send(at(1 << b), T[to_ + "s"][:, a:a + n], T[o + "s"][:, 0:n], "h%ds" % b))

    zero = lambda o: act(o, T.lut[:, 353:353 + int(o.shape[1])], F.Copy)
    op("zt", "s", "cv", zero(T.ta[:, 32:48]))
    flat = lambda o, c: (lambda: g.iota(o, [[0, int(o.shape[1])]], c, 0, allow_small_or_imprecise_dtypes=True))
    op("zg", "p", "cp", flat(T.gg[:, VW:2 * VB:VB], 0))
    op("zl", "p", "cp", flat(T.lt[:, 2 + 2 * hi:4 + 2 * hi], COLS if hi else -COLS))
    op("zn", "p", "cp", flat(T.nfo[:, :], 0))
    op("zw", "p", "cp", flat(T.w2[:, XC - 16:XC + 32], 0))
    op("lc", "s", "cp", act(lut2, lut1, F.Copy))
    op("zm", "p", "lc", *[flat(T.lut[:, 672 + c.start:672 + c.stop:c.step], int(BIG))
                          for c in both(1 << place((q ^ 2) & 3))])
    op("zx", "v", "", lambda: V.memset(T.xt[:, 512:520], 0.0))
    op("cu", "v", "cv", ts(T.cu[:, :], T.ra[:, 2:4], sg, -0.5, A.mult, A.add))
    op("zr", "s", "cv", zero(T.gr[:, ZERO:2 * GW:GW]))
    op("ti", "v", "cs", ts(T.ti[:, :], T.ki[:, 6:10], COLS * (1 - hi) - 0.5, None, A.add))

    same, other = T.tab[:, 8 * (q & 3):8 * (q & 3) + 8], T.tx[:, :]
    nl = OPT["nl"]
    L = slice(0, 16 * nl)
    parts = [slice(16 * nl * i, 16 * nl * (i + 1)) for i in range(8 // nl)]
    op("and1", "v", "dm", ts(T.xi[L, 8:16], T.dmi[L, :], 1 - hi, 0x55, A.logical_shift_right, A.bitwise_and))
    op("and0", "v", "dm", ts(T.xi[L, 0:8], T.dmi[L, :], hi, 0x55, A.logical_shift_right, A.bitwise_and))
    op("cast1", "v", "and1", *[cp_(T.tx[r, :], T.xi[L, 8:16]) for r in parts])
    op("cast0", "v", "and0", *[cp_(T.tab[r, 8 * (q & 3):8 * (q & 3) + 8], T.xi[L, 0:8]) for r in parts])
    op("rm1", "p", "cast1", lambda: send(at(1), same, other, "rm1", OPT["e1"]))
    op("rm2", "p", "cast0 cast1", lambda: send2([(at(2), same, same), (at(3), same, other)], "rm2"))
    op("q0", "v", "xl cv", lambda: quantize("c0", 0, 0, COLS + 2))
    op("q1", "v", "xl", lambda: quantize("c1", H0 * hi, 0, COLS))
    op("q2", "v", "xl", lambda: quantize("c2", cp + H0 * hi, 0, COLS))
    for i in range(2):
        op("qw%d" % i, "v", "wl", lambda i=i: V.quantize_mx(T.wqc[:, 128 * i:128 * i + 128], T.wqs[:, 128 * i:128 * i + 128],
                                                          T.wt[:, 512 * i:512 * i + 512]))

    op("castz", "v", "and1", cp_(T.tz[:, :], T.xi[:, 8:16]))
    op("castq", "v", "and0 castz", cp_(T.tz[QO, :], T.xi[QO, 0:8]))
    op("f", "s", "castq cv cs", act(T.fb[:, 0:COLS], lut0.indirect(T.tz[:, :]), F.Copy, accum_out=T.n0[:, 0:1]))
    op("m0", "s", "cast1 cv cs", act(T.fb[:, COLS + 1:2 * COLS + 1], lutz.indirect(other), F.Copy, scale=-1.0, accum_out=T.n0[:, 1:2] if hi else None))
    op("k0", "v", "f m0", lambda: V.tensor_tensor_scan(T.k0[:, :], T.fb[:, 0:COLS], T.fb[:, COLS:2 * COLS], 0.0, A.add, A.add))
    if hi:
        op("km", "s", "m0 cs", act(T.km[UP, :], T.ki[UP, 0:6], F.Identity, bias=T.n0[UP, 1:2]))
        op("kz", "s", "f km", act(T.kz[UP, :], T.km[UP, :], F.Identity, bias=T.n0[UP, 0:1]))
    else:
        op("kz", "s", "f cs", act(T.kz[LOW, :], T.ki[LOW, 2:8], F.Identity, bias=T.n0[LOW, 0:1]))
    nv = OPT["j0v"]
    for i in range(nv):
        op("a%d" % i, "v", "k0 kz cs", compare(T.jv[:, COLS * i:COLS * i + COLS], T.k0[:, 0:COLS], T.kz[:, i:i + 1]))
        op("b%d" % i, "v", "a%d" % i, total(T.w0[:, i:8 * COLS:8], T.jv[:, COLS * i:COLS * i + COLS], 0.0))
    for i in range(nv, 6):
        op("c%d" % i, "s", "k0 kz cs", count(T.w0[:, OC + i:OC + i + 1], T.k0[:, 0:COLS], T.kz[:, i:i + 1]))
    op("t0", "v", "b0 b1 b2 c0 c1 c2 c3", *[ts(T.t0[r, :], T.w0[LOW, OC:OC + 4], 0.5, COLS / 2, A.mult, A.add) for r in (LOW, UP)])
    step(0, ["t0 q0"] * 2, "c0", T.t0, H0, "c1", COLS * hi)
    own = " ".join(("b%d" if i < nv else "c%d") % i for i in range(6))
    op("sl1", "p", " ".join(own.split()[2 * hi:2 * hi + 4]), lambda: send(at(1), T.lt[:, 4 * hi:4 * hi + 4], T.w0[:, OC + 2 * hi:OC + 2 * hi + 4], "l1"))
    op("u1", "v", "L1 cs " + own, *[lambda r=r: V.tensor_tensor(T.u1[r, :], T.w0[QO, OC:OC + 6], T.lt[QO, 2 - 2 * hi:8 - 2 * hi], A.add)
                                    for r in Q[0:2]])
    op("t1", "v", "u1", *[ts(T.t1[r, :], T.u1[LOW, :], 0.5, COLS - H0 * hi, A.mult, A.add) for r in (LOW, UP)])
    step(1, ["t1 q1 cv H0c", "t1 q1 cv H0s"], "c1", T.t1, H1, "c2", PAIR * up)
    if OPT["cq"]:
        pick(("sc", "ss"), ["cv H0c q1", "cv H0s q1"], "c2", cp + COLS * (1 - hi), H0, "c1", T.ti)
    else:
        del ops["q2"]
        op("sc2", "y", "q1 H0c H0s", lambda: Y.dma_start(codes(T.c2c, cp, cp + PAIR), codes(T.c1c, 0, PAIR)).then_inc(T.sem.cp2, 16),
           lambda: Y.dma_start(T.c2s[:, cp:cp + PAIR], T.c1s[:, :]).then_inc(T.sem.cp2, 16))
        tok["q2"] = ("cp2", 32)

    x1, x2 = T.tab[:, 8 * ((q ^ 1) & 3):8 * ((q ^ 1) & 3) + 8], T.tab[:, 16 * (1 - up):16 * (1 - up) + 16]
    keys = lambda b, init: (lambda: V.tensor_tensor_scan(T.kk[:, VB * b:VB * b + VW + 1], T.gg[:, VB * b:VB * b + VW + 1],
                                                         T.bz[:, (VW + 1) * b:(VW + 1) * (b + 1)], init, A.add, A.subtract))
    if OPT["go"] == "s":
        op("go", "s", "cast0 cp", act(row(T.gg, vo, COLS), lut1.indirect(same), F.Copy))
    else:
        op("go", "v", "cast0 cp", cp_(row(T.gg, vo, COLS), lut1.indirect(same)))
    op("mark", "s", "go", lambda: fill(T.lut[:, 544:545], ALL, s1))
    op("g1", "v", "Rm1 mark", cp_(row(T.gg, vs, COLS), lut1.indirect(x1)))
    op("m1", "s", "Rm1 cs cv", act(row(T.bz, vs + 1, COLS), lutm.indirect(x1), F.Copy, accum_out=None if last else T.nh[:, 0:1]))
    op("kp", "v", "g1 m1 go", keys(0, -BIG))
    if OPT["m2"] == "s":
        op("gx", "s", "Rm2 cs", act(row(T.gg, VB, VW), lut2.indirect(x2), F.Copy))
        op("m2", "s", "gx", act(T.bz[:, VW + 2:2 * VW + 2], T.gg[:, VB:VB + VW], F.Relu, scale=2.0, bias=-BIG, accum_out=T.nh[:, 1:2]))
        op("nb", "s", "m2", act(T.nb[:, 1:2], T.nh[:, 1:2], F.Copy, scale=2 / BIG, bias=-2.0 * (VW - H1)))
    else:
        op("gx", "s", "Rm2 cs", act(row(T.gg, VB, VW), lut2.indirect(x2), F.Copy, accum_out=T.nh[:, 1:2]))
        op("m2", "v", "gx", ts(T.bz[:, VW + 2:2 * VW + 2], T.gg[:, VB:VB + VW], 2.0, BIG, A.is_gt, A.mult))
        op("nh", "s", "gx", act(T.nh[:, 2:3], T.nh[:, 1:2], F.Copy, bias=ROUND))
        op("nb", "s", "nh", act(T.nb[:, 1:2], T.nh[:, 2:3], F.Copy, scale=2 / BIG, bias=-2.0 * (ROUND / BIG + VW - H1)))
    op("kx", "v", "m2 gx kp", keys(1, end_p(ALL)))
    pv = OPT["pv"]
    mine = [(i, 48 - 16 * i) if up else (3 - i, 48 - 16 * i) for i in range(pv)]
    jv = lambda i, n: T.jv[:, VW * (2 + i) + n:VW * (3 + i)]
    for j, (i, n) in enumerate(mine):
        op("pa%d" % j, "v", "kp cs", compare(jv(j, n), T.kk[:, n:VW], T.kp[:, i:i + 1]))
        op("pb%d" % j, "v", "pa%d" % j, total(T.w1[:, i + 8 * n:8 * VW:8], jv(j, n), float(n)))
    for j, i in enumerate([i for i in range(4) if i not in [m[0] for m in mine]]):
        op("p%d" % j, "s", "kp cs", count(T.w1[:, PC + i:PC + i + 1], T.kk[:, 0:VW], T.kp[:, i:i + 1]))
    P = "pb0 pb1 pb2 p0 p1 p2 p3"

    R = UP
    op("nf", "s", "kx cs", act(T.nfo[R, :], end_x(LOW), F.Copy, bias=BIG))
    op("snf", "p", "nf", lambda: send(at(4), T.nfa[:, :], T.nfo[:, :], "nf"))
    op("an", "s", "kx", act(T.an[R, 0:1], end_x(R), F.Copy, bias=BIG))
    xv = OPT["xv"]
    for i in range(xv, 4):
        op("x%d" % i, "s", "kx cs", count(T.cs[:, 4 + i:5 + i], T.kk[:, VB:VB + VW], T.kp[:, i:i + 1]))
    pc = T.w1[:, PC:PC + 4]
    if not last:
        op("nb1", "s", "m1", act(T.nb[:, 0:1], T.nh[:, 0:1], F.Copy, scale=2 / BIG, bias=-2.0 * (COLS - H0)))
        op("ad1", "v", "nb1 kp cs", ts(T.ad[:, 4:8], T.kp[:, 0:4], end_p(ALL), T.nb[:, 0:1], A.is_gt, A.mult))
        op("pp", "v", "ad1 " + P, lambda pc=pc: V.tensor_tensor(T.ad[:, 8:12], T.ad[:, 4:8], pc, A.add))
        pc = T.ad[:, 8:12]
    op("ca", "s", "kx", act(T.nb[:, 2:3], T.bz[:, VW + 1 + COLS:VW + 2 + COLS], F.Identity, scale=-1.0, bias=T.kk[:, VB + COLS - 1:VB + COLS]))
    op("ad", "v", "nb ca cs", ts(T.ad[:, 0:4], T.kp[:, 0:4], T.nb[:, 2:3], T.nb[:, 1:2], A.is_gt, A.mult))
    op("pa", "v", "ad pp " + P, lambda: V.tensor_tensor(T.pa[:, :], T.ad[:, 0:4], pc, A.add))
    if xv:
        op("xa", "v", "kx cs", compare(jv(3, 0), T.kk[:, VB:VB + VW], T.kp[:, 0:1]))
        op("xb", "v", "xa pa cs", total(T.w2[:, 0:VW], jv(3, 0), T.pa[:, 0:1]))
    op("x", "v", "x0 x1 x2 x3 pa cs", lambda: V.tensor_tensor(T.w2[:, XC + 4 * xv:XC + 16:4], T.cs[:, 4 + xv:8], T.pa[:, xv:4], A.add))
    c0 = float(to(VW - H0 * last, NEAR))
    if OPT["t2"] == "v":
        op("t2a", "v", "x xb", *[ts(T.t2[r, 4 * i:4 * i + 4], T.w2[Q[i], XC:XC + 16:4], half, c0, A.mult, A.add) for r in Q[0:2] for i in range(2)])
        op("t2", "v", "t2a", cp_(T.t2[UP, :], T.t2[LOW, :]))
    else:
        op("t2a", "s", "x xb", *[act(T.tr[r, 4 * i:4 * i + 4], T.w2[Q[i], XC:XC + 16:4], F.Copy, scale=half, bias=c0) for r in Q[0:2] for i in range(2)])
        op("t2", "v", "t2a", *[ts(T.t2[r, :], T.tr[LOW, :], NEAR - 1.0, None, A.min) for r in (LOW, UP)])
    step(2, ["t2 q2 sc cv H1c", "t2 q2 ss cv H1s"], "c2", T.t2, H2, "a2", 0)
    op("turn1", "v", "x xb cs", lambda: V.transpose(T.ta[:, 0:32], T.w2[:, XC:XC + 32]),
       lambda: V.transpose(T.ta[:, 48:80], T.w2[:, XC - 16:XC + 16]))
    op("turn2", "v", "turn1 cs cv", ts(T.tb[:, :], T.ta[:, :].indirect(T.cu[:, :]), half, c0, A.mult, A.add))
    op("turn3", "v", "turn2", lambda: V.transpose(T.tc[:, :], T.tb[:, :]))
    op("tq", "s", "turn3", *[act(T.tq[r, 8 * i:8 * i + 8], T.tc[Q[2 + i], 0:32:4], F.Copy) for r in Q[0:2] for i in range(2)])
    op("tn", "v", "tq", *[ts(T.tn[r, :], T.tq[LOW, :], NEAR - 1.0, None, A.min) for r in (LOW, UP)])
    pick(("pkn", "pln"), ["tn q2 sc cv H1c", "tn q2 ss cv H1s"], "cn", 0, S, "c2", T.tn)

    def product(name, deps, o, bank, c, n):
        op(name, "t", deps, lambda: TE.matmul_mx(T.ps[:, 512 * bank:512 * bank + n], T.wqc[:, 128 * o:128 * o + 128],
                                                 T.wqs[:, 128 * o:128 * o + 128], T[c + "c"][:, 0:n], T[c + "s"][:, 0:n], True, True))
    for o in range(2):
        product("mn%d" % o, "pkn pln qw%d" % o, o, o, "cn", S)
        product("mf%d" % o, "H2c H2s qw%d" % o, o, 2 + o, "a2", H2)
    op("n0", "v", "mn0", cp_(T.gr[:, gn:gn + S], T.ps[:, 0:S]))
    op("n1", "s", "mn1", act(T.gr[:, GW + gn:GW + gn + S], T.ps[:, 512:512 + S], F.Copy))
    op("f0", "v", "mf0", cp_(T.gr[:, gf:gf + H2], T.ps[:, 1024:1024 + H2]))
    op("f1", "s", "mf1", act(T.gr[:, GW + gf:GW + gf + H2], T.ps[:, 1536:1536 + H2], F.Copy))

    near, away = T.an[R, 0:1], T.nfa[R, :]
    first, second, n1, n2 = (away, near, H2, S) if far else (near, away, S, H2)
    e0, e1 = ("Nf", "an") if far else ("an", "Nf")
    if up:
        op("l0", "s", e0, act(T.an[R, 2:3], first, F.Copy, scale=-1.0, bias=n1 - 0.5))
        op("l1", "s", e1, act(T.an[R, 1:2], second, F.Copy, scale=-1.0, bias=float(n2)))
    else:
        op("l1", "s", e0, act(T.an[R, 1:2], first, F.Copy, scale=-1.0, bias=float(n1)))
    op("l2", "v", "l1 cs " + e0, ts(T.la[R, 0:16], T.ki[R, 6:22], first, T.an[R, 1:2], A.is_gt, A.mult))
    ki = T.ki[R, 6:22]
    if not up:
        op("l3", "v", "all cs", ts(T.la[R, 32:48], ki, T.lnb[R, 0:1], 4 * BIG, A.is_gt, A.mult))
        op("lb", "v", "l3", lambda ki=ki: V.tensor_tensor(T.la[R, 48:64], T.la[R, 32:48], ki, A.add))
        ki = T.la[R, 48:64]
    op("la", "v", "l2 lb", lambda: V.tensor_tensor(T.la[R, 16:32], T.la[R, 0:16], ki, A.add))
    op("tf", "v", "la l0", *[ts(T.tf[r, :], T.la[R, 16:32], T.an[R, 2:3] if up else -0.5, float(ZERO), A.add, A.min) for r in (LOW, UP)])
    store = lambda e, o, i, sem: (lambda: e.dma_start(o, i).then_inc(T.sem[sem], 16) and None)
    ns = OPT["ns"]
    for i in range(ns):
        a, b = S * i // ns, S * (i + 1) // ns
        op("y0%d" % i, "v", "tf n0 f0 cs", cp_(T.y0[:, a:b], T.gr[:, 0:ZERO + 1].indirect(T.tf[:, a // 16:b // 16])))
        op("y1%d" % i, "s", "tf n1 f1 cs", act(T.y1[:, a:b], T.gr[:, GW:GW + ZERO + 1].indirect(T.tf[:, a // 16:b // 16]), F.Copy))
        op("sy0%d" % i, "y", "y0%d" % i, store(Y, T.y[:, a:b], T.y0[:, a:b], "sya"))
        if i == ns - 1:
            op("sy1%d" % i, "s", "y1%d" % i, store(SC, T.y[:, S + a:S + b], T.y1[:, a:b], "syb"))
        else:
            op("sy1%d" % i, "y", "y1%d" % i, store(Y, T.y[:, S + a:S + b], T.y1[:, a:b], "sya"))
    op("sw", "y", OPT["sw"], store(Y, T.wt[:, :], T.w[:, :], "lw"))
    op("all", "s", "an Nf", act(T.lnb[R, 0:1], near, F.Identity, bias=away))
    op("own", "s", "go", act(junk(COLS, R), T.gg[R, vo:vo + COLS], F.Copy, accum_out=T.lnb[R, 1:2]))
    op("sln", "y", "all own", store(Y, T.ln[:, :], T.lnb[64:65, :], "sln"))

    for c, users in (("zg", "kp kx"), ("zl", "u1"), ("zn", "nf"), ("zm", "gx"), ("lc", "mark"), ("zw", "xb x"), ("zt cu", "turn2"), ("zr", "y00 y10"), ("ti", "sc ss"), ("zx", "q0")):
        for n in users.split():
            if n in ops:
                ops[n][1].extend(c.split())

    todo = {e: [n for n in ORDER[e].split() if n in ops and ops[n][0] == e] for e in ORDER}
    assert sum(len(l) for l in todo.values()) == len(ops)
    while any(todo.values()):
        e = [e for e in todo if todo[e] and all(d in tok or d not in ops for d in ops[todo[e][0]][1])][0]
        n = todo[e].pop(0)
        need(e, *[tok[d] for d in ops[n][1] if d in tok])
        for call in ops[n][2]:
            ins = call()
            tok[n] = mark(e, ins) if (e in "vst" and n[0:2] != "sy") or n[0] == "z" else None

    need("p", ("loc", sent[0]), ("qv", done["v"]), ("qs", done["s"]), ("qt", done["t"]), ("qp", done["p"]))
    need("y", ("sln", 16), ("sya", 16 * (2 * ns - 1)))
    need("s", ("syb", 16))
